import numpy as np, ml_dtypes
CORES = [3,11,19,27,35,43,51,59]
N = 8
BF = ml_dtypes.bfloat16
def gentries(a):
    return np.ascontiguousarray(a.reshape(8, 16, -1).transpose(0, 2, 1)).reshape(8, -1)
def gtable(e):
    e = np.asarray(e); return np.ascontiguousarray(e.reshape(8, -1, 16).transpose(0, 2, 1)).reshape(128, -1).astype(np.int32)
V, H, RO, SQ, K = 2048, 384, 2, 3, 85
W = V + 2 * H; Z = 8 * N
def ring(a):
    return np.ascontiguousarray(np.swapaxes(a, 0, 1)).reshape((Z,) + a.shape[2:])
def unring(a):
    return np.ascontiguousarray(np.swapaxes(a.reshape((8, N) + a.shape[1:]), 0, 1))
def tiles(a):
    return np.ascontiguousarray(unring(a).transpose(0, 1, 3, 2)).reshape(N, 128, V)
def pack(x, lf, rt):
    return {"x0": (tiles(x).astype(np.float32) * np.float32(0.015625)).astype(BF), "lf": np.stack([gtable(a) for a in unring(lf)]), "rt": np.stack([gtable(a) for a in unring(rt)])}
def loose(rng):
    v = np.arange(H, H + V)
    return (rng.random((Z, V)) * v).astype(np.int64), v + 1 + (rng.random((Z, V)) * (W - 1 - v)).astype(np.int64)
def textures(rng, lf, rt, scale):
    B = V // 4; i = np.arange(4)
    prof = (rng.integers(0, 257, (K, 4, 16)) * scale).astype(np.int64); good = rng.integers(0, 5, K); amp = rng.choice(np.array([2, 8, 20, 40]), (K, 1, 1))
    lab = np.minimum((K * rng.random((Z, B)) ** 2).astype(np.int64), K - 1)
    x = prof[lab] + np.rint((2 * rng.random((Z, B, 4, 16)) - 1) * amp[lab]).astype(np.int64)
    for z in range(Z):
        o = np.argsort(lab[z], kind="stable"); a, b = o[:-1], o[1:]; s = lab[z][a] == lab[z][b]; a, b = a[s], b[s]
        g = good[lab[z][a]][:, None]; on = (g == i) | (g == 4); u = rng.random((a.size, 1))
        pa = 4 * a[:, None] + i; pb = 4 * b[:, None] + i
        m = on & (u > 0.04); rt[z, pa[m]] = H + pb[m]
        m = on & (u < 0.96); lf[z, pb[m]] = H + pa[m]
        y = (z + 1) % Z
        last = np.full(K, -1); last[lab[z]] = np.arange(B); first = np.full(K, B); first[lab[y][::-1]] = np.arange(B)[::-1]
        k = np.nonzero((last >= (V - H) // 4) & (first < H // 4))[0]
        g = good[k][:, None]; on = (g == i) | (g == 4); pa = 4 * last[k][:, None] + i; pb = 4 * first[k][:, None] + i
        rt[z, pa[on]] = H + V + pb[on]; lf[y, pb[on]] = H - V + pa[on]
    return np.clip(x, 0, 256).reshape(Z, V, 16)
def setup_inputs(rng):
    lf, rt = loose(rng); x = textures(rng, lf, rt, 1)
    return pack(x, lf, rt)
def setup_inputs_spread(rng):
    v = np.arange(H, H + V)
    lf = v - np.floor(np.power(1.0 * v, rng.random((Z, V)))).astype(np.int64)
    rt = v + np.floor(np.power(1.0 * (W - 1 - v), rng.random((Z, V)))).astype(np.int64)
    x = textures(rng, lf, rt, rng.choice(np.array([1.0, 0.5, 0.25]), (K, 1, 16), p=[0.5, 0.25, 0.25]))
    return pack(x * (rng.random((Z, V, 1)) > 0.03), lf, rt)
def setup_inputs_ends(rng):
    v = np.arange(H, H + V); near = np.zeros((Z, V), bool); n = V // 2 + 40
    for z in range(Z):
        runs = np.stack([rng.integers(1, 21, n), rng.integers(1, 51, n)], axis=1).reshape(-1); o = rng.integers(0, 40)
        near[z] = np.repeat(np.arange(2 * n) % 2 == 0, runs)[o:o + V]
        g = z // N
        if g % 2 == 0 or g == 7: near[z, 0] = True
        if g % 2 == 1: near[z, V - 1] = True
    near[Z - 1, V - 30:] = True
    arch = rng.integers(0, 2, 16); flip = rng.random((Z, V, 16)) < rng.choice(np.array([0.0, 0.1, 0.4]), (Z, V, 1))
    x = 256 * ((arch + rng.integers(0, 2, (Z, V, 1)) + flip) % 2)
    x = np.where(rng.random((Z, V, 1)) < 0.28, rng.integers(0, 257, (Z, V, 16)), x)
    return pack(x, np.where(near, v - 1, 0), np.where(near, v + 1, W - 1))
def setup_inputs_corners(rng):
    lf, rt = loose(rng); x = np.zeros((Z, V, 16), np.int64); T = 2 ** SQ
    sizes = [[1], [1, 2, 3], [3, 4, 5], [T - 1, T, T + 1, T + 2], [3 * T], [V], [1, 2, 3, 4, T, T + 1, 2 * T], [4]]
    for z in range(Z):
        k = np.array(sizes[(z // N + z % N) % 8]); n = rng.choice(k, V // int(k.min()) + 1)
        lab = np.empty(V, np.int64); lab[rng.permutation(V)] = np.repeat(np.arange(n.size), n)[:V]
        o = np.argsort(lab, kind="stable"); a, b = o[:-1], o[1:]; s = lab[a] == lab[b]; a, b = a[s], b[s]
        rt[z, a] = H + b; lf[z, b] = H + a
        amp = 40 if k[0] == V else 3
        x[z] = rng.integers(0, 257, (V, 16))[lab] + rng.integers(-amp, amp + 1, (V, 16))
    for z in range(Z):
        y = (z + 1) % Z
        if (z // N) % 2 == 0: rt[z, V - 1] = H + V; lf[y, 0] = H - 1
        else: rt[z, V - H] = W - 1; lf[y, H - 1] = 0
    return pack(np.clip(x, 0, 256), lf, rt)
def setup_inputs_crowd(rng):
    lf, rt = loose(rng); x = textures(rng, lf, rt, 1); v = np.arange(H, H + V); kind = rng.permutation(8)
    for z in range(Z):
        k = kind[z // N]
        if k < 2:
            j = rng.integers(0, V); a, b = lf[z, j], rt[z, j]; lf[z] = 0; rt[z] = W - 1
            if k == 1: lf[z, j] = a; rt[z, j] = b
        elif k == 2:
            rt[z] = np.where(v < H + V - 1, H + V - 1, W - 1); lf[z] = np.where(v > H, H, 0)
        elif k == 3:
            h = np.sort(H + rng.permutation(V)[:5])
            rt[z] = np.concatenate([h, [W - 1]])[np.searchsorted(h, v, side="right")]
            lf[z] = np.concatenate([[0], h])[np.searchsorted(h, v, side="left")]
    return pack(x, lf, rt)
def setup_inputs_calm(rng):
    lf, rt = loose(rng); x = textures(rng, lf, rt, 1); kind = rng.permutation(8)
    for z in range(Z):
        k = kind[z // N] % 4
        if k < 3: x[z] = (0, 253, 192)[k] + rng.integers(0, 4, (V, 16))
    return pack(x, lf, rt)
def check_ranges(d):
    bad = []; v = np.arange(H, H + V)
    x = np.asarray(d["x0"]).astype(np.float64)
    if not np.all((x >= 0) & (x <= 4)): bad.append("range of x0")
    elif np.any(x * 64 != np.floor(x * 64)): bad.append("x0 holds a number that is no multiple of 2**-6")
    elif np.min(np.mean(x.reshape(N, -1), axis=1)) < 1: bad.append("the mean of a rank's x0 is under 1")
    a = np.stack([gentries(e) for e in np.asarray(d["lf"])]).astype(np.int64); b = np.stack([gentries(e) for e in np.asarray(d["rt"])]).astype(np.int64)
    if np.min(a) < 0 or np.max(a) > H + V - 2: bad.append("range of lf")
    if np.any(a >= v): bad.append("an entry of lf isn't under its place")
    if np.min(b) < H + 1 or np.max(b) > W - 1: bad.append("range of rt")
    if np.any(b <= v): bad.append("an entry of rt isn't over its place")
    return bad
def pick(w, i):
    return w.reshape(-1, 16)[i + w.shape[1] * np.arange(Z)[:, None]]
def better(w, x, c, cur):
    c = np.where((c >= 0) & (c < W), c, cur)
    near = np.abs(pick(w, c) - x) < np.abs(pick(w, cur) - x)
    return np.where(np.add.reduce(near.astype(np.int64), axis=2) >= 9, c, cur)
def reference(x0, lf, rt):
    x = ring(np.asarray(x0).astype(np.float32).reshape(N, 8, 16, V).transpose(0, 1, 3, 2))
    l = ring(np.stack([gentries(a) for a in lf]).astype(np.int64)); r = ring(np.stack([gentries(a) for a in rt]).astype(np.int64))
    y = np.zeros((Z, V, 16)); own = np.arange(H, H + V)
    for t in range(RO):
        w = np.concatenate([np.roll(x, 1, axis=0)[:, V - H:], x, np.roll(x, -1, axis=0)[:, :H]], axis=1)
        if t % 2 == 0:
            cl = np.concatenate([np.roll(l, 1, axis=0)[:, V - 1:] - V, l[:, :V - 1]], axis=1) + 1
            cr = np.concatenate([np.roll(r, 1, axis=0)[:, V - 1:] - V, r[:, :V - 1]], axis=1) + 1
        else:
            cl = np.concatenate([l[:, 1:], np.roll(l, -1, axis=0)[:, :1] + V], axis=1) - 1
            cr = np.concatenate([r[:, 1:], np.roll(r, -1, axis=0)[:, :1] + V], axis=1) - 1
        l = better(w, x, cl, l); r = better(w, x, cr, r)
        rw = np.concatenate([np.roll(r, 1, axis=0)[:, V - H:] - V, r], axis=1)
        lw = np.concatenate([l, np.roll(l, -1, axis=0)[:, :H] + V], axis=1)
        back = np.where(np.take_along_axis(rw, l, 1) == own, l, own)
        end = np.take_along_axis(lw, r - H, 1) != own
        a = np.concatenate([np.tile(np.arange(H), (Z, 1)), back], axis=1); n = (a != np.arange(H + V)).astype(np.int64); m = np.ascontiguousarray(w[:, :H + V])
        for k in range(SQ):
            m = np.maximum(m, pick(m, a)); n = n + np.take_along_axis(n, a, 1); a = np.take_along_axis(a, a, 1)
        y = y + m[:, H:].astype(np.float64) * np.exp(-np.abs(x - pick(w, r)).astype(np.float64))
        go = end & (n[:, H:] >= 3)
        moved = np.minimum(np.maximum(x + np.float32(0.125) * (x - pick(w, a[:, H:])), np.float32(0)), np.float32(4))
        x = np.where(go[:, :, None], moved, x)
    return {"xe": tiles(x).astype(np.float32), "ye": tiles(y).astype(np.float32)}

def check_inputs(d):
    bad = list(check_ranges(d))
    if not bad:
        for name, y in reference(**d).items():
            for q in range(N):
                v = np.abs(np.asarray(y[q], np.float64)); s = np.sqrt(np.mean(v * v))
                if v.max() > 5 * s or s < 2.0 ** -1: bad.append('%s of rank %d is uneven or too small' % (name, q))
    return bad

@@ -1,0 +1,775 @@
+from concourse.bass import DstId, RemoteDMATransfer
+from concourse.mybir import AluOpType as A, ActivationFunctionType as F
+
+V_, H_, W_ = 2048, 384, 2816
+XO = V_ + H_
+OFF = 1408
+BLK = {("r", 0): 0, ("r", 1): 1, ("l", 0): 2, ("l", 1): 3}
+
+
+def scratch():
+    s = {"ps": ("psum", [128, 4096], "float32")}
+
+    def add(names, shape, dt):
+        for n in names.split():
+            s[n] = ("sbuf", [128] + shape, dt)
+    add("xw0", [XO + W_], "bfloat16"); add("xh0 m2c0 m4c0", [V_], "bfloat16"); add("m2t0 m4t0", [XO], "bfloat16")
+    add("es0 et0", [H_], "bfloat16")
+    add("xw1", [XO + W_], "float32"); add("xh1", [W_], "float16"); add("es1 et1", [H_], "float16")
+    add("m2c1 m4c1 yy x2", [V_], "float32"); add("m2t1 m4t1", [XO], "float32"); add("a2t", [XO], "bfloat16")
+    add("dc de rc re nr xc xg sa pr nl ob oe o4 mm dn rn xs", [V_], "float16")
+    add("tb", [W_], "float32"); add("a1t", [XO], "bfloat16")
+    add("fold", [256], "float16"); add("fm", [512], "float16"); add("cw", [8, 128], "float16")
+    add("a1h", [128], "bfloat16"); add("a1l", [128], "float16")
+    add("li", [4, 64], "int32"); add("st0 st1 st2", [4, 64], "float16"); add("ul0 ul1 ul2 uc", [4, 64], "uint16")
+    add("thr", [4, 64], "bfloat16"); add("dl tt", [4, 64], "float32"); add("dec", [4, 64], "float16")
+    add("w1", [128], "bfloat16"); add("jk", [128], "float16"); add("jf", [128], "float32")
+    add("vq a1w a2w w2 w3 w4", [128], "float16"); add("vq2 vi w5 w6 w7", [128], "float32")
+    add("ua1 ua2 ua4 uix", [128], "uint16")
+    add("sb0 gb0", [16], "float16"); add("sr0 sr1 gl0 gl1", [24], "float16"); add("sl0 sl1 gr0 gr1", [32], "float16")
+    add("dd dm", [256], "int32"); add("jj ja jb", [256], "float16"); add("jn j2 jm s1 s3", [128], "float16")
+    add("zc z0 z8 zf", [144], "float16"); add("cv", [16, 136], "float16")
+    add("pi", [4], "int32"); add("pm c15", [4], "float32"); add("rr oh no", [16], "float32")
+    return s
+
+
+SCRATCH = scratch()
+NDMA = 40
+SEMAPHORES = ["cV", "cS", "cP", "cG", "sent"] + ["d%d" % k for k in range(NDMA)] + \
+    ["x0l", "x0r", "b0", "r0", "l0", "x1l", "x1r", "r1", "l1"]
+
+MODEL = dict(cyc=0.83e-3 * 1.25, gat=1.56, fix=0.06, pe=0.42e-3 * 1.25, hop=0.1, dma=2.0, dmab=0.22e-3, iss=0.06,
+             giss=1.0, riss=0.8, rlat=2.2, remb=1.6e-3, gfix=0.17, exp1=1.3)
+DIGITS = "0123456789abcdefghijklmnopqrstuvwxyz"
+ENG = "moder00:S model00:V model10:V moder10:S rel00:S rcl10:S rn00:P rn01:P rn10:S rn11:V tb00a:V tb01a:V tb01b:V back01:V end00:V a200:V c200:V c201:V cast0:G cast1:G cast3:G castl:V dn00:V tb10b:V back10:V c211:V a410:V"
+ORDER = "000f0e010302040d110m0n0h0p0i0g060k0l0q0s120t0j0o0y090a15190x1b13051d1g1c1e0z0v0u10141h1i1a0w0r1l071f080b1n0c1x1m1k1o1z1j2b332g1y1p21202223242d2c252e2p262q2h2728292s322f343g3h352i1s373i2a2j382r362t392u2v1t2k1q3a2l1r3b2w2m2x3c2n3d3j3p2y3e2z3q3x2o303t313f3v3y3z3u3w3k164041424d434e3m3l44454f474g484h464j4b494i4k4l4n6b176r184c4a4m4v3n3o3r4o6d4w4x3s4p4z504q4s516c1v6f4y1u53545b4r52555j6e5c1w6g4t566i5d5k5e6x4u575f585g595h6j5a5l5o5i5t6o6p5m5w5u6k5p5n5q5x5v5y5z5r656z666l6y6h6s61676t726u626q6369706a646v6068715s7k7p7m767l7a8b77787n7o7b6m7q797c8g7y7r7d7z8d808c8e8h7e7f827g8f8i837h8j7i7s7j81848k8p85868q7t8l8m8n878897898t958u7u8o8r8v8w7v7w938s9196bk9892948a8x8y9l8z90a0999m7x9xbl9n9o9aa19b9p9c9d9r9f9g9s9j9v9t9e9q9h9k9w9ub7a2b5bc9i9ya79za8a9aa7574b8b66nbh73a3a4a5abajakala6bdasb9acadaebibmaramafanagaoahapaibjaqbn6wbobpbabbbebfatauavaxayawazb0b1b2b3bgb4"
+ENG = "moder00:S model00:V model10:V moder10:S rel00:S rcl10:S rn00:P rn01:P rn10:S rn11:V tgl0:V tb00f:V back00:V a100a:V a100b:V a101f:V a101b:V a200:V c200:V cast0:G cast1:G cast2:G cast3:V tgl1:V tb11a:V a110a:V a111f:V a111b:V c210:V"
+ORDER = "0e0f01030a0002040c110g0d0h120i1d0m0k160n0j091h0l1c1j060807131l1k0y0q19140p0r0v0x0o1e0s0t171i0u1f1o1a1p1g050b1q0w1s3a1b100z183b2j1m1n1v1x2526273c292y3f3d3e3g1w2k2a282b1r3h2c2o2d2l2m2e2x212z2p3i302f2n1t1u1z2g2h31321y203o333p342q3j2r3k2s352i3l3m2t472u36482v3q154b3738413s42494c45393u433r3t3v463x3n3y444a4r4d4e4f4g4h774s3w3z4t4j4k404u4l4i2w4v4x4w4m4p4y4q4n4o4z5051535b58555954525c565f5g5d5j7d5a6t5e5k5h576r5m5l5n5r5s5i5z5o5u5t605v5p5w5q23226u5x74246s6162645y696v636c656d6a6b7e7578666e76676f6h6i6l6j6y6m796n7f6o7a686g7b6q6k6p80817m7n85827o7q7p867g7h837r8r848e7s877t8w887i7u8i8t8f7v897w8g7x8s8u8h8j7y958x8v8k968a8l8y8b7z8z6w6z8m70908c8n8o8p99919h928d93c8719a9i979b9c989n9l9j9d9o9r9p9e9m9k949s8q9q9t9ua79fa89galao6xc09v9wa99xaaab9y9zada0aebtafaca1a2aga3a5ahc1aja4a6amaibvakapanarav7k7lbu7jbw72asatauawbxaxaqazb0b7ayb8c5b1b2b3bfb9bgbab4bbb573bybcb6bdc2c9bzbebhc6c7c3c4cabicb7cccbjbkbpbqblbrbmbsbnbocd"
+OPTS = dict(eps=0.12, eng=dict(x.split(":") for x in ENG.split()), off={}, order=ORDER,
+            groups=[[[("r", 1)], [("r", 0)], [("l", 0)], [("l", 1)]]] * 2,
+            cut=[[(0, 384), (1664, 2048), (384, 1024), (1024, 1664)], [(0, 768), (768, 1536), (1536, 2048)]])
+DEBUG = {}
+
+
+def cost(op, m):
+    k, n = op["c"]
+    if k == "g":
+        return m["fix"] + n * m["gat"] * m["cyc"], 0.0
+    if k == "e":
+        return m["fix"] + max(n, 64) * m["cyc"], 0.0
+    if k == "pe":
+        return n * m["pe"] + 0.05, 0.0
+    if k == "gp":
+        return m["gfix"] + 2 * n * m["cyc"], 0.0
+    if k == "dma":
+        return (m["giss"] if op["eng"] == "G" else m["iss"]), m["dma"] + n * m["dmab"]
+    if k == "rem":
+        return m["riss"], 0.0
+    return 0.0, m["rlat"] + n * m["remb"]
+
+
+def deal_banks(ops, order):
+    jobs = {}
+    for k in order:
+        if ops[k]["job"]:
+            jobs.setdefault(ops[k]["job"][0], []).append(k)
+    holder = [None] * 8
+    since = [-1] * 8
+    bank = {}
+    extra = {}
+    for pos, k in enumerate(order):
+        jb = ops[k]["job"]
+        if not jb:
+            continue
+        j, size = jb
+        if j not in bank:
+            best = None
+            for b in range(0, 8, size):
+                if size == 2:
+                    if since[b] is None or since[b + 1] is None:
+                        continue
+                    key = max(since[b], since[b + 1])
+                else:
+                    if since[b] is None:
+                        continue
+                    key = since[b] - (1000 if since[b ^ 1] is None else 0)
+                if best is None or key < best[0]:
+                    best = (key, b)
+            if best is None:
+                raise ValueError("no PSUM bank left")
+            b = best[1]
+            bank[j] = b
+            extra[k] = [p for i in range(size) if holder[b + i] is not None for p in jobs[holder[b + i]]]
+            for i in range(size):
+                holder[b + i] = j
+                since[b + i] = None
+        if k == jobs[j][-1]:
+            for i in range(size):
+                since[bank[j] + i] = pos
+    return bank, extra
+
+
+def issue_order(ops, names, code):
+    where = {op["name"]: k for k, op in enumerate(ops)}
+    order = []
+    placed = set()
+
+    def put(k):
+        for p in ops[k]["pre"]:
+            if p not in placed:
+                put(p)
+        placed.add(k)
+        order.append(k)
+    for i in range(0, len(code), 2):
+        k = where.get(names[DIGITS.index(code[i]) * len(DIGITS) + DIGITS.index(code[i + 1])])
+        if k is not None and k not in placed:
+            put(k)
+    for k in range(len(ops)):
+        if k not in placed:
+            put(k)
+    return order
+
+
+def schedule(ops, m, opts):
+    n = len(ops)
+    succ = [[] for _ in range(n)]
+    for k, op in enumerate(ops):
+        for p in op["pre"]:
+            succ[p].append(k)
+    cs = [cost(op, m) for op in ops]
+    prio = [0.0] * n
+    for k in range(n - 1, -1, -1):
+        prio[k] = cs[k][0] + cs[k][1] + m["hop"] + max([prio[s] for s in succ[k]] + [0.0])
+    for k in range(n):
+        prio[k] += opts["off"].get(ops[k]["name"], 0.0)
+    jobs = {}
+    for k, op in enumerate(ops):
+        if op["job"]:
+            jobs.setdefault(op["job"][0], []).append(k)
+    left = {j: len(v) for j, v in jobs.items()}
+    holder = [None] * 8
+    bank = {}
+    fin = [None] * n
+    start = [None] * n
+    free = {}
+    wait = [len(op["pre"]) for op in ops]
+    ready = [k for k in range(n) if wait[k] == 0]
+    order = []
+    extra = [[] for _ in range(n)]
+
+    def banks_for(size):
+        best = None
+        for b in range(0, 8, size):
+            hs = [holder[b + i] for i in range(size)]
+            if any(h is not None and left[h] > 0 for h in hs):
+                continue
+            t = max([fin[k] for h in hs if h is not None for k in jobs[h]] + [0.0])
+            o = holder[b ^ 1]
+            key = (t, b) if size == 2 else (t + (0.0 if (o is not None and left[o] > 0) or b >= 6 else 1.0), -b)
+            if best is None or key < best[0]:
+                best = (key, b, t)
+        return best
+    while ready:
+        cand = []
+        for k in ready:
+            op = ops[k]
+            t = max([fin[p] + m["hop"] for p in op["pre"]] + [free.get(op["eng"], 0.0)])
+            b = None
+            if op["job"] and op["job"][0] not in bank:
+                b = banks_for(op["job"][1])
+                if b is None:
+                    continue
+                t = max(t, b[2] + m["hop"])
+            cand.append((t, k, b))
+        if not cand:
+            raise ValueError("no PSUM bank left")
+        t0, k0, _b = min(cand, key=lambda c: (c[0], -prio[c[1]]))
+        e = ops[k0]["eng"]
+        t, k, b = max([c for c in cand if ops[c[1]]["eng"] == e and c[0] <= t0 + opts["eps"]], key=lambda c: prio[c[1]])
+        op = ops[k]
+        if b is not None:
+            j, size = op["job"]
+            for i in range(size):
+                h = holder[b[1] + i]
+                if h is not None:
+                    extra[k] += jobs[h]
+                holder[b[1] + i] = j
+            bank[j] = b[1]
+        if op["job"]:
+            left[op["job"][0]] -= 1
+        start[k] = t
+        if op["eng"]:
+            free[op["eng"]] = t + cs[k][0]
+        fin[k] = t + cs[k][0] + cs[k][1]
+        order.append(k)
+        ready.remove(k)
+        for s in succ[k]:
+            wait[s] -= 1
+            if wait[s] == 0:
+                ready.append(s)
+    if len(order) != n:
+        raise ValueError("calls left over")
+    return order, bank, extra, start, fin
+
+
+def plan(g, core, T, topo, turn_r, turn_l):
+    rank = T.rank_of(core)
+    N = len(T.cores)
+    right, left = T.cores[(rank + 1) % N], T.cores[(rank - 1) % N]
+    for dst in (right, left):
+        if not topo.may_write(core, dst):
+            raise ValueError("this core can't reach its neighbour")
+    Q = {"V": g.vector, "S": g.scalar, "P": g.tensor, "G": g, "Y": g.sync}
+    ops = []
+    bank = {}
+    acc = {}
+    jacc = {}
+    seen = {}
+    wide = {n: (2 if s[2] in ("float16", "bfloat16", "uint16") else 4) for n, s in SCRATCH.items()}
+
+    def sb(name, lo, hi, step=1):
+        return (lambda: T[name][:, lo:hi:step] if step > 1 else T[name][:, lo:hi], [(name, lo, hi)], None,
+                (hi - lo + step - 1) // step, wide[name])
+
+    def b3(name, k0, k1, ks, c0, c1):
+        inner = SCRATCH[name][1][2]
+        ks_ = list(range(k0, k1, ks))
+        rng = [(name, k * inner + c0, k * inner + c1) for k in ks_] if ks > 1 else [(name, k0 * inner, k1 * inner)]
+        if len(ks_) == 1:
+            return (lambda: T[name][:, k0, c0:c1], [(name, k0 * inner + c0, k0 * inner + c1)], None, c1 - c0, wide[name])
+        return (lambda: T[name][:, k0:k1:ks, c0:c1], rng, None, len(ks_) * (c1 - c0), wide[name])
+
+    def ps(job, lo, hi, step=1):
+        return (lambda: T.ps[:, 512 * bank[job[0]] + lo:512 * bank[job[0]] + hi:step], [], job, (hi - lo + step - 1) // step, 4)
+
+    def ind(win, off):
+        return (lambda: win[0]().indirect(off[0]()), win[1] + off[1], None, 16 * off[3], 0)
+
+    def hbm(f):
+        return (f, [], None, 0, 0)
+
+    def add(name, eng, c, outs, ins, emit, after=(), ninc=1, sem=None):
+        k = len(ops)
+        pre = set(after)
+        job = None
+        for lst, wr in ((ins, False), (outs, True)):
+            for o in lst:
+                if o[2]:
+                    job = o[2]
+                for (b, lo, hi) in o[1]:
+                    for (l2, h2, p, w2) in acc.get(b, []):
+                        if l2 < hi and lo < h2 and (wr or w2) and p != k:
+                            pre.add(p)
+                    acc.setdefault(b, []).append((lo, hi, k, wr))
+        if job:
+            wr = any(o[2] for o in outs)
+            for (p, w2) in jacc.get(job[0], []):
+                if ops[p]["eng"] != eng or wr or w2:
+                    pre.add(p)
+            jacc.setdefault(job[0], []).append((k, wr))
+        seen[name] = seen.get(name, 0) + 1
+        if seen[name] > 1:
+            name = "%s_%d" % (name, seen[name])
+        ops.append(dict(name=name, eng=eng, c=c, pre=sorted(pre), job=job, emit=emit, ninc=ninc, sem=sem))
+        return k
+
+    def cyc(out, ins):
+        return out[3] * (0.5 if all(o[4] == 2 for o in [out] + ins) else 1.0)
+
+    def ts(name, out, a, s1, s2, o0, o1=None, after=()):
+        ex = [s for s in (s1, s2) if isinstance(s, tuple)]
+        v = lambda s: s[0]() if isinstance(s, tuple) else s
+        if o1 is None:
+            f = lambda: [g.vector.tensor_scalar(out[0](), a[0](), v(s1), None, o0)]
+        else:
+            f = lambda: [g.vector.tensor_scalar(out[0](), a[0](), v(s1), v(s2), o0, o1)]
+        return add(name, "V", ("e", cyc(out, [a])), [out], [a] + ex, f, after)
+
+    def tt(name, out, a, b, o, after=()):
+        c = ("g", out[3]) if a[4] == 0 else ("e", out[3] * (1 if a[2] or b[2] else 2))
+        return add(name, "V", c, [out], [a, b], lambda: [g.vector.tensor_tensor(out[0](), a[0](), b[0](), o)], after)
+
+    def act(name, out, a, fn, bias=None, scale=None, after=()):
+        kw = {}
+        if bias is not None:
+            kw["bias"] = bias
+        if scale is not None:
+            kw["scale"] = scale
+        c = ("g", out[3]) if a[4] == 0 else ("e", out[3])
+        return add(name, "S", c, [out], [a], lambda: [g.scalar.activation(out[0](), a[0](), fn, **kw)], after)
+
+    def cp(name, out, a, after=(), default="S"):
+        e = OPTS["eng"].get(name, default)
+        DEBUG.setdefault("flex", {})[name] = {"S": ("g" if a[4] == 0 else "e", out[3]), "G": ("gp", out[3]),
+                                              "V": ("g", out[3]) if a[4] == 0 else ("e", cyc(out, [a]))}
+        if e == "S":
+            return act(name, out, a, F.Copy, after=after)
+        if e == "G":
+            return add(name, "G", ("gp", out[3]), [out], [a],
+                       lambda: [g.affine_select(out[0](), a[0](), [[0, out[3]]], A.is_ge, 0.0, 0, 0)], after)
+        c = ("g", out[3]) if a[4] == 0 else ("e", cyc(out, [a]))
+        return add(name, "V", c, [out], [a], lambda: [g.vector.tensor_copy(out[0](), a[0]())], after)
+
+    def mm(name, groups, after=(), first=True, last=True):
+        def f():
+            r = []
+            for gr in groups:
+                for i, (o, l, x) in enumerate(gr):
+                    ins = g.tensor.matmul(o[0](), l[0](), x[0](), first and i == 0, last and i == len(gr) - 1)
+                r.append(ins)
+            return r
+        n = sum(max(64, x[3]) * (4 if x[4] == 4 else 1) for gr in groups for (o, l, x) in gr)
+        return add(name, "P", ("pe", n), [gr[0][0] for gr in groups], [y for gr in groups for (o, l, x) in gr for y in (l, x)],
+                   f, after, ninc=len(groups))
+
+    nd = [0]
+
+    def dma(name, q, out, a, nbytes, after=(), accum=False):
+        sem = "d%d" % nd[0]
+        nd[0] += 1
+        if accum:
+            f = lambda: [g.dma_start(out[0](), a[0](), accum_op=A.add)]
+        else:
+            f = lambda: [Q[q].dma_start(out[0](), a[0]())]
+        return add(name, q, ("dma", nbytes), [out], [a], f, after, sem=(sem, 16))
+
+    last_send = []
+    sent = [0]
+
+    def send(name, parts):
+        es = [e for e in topo.engines(core, parts[0][0]) if all(e in topo.engines(core, p[0]) for p in parts)]
+        per = len(es) // len(parts)
+        masks = [sum(1 << e for e in es[i * per:(i + 1) * per]) for i in range(len(parts))]
+
+        def f():
+            if len(parts) == 1:
+                dst, src, land, sem = parts[0]
+                rid, pid, _s = topo.addr(dst)
+                g.remote_dma(land[0](), src[0](), T.sem[sem], T.sem.sent, pid, rid, masks[0])
+            else:
+                g.remote_dma_fused([RemoteDMATransfer(dst_ids=[DstId(rid=topo.addr(p[0])[0], pnc=topo.addr(p[0])[1])],
+                                                      dma_engine_mask=masks[i], remote_sem=T.sem[p[3]], src=p[1][0](), dst=p[2][0]())
+                                    for i, p in enumerate(parts)], local_sem=T.sem.sent)
+            return []
+        k = add(name, "G", ("rem", 0), [], [p[1] for p in parts], f, last_send[-1:], ninc=0)
+        last_send.append(k)
+        sent[0] += per * len(parts)
+        for p in parts:
+            add("arr_" + p[3], None, ("arr", p[1][3] * p[1][4] * len(parts)), [p[2]], [], None, [k], sem=(p[3], per))
+
+    def io(name, out, pat, base, cm, flt):
+        kw = {"allow_small_or_imprecise_dtypes": True} if flt else {}
+        return add(name, "G", ("gp", out[3]), [out], [], lambda: [g.iota(out[0](), pat, base, cm, **kw)])
+
+    jn_ = [0]
+
+    def job(size):
+        jn_[0] += 1
+        return (jn_[0], size)
+
+    x0 = T.x0
+    own = XO + H_
+    src_r, src_l = sb("xw0", own + V_ - H_, own + V_), sb("xw0", own, own + H_)
+    if turn_r:
+        dma("Xld_a", "Y", (lambda: T.es0[16:128, :], [("es0", 0, H_)], None, 0, 2), hbm(lambda: x0[0:112, V_ - H_:V_]), 768)
+        dma("Xld_b", "S", (lambda: T.es0[0:16, :], [("es0b", 0, 1)], None, 0, 2), hbm(lambda: x0[112:128, V_ - H_:V_]), 768)
+        src_r = (lambda: T.es0[:, :], [("es0", 0, H_), ("es0b", 0, 1)], None, H_, 2)
+    if turn_l:
+        dma("Xld_c", "Y", (lambda: T.et0[0:112, :], [("et0", 0, H_)], None, 0, 2), hbm(lambda: x0[16:128, 0:H_]), 768)
+        dma("Xld_d", "S", (lambda: T.et0[112:128, :], [("et0b", 0, 1)], None, 0, 2), hbm(lambda: x0[0:16, 0:H_]), 768)
+        src_l = (lambda: T.et0[:, :], [("et0", 0, H_), ("et0b", 0, 1)], None, H_, 2)
+    dma("ld_r", "Y", sb("xw0", own + V_ - H_, own + V_), hbm(lambda: x0[:, V_ - H_:V_]), 768)
+    dma("ld_l", "S", sb("xw0", own, own + H_), hbm(lambda: x0[:, 0:H_]), 768)
+    send("sx0", [(right, src_r, sb("xw0", XO, XO + H_), "x0l"), (left, src_l, sb("xw0", own + V_, XO + W_), "x0r")])
+    dma("ld_rt", "Y", b3("li", 0, 2, 1, 0, 64), hbm(lambda: T.rt[:, :]), 512)
+    dma("ld_lf", "S", b3("li", 2, 4, 1, 0, 64), hbm(lambda: T.lf[:, :]), 512)
+    dma("ld_m", "Y", sb("xw0", own + H_, own + V_ - H_), hbm(lambda: x0[:, H_:V_ - H_]), 2560)
+    dma("ld_h", "Y", sb("xh0", 0, V_), hbm(lambda: x0[:, :]), 4096)
+
+    io("dd", sb("dd", 0, 256), [[1, 256]], 0, -1, False)
+    io("pi", sb("pi", 0, 1), [[0, 1]], 0, 1, False)
+    io("rr", sb("rr", 0, 16), [[1, 16]], 0, 0, True)
+    io("vi", sb("vi", 0, 128), [[16, 128]], H_ - OFF, 0, True)
+    ts("pi15", sb("pi", 1, 2), sb("pi", 0, 1), 15, None, A.bitwise_and)
+    cp("pm", sb("pm", 0, 1), sb("pi", 1, 2), default="V")
+    pm = sb("pm", 0, 1)
+    ts("oh", sb("oh", 0, 16), sb("rr", 0, 16), pm, None, A.is_equal)
+    ts("no", sb("no", 0, 16), sb("rr", 0, 16), pm, None, A.not_equal)
+    ts("c15", sb("c15", 0, 1), pm, -1.0, 15.0, A.mult, A.add)
+    ts("dm", sb("dm", 0, 256), sb("dd", 0, 256), 127, None, A.bitwise_and)
+    ts("jj", sb("jj", 0, 256), sb("dm", 0, 256), 0.0, None, A.is_equal)
+    for n, c, w in (("jn", -1.0, 128), ("j2", 2.0, 128), ("jm", -2.0, 128), ("ja", 1.125, 256), ("jb", -0.125, 256)):
+        ts(n, sb(n, 0, w), sb("jj", 0, w), c, None, A.mult)
+    if OPTS.get("off_b"):
+        ts("jk", sb("jk", 0, 128), sb("jj", 0, 128), 4096.0, None, A.mult)
+    if OPTS.get("off_c"):
+        ts("jf", sb("jf", 0, 128), sb("jj", 0, 128), 0.5, None, A.mult)
+    ts("zc", sb("zc", 0, 144), sb("dd", 0, 144), sb("c15", 0, 1), None, A.is_equal)
+    ts("z0", sb("z0", 0, 144), sb("dd", 0, 144), 15.0, sb("oh", 0, 1), A.is_equal, A.mult)
+    ts("z8", sb("z8", 0, 144), sb("dd", 0, 144), 7.0, sb("oh", 8, 9), A.is_equal, A.mult)
+    tt("zf", sb("zf", 0, 144), sb("z0", 0, 144), sb("z8", 0, 144), A.add)
+    ts("s1", sb("s1", 0, 128), sb("dd", 0, 128), 1.0, sb("no", 15, 16), A.is_equal, A.mult)
+    ts("s3", sb("s3", 0, 128), sb("dd", 0, 128), -1.0, sb("no", 0, 1), A.is_equal, A.mult)
+    ts("vq", sb("vq", 0, 128), sb("vi", 0, 128), pm, None, A.add)
+    ts("vq2", sb("vq2", 0, 128), sb("vi", 0, 128), pm, float(XO), A.add, A.add)
+    cva = b3("cv", 0, 16, 1, 0, 136)
+    add("cv0", "V", ("e", 1088), [cva], [], lambda: [g.vector.memset(T.cv[:], 0.0)])
+    ts("one", sb("a1w", 0, 128), sb("vi", 0, 128), 0.0, 1.0, A.mult, A.add)
+    add("cv1", "G", ("gp", 128), [cva], [sb("a1w", 0, 128)],
+        lambda: [g.affine_select(T.cv[:, :, 8:136:16], T.a1w[:, 0:128], [[-1, 16], [-16, 8]], A.is_equal, 0.0, 0, 1)])
+    cwa = b3("cw", 0, 8, 1, 0, 128)
+    add("cw0", "V", ("e", 512), [cwa], [], lambda: [g.vector.memset(T.cw[:], 0.0)])
+    add("cw1", "G", ("gp", 128), [cwa], [sb("a1w", 0, 128)],
+        lambda: [g.affine_select(T.cw[:, :, 0:128:8], T.a1w[:, 0:128], [[-1, 8], [-8, 16]], A.is_equal, 0.0, 0, 1)])
+    ts("low", sb("c15", 1, 2), pm, 8.0, None, A.is_lt)
+    ts("high", sb("c15", 2, 3), pm, 8.0, None, A.is_ge)
+    for i, (step, m_) in enumerate(((0.0, 1), (8.0, 1), (-8.0, 2), (0.0, 2))):
+        ts("fm", sb("fm", 128 * i, 128 * i + 128), sb("dd", 0, 128), step, sb("c15", m_, m_ + 1), A.is_equal, A.mult)
+    I_, In, I2, Im = sb("jj", 0, 128), sb("jn", 0, 128), sb("j2", 0, 128), sb("jm", 0, 128)
+    SA = lambda i: b3("cv", i, i + 1, 1, 8, 136)
+    SB = lambda i: b3("cv", i, i + 1, 1, 0, 128)
+    ts("ghi", sb("a1h", 0, 24), sb("vi", 0, 24), float(-H_), None, A.add)
+    ts("glo", sb("a1l", 0, 24), sb("vi", 0, 24), 0.0, pm, A.mult, A.add)
+    jg = job(1)
+    mm("ghp", [[(ps(jg, i, H_, 16), SA(i), sb("a1h", 0, 24)), (ps(jg, i, H_, 16), SB(i), sb("a1l", 0, 24))] for i in range(16)])
+    act("a1g", sb("a1t", 0, H_), ps(jg, 0, H_), F.Copy)
+    act("a2g", sb("a2t", 0, H_), ps(jg, 0, H_), F.Copy)
+    early = [k for k, op in enumerate(ops) if op["eng"] == "V"]
+    Z = lambda n, i: sb(n, 15 - i, 143 - i)
+    RS, LS = 112, 16
+
+    def ext(z, out, src, lo, more=()):
+        return [(out, Z(z, i), sb(src, lo + i, lo + 1024, 16)) for i in range(16)] + list(more)
+
+    def lk(name, side, h, c0=0, c1=64):
+        b = BLK[(side, h)]
+        return b3(name, b, b + 1, 1, c0, c1)
+
+    def tile_out(name, out, parts, turn, col, bias):
+        if turn:
+            j = job(1)
+            c = 0
+            gs = []
+            for p in parts:
+                gs.append([(ps(j, c, c + p[3]), sb("jj", col, col + 128), p)])
+                c += p[3]
+            mm("X" + name, gs)
+        c = 0
+        for p in parts:
+            act(name, sb(out, c, c + p[3]), ps(j, c, c + p[3]) if turn else p, F.Identity, bias=bias)
+            c += p[3]
+
+    allb = lambda n: b3(n, 0, 4, 1, 0, 64)
+    ts("st0", allb("st0"), allb("li"), float(-OFF), None, A.add)
+    cp("ul0", allb("ul0"), allb("li"), default="V")
+    tile_out("sb0", "sb0", [lk("st0", "l", 1, 56, 64), lk("st0", "r", 1, 56, 64)], turn_r, RS, float(-V_))
+    send("sb0", [(right, sb("sb0", 0, 16), sb("gb0", 0, 16), "b0")])
+
+    ydone = []
+    for t in range(2):
+        d = 1 if t == 0 else -1
+        R = "%d" % t
+        xw, so, sn, uo, un = "xw" + R, "st" + R, "st%d" % (t + 1), "ul" + R, "ul%d" % (t + 1)
+        xh = (lambda lo, hi: sb("xh0", lo, hi)) if t == 0 else (lambda lo, hi: sb("xh1", H_ + lo, H_ + hi))
+        win = sb(xw, XO, XO + W_)
+        j = job(1)
+
+        def shift(out, side, h):
+            o = lambda a, b: ps(j, out + a, out + b)
+            if d == 1:
+                edge = lk(so, side, 0, 63, 64) if h == 1 else sb("gb0", 15 if side == "r" else 7, 16 if side == "r" else 8)
+                return [(o(0, 64), sb("s1", 0, 128), lk(so, side, h)), (o(1, 64), SA(15), lk(so, side, h, 0, 63)),
+                        (o(0, 1), SA(15), edge)]
+            edge = lk(so, side, 1, 0, 1) if h == 0 else sb("gr0", 24 if side == "r" else 0, 25 if side == "r" else 1)
+            return [(o(0, 64), sb("s3", 0, 128), lk(so, side, h)), (o(0, 63), Z("z0", 15), lk(so, side, h, 1, 64)),
+                    (o(63, 64), Z("z0", 15), edge)]
+        parts = [[("r", 1), ("l", 1)], [("r", 0), ("l", 0)]] if t == 0 else [[("r", 0), ("r", 1), ("l", 0), ("l", 1)]]
+        for pi_, part in enumerate(parts):
+            if pi_ > 0:
+                j = job(1)
+            gs = []
+            for (side, h) in part:
+                b = BLK[(side, h)]
+                gs.append(shift(64 * b, side, h))
+                gs.append(shift(256 + 64 * b, side, h) + [(ps(j, 256 + 64 * b, 320 + 64 * b), In, lk(so, side, h))])
+            mm("shift" + R, gs)
+            runs = [(s_, BLK[(s_, h)], 1) for (s_, h) in part] if t == 0 else [("r", 0, 2), ("l", 2, 2)]
+            for (side, b, w) in runs:
+                p = ps(j, 64 * b, 64 * (b + w))
+                if side == "r":
+                    ts("uc" + R, b3("uc", b, b + w, 1, 0, 64), p, float(OFF + d), float(W_ - 1), A.add, A.min)
+                else:
+                    ts("uc" + R, b3("uc", b, b + w, 1, 0, 64), p, float(OFF + d), 0.0, A.add, A.max)
+            for (side, b, w) in runs:
+                p = ps(j, 64 * b, 64 * (b + w))
+                if side == "r":
+                    act("thr" + R, b3("thr", b, b + w, 1, 0, 64), p, F.Relu, bias=-100.0 * (W_ - 1 - OFF + 0.5 - d), scale=100.0)
+                else:
+                    act("thr" + R, b3("thr", b, b + w, 1, 0, 64), p, F.Relu, bias=100.0 * (-OFF - 0.5 - d), scale=-100.0)
+                if t == 0:
+                    act("dl" + R, b3("dl", b, b + 1, 1, 0, 64), ps(j, 256 + 64 * b, 320 + 64 * b), F.Identity, bias=float(d))
+            if t == 1:
+                act("dl" + R, allb("dl"), ps(j, 256, 512), F.Identity, bias=float(d))
+        for n in (xw, "m2t" + R, "m4t" + R):
+            dma("gh_" + n, "Y", sb(n, 0, H_), sb(xw, XO, XO + H_), H_ * wide[n])
+
+        def judge(side, h, jc, c):
+            lo, hi = 1024 * h, 1024 * h + 1024
+            nm = "%s%d%d" % (side, t, h)
+            b0, b1, b2, b3_, near = ("de", "dc", "re", "rc", "nr") if side == "r" else ("xg", "xc", "sa", "pr", "nl")
+            part = lambda j1, l, n: [[(ps(j1, q, q + 512), l, sb(n, lo + q, lo + q + 512))] for q in (0, 512)]
+            mode = OPTS["eng"].get("mode" + nm, "V" if side == "r" else "S")
+            if mode != "S":
+                tt("de" + nm, sb(b0, lo, hi), ind(win, lk(uo, side, h)), xh(lo, hi), A.subtract, early)
+                tt("dc" + nm, sb(b1, lo, hi), ind(win, lk("uc", side, h)), xh(lo, hi), A.subtract, early)
+                terms = []
+                for (n, a, b, lv, ls) in (("re", b0, b2, [(I_, b0), (Im, b2)], [(In, b2)]), ("rc", b1, b3_, [(In, b1), (I2, b3_)], [(I_, b3_)])):
+                    if OPTS["eng"].get(n + nm, "V") == "V":
+                        ts(n + nm, sb(b, lo, hi), sb(a, lo, hi), 0.0, None, A.max)
+                        terms += lv
+                    else:
+                        act(n + nm, sb(b, lo, hi), sb(a, lo, hi), F.Abs)
+                        terms += ls
+                j1 = job(2)
+                for i, (l, n) in enumerate(terms):
+                    mm("dif%d" % i + nm, part(j1, l, n), first=i == 0, last=i == len(terms) - 1)
+                if OPTS["eng"].get("nr" + nm, "S") == "S":
+                    act("nr" + nm, sb(near, lo, hi), ps(j1, 0, 1024), F.Sign, bias=-2.0 ** -11, scale=-1.0)
+                else:
+                    ts("nr" + nm, sb(near, lo, hi), ps(j1, 0, 1024), 0.0, -0.5, A.is_lt, A.add)
+            else:
+                cp("xg" + nm, sb(b0, lo, hi), ind(win, lk(uo, side, h)))
+                cp("xc" + nm, sb(b1, lo, hi), ind(win, lk("uc", side, h)))
+                j1, j2 = job(2), job(2)
+                mm("Ag" + nm, part(j1, In, b0), last=False)
+                mm("Ac" + nm, part(j1, I_, b1), first=False)
+                act("sa" + nm, sb(b2, lo, hi), ps(j1, 0, 1024), F.Sign)
+                mm("Bg" + nm, [[(ps(j2, q, q + 512), Im, xh(lo + q, lo + q + 512)),
+                                (ps(j2, q, q + 512), I_, sb(b0, lo + q, lo + q + 512))] for q in (0, 512)], last=False)
+                mm("Bc" + nm, part(j2, I_, b1), first=False)
+                tt("pr" + nm, sb(b3_, lo, hi), ps(j2, 0, 1024), sb(b2, lo, hi), A.mult)
+                ts("nl" + nm, sb(near, lo, hi), sb(b3_, lo, hi), 0.0, -0.5, A.is_lt, A.add)
+            less = [(ps(jc, c, c + 64), In, lk("thr", side, h))] if OPTS.get("off_c") else []
+            mm("cnt" + nm, [ext("zc", ps(jc, c, c + 64), near, lo, less)])
+
+        for grp in OPTS["groups"][t]:
+            jc = job(1)
+            b = min(BLK[x] for x in grp)
+            for x in grp:
+                judge(x[0], x[1], jc, 64 * (BLK[x] - b))
+            pr_ = lambda n: b3(n, b, b + len(grp), 1, 0, 64)
+            w = 64 * len(grp)
+            if OPTS.get("off_c"):
+                act("dec" + R, ps(jc, 0, w), ps(jc, 0, w), F.Sign, bias=-0.5)
+                tt("tt" + R, pr_("tt"), ps(jc, 0, w), pr_("dl"), A.mult)
+                mm("newp" + R, [[(ps(jc, 256, 256 + w), I_, pr_(so)), (ps(jc, 256, 256 + w), sb("jf", 0, 128), pr_("dl")),
+                                 (ps(jc, 256, 256 + w), sb("jf", 0, 128), pr_("tt"))]])
+                act("new" + R, pr_(sn), ps(jc, 256, 256 + w), F.Copy)
+            else:
+                tt("dec" + R, pr_("dec"), ps(jc, 0, w), pr_("thr"), A.is_gt)
+                tt("tt" + R, pr_("tt"), pr_("dec"), pr_("dl"), A.mult)
+                tt("new" + R, pr_(sn), pr_("tt"), pr_(so), A.add)
+            ts("unew" + R, pr_(un), pr_(sn), float(OFF), None, A.add)
+        tile_out("sr" + R, "sr" + R, [lk(sn, "r", 1, 40, 64)], turn_r, RS, float(-V_))
+        send("sr" + R, [(right, sb("sr" + R, 0, 24), sb("gl" + R, 0, 24), "r" + R)])
+        tile_out("sl" + R, "sl" + R, [lk(sn, "l", 0, 0, 24), lk(sn, "r", 0, 0, 8)][:2 - t], turn_l, LS, float(V_))
+        wl = 32 - 8 * t
+        send("sl" + R, [(left, sb("sl" + R, 0, wl), sb("gr" + R, 0, wl), "l" + R)])
+
+        def spread(name, tab, k0, srcs):
+            j0 = job(1)
+            w = sb("fold", 128 * (k0 // 64), 128 * (k0 // 64) + 128)
+            mm(name + "q", [[(ps(j0, s, 128, 2), sb("fm", 256 * s + 128 * i, 256 * s + 128 * i + 128), srcs[i]) for i in (0, 1)]
+                            for s in (0, 1)])
+            cp(name + "f", w, ps(j0, 0, 128))
+            for b in (0, 1):
+                j1 = job(1)
+                c = w[1][0][1] + 64 * b
+                mm(name + "p", [[(ps(j1, i, 512, 8), b3("cw", i, i + 1, 1, 0, 128), sb("fold", c, c + 64))] for i in range(8)])
+                cp(name + "ab"[b], sb(tab, 16 * k0 + 512 * b, 16 * k0 + 512 * b + 512), ps(j1, 0, 512))
+
+        def table(tab, k1):
+            return sb(tab, 0, 16 * k1)
+        for (nm, s, src, k0) in (("tgl", SA, "gl", 0), ("tgr", SB, "gr", 152)):
+            j1 = job(1)
+            mm(nm + R + "p", [[(ps(j1, i, H_, 16), s(i), sb(src + R, 0, 24))] for i in range(16)])
+            cp(nm + R, sb("tb", 16 * k0, 16 * k0 + H_), ps(j1, 0, H_))
+        for h in (0, 1):
+            spread("tb%d%d" % (t, h), "tb", 24 + 64 * h, [lk(sn, "r", h), lk(sn, "l", h)])
+        col = lambda n, h: sb(n, 64 * h, 64 * h + 64)
+        for h in (0, 1):
+            lo, hi = 1024 * h, 1024 * h + 1024
+            nm = "%d%d" % (t, h)
+            cp("back" + nm, sb("ob", lo, hi), ind(table("tb", 88 + 64 * h), lk(un, "l", h)))
+            j1 = job(1)
+            mm("backx" + nm, [ext("z0", ps(j1, 0, 64), "ob", lo, [(ps(j1, 0, 64), In, col("vq", h))])])
+            if OPTS.get("off_b"):
+                act("b1" + nm, col("w1", h), ps(j1, 0, 64), F.Abs)
+                mm("b2" + nm, [[(ps(j1, 64, 128), I_, lk(sn, "l", h)), (ps(j1, 64, 128), sb("jk", 0, 128), col("w1", h))]])
+                tt("b3" + nm, col("a1w", h), ps(j1, 64, 128), col("vq", h), A.min)
+            else:
+                ts("b1" + nm, col("w1", h), ps(j1, 0, 64), 0.0, -4096.0, A.is_equal, A.mult)
+                tt("b2" + nm, col("w2", h), col("w1", h), col("vq", h), A.add)
+                tt("b3" + nm, col("a1w", h), col("w2", h), lk(sn, "l", h), A.max)
+            ts("b4" + nm, col("ua1", h), col("a1w", h), float(OFF), None, A.add)
+            cp("b5" + nm, col("a1h", h), col("a1w", h), default="V")
+            tt("b6" + nm, col("a1l", h), col("a1w", h), col("a1h", h), A.subtract)
+            spread("a1" + nm, "a1t", 24 + 64 * h, [col("a1h", h), col("a1l", h)])
+        for h in (0, 1):
+            lo, hi = 1024 * h, 1024 * h + 1024
+            nm = "%d%d" % (t, h)
+            cp("end" + nm, sb("oe", lo, hi), ind(table("tb", 176), lk(un, "r", h)))
+            j1 = job(1)
+            mm("endx" + nm, [ext("z8", ps(j1, 0, 64), "oe", lo, [(ps(j1, 0, 64), In, col("vq", h))])])
+            ts("g1" + nm, col("w3", h), ps(j1, 0, 64), 0.0, 8192.0, A.not_equal, A.mult)
+        for h in (0, 1):
+            lo, hi = 1024 * h, 1024 * h + 1024
+            nm = "%d%d" % (t, h)
+            cp("a2" + nm, sb("a2t", H_ + lo, H_ + hi), ind(table("a1t", 88 + 64 * h), col("ua1", h)))
+            j1 = job(1)
+            mm("a2x" + nm, [ext("zf", ps(j1, 0, 64), "a2t", H_ + lo)])
+            ts("c1" + nm, col("ua2", h), ps(j1, 0, 64), float(OFF), None, A.add)
+            cp("c2" + nm, col("a2w", h), ps(j1, 0, 64))
+        for h in (0, 1):
+            lo, hi = 1024 * h, 1024 * h + 1024
+            nm = "%d%d" % (t, h)
+            cp("a4" + nm, sb("o4", lo, hi), ind(sb("a2t", 0, H_ + hi), col("ua2", h)))
+            j1 = job(1)
+            p = ps(j1, 0, 64)
+            mm("a4x" + nm, [ext("zf", p, "o4", lo)])
+            ts("d1" + nm, col("ua4", h), p, float(OFF), None, A.add)
+            tt("d2" + nm, col("w4", h), p, col("a2w", h), A.subtract)
+            tt("d3" + nm, col("w5", h), col("w4", h), col("w3", h), A.mult)
+            tt("d4" + nm, col("w6", h), col("w5", h), col("vq2", h), A.add)
+            tt("d5" + nm, col("w7", h), p, col("w6", h), A.max)
+            ts("d6" + nm, col("uix", h), col("w7", h), float(OFF), None, A.add)
+        for h in (0, 1):
+            lo, hi = 1024 * h, 1024 * h + 1024
+            cp("xa4%d%d" % (t, h), sb(xw, H_ + lo, H_ + hi), ind(sb(xw, XO, own + hi), col("ua4", h)))
+        for h, (lo, hi) in enumerate(OPTS["cut"][t]):
+            nm = "%d%d" % (t, h)
+            cp("xs" + nm, sb("xs", lo, hi), ind(sb(xw, 0, own + hi), sb("uix", lo // 16, hi // 16)))
+            mv = lambda jj, c, a, b, c0: [(ps(jj, c, c + b - a), sb("ja", c0, c0 + 128), xh(a, b)),
+                                          (ps(jj, c, c + b - a), sb("jb", c0, c0 + 128), sb("xs", a, b))]
+            turn = t == 0 and ((turn_r and hi == V_) or (turn_l and lo == 0))
+            ea, eb = (V_ - H_, V_) if hi == V_ else (0, H_)
+            if turn:
+                j2 = job(1)
+                mm("Xmve" + nm, [mv(j2, 0, ea, eb, RS if hi == V_ else LS)])
+                ts("Xcle" + nm, sb("es1" if hi == V_ else "et1", 0, H_), ps(j2, 0, H_), 0.0, 4.0, A.max, A.min)
+            j1 = job(2 if hi - lo > 512 else 1)
+            mm("mv" + nm, [mv(j1, q, lo + q, min(hi, lo + q + 512), 0) for q in range(0, hi - lo, 512)])
+            if t == 0:
+                ts("cl" + nm, sb("xh1", H_ + lo, H_ + hi), ps(j1, 0, hi - lo), 0.0, 4.0, A.max, A.min)
+                src = sb("xh1", H_ + ea, H_ + eb)
+                if turn:
+                    e1 = sb("es1" if hi == V_ else "et1", 0, H_)
+                    src = (e1[0], e1[1] + src[1]) + e1[2:]
+                if hi == V_:
+                    send("sx1r", [(right, src, sb("xh1", 0, H_), "x1l")])
+                if lo == 0:
+                    send("sx1l", [(left, src, sb("xh1", XO, W_), "x1r")])
+                cp("cast%d" % h, sb("xw1", own + lo, own + hi), sb("xh1", H_ + lo, H_ + hi))
+            else:
+                ts("cl" + nm, sb("x2", lo, hi), ps(j1, 0, hi - lo), 0.0, 4.0, A.max, A.min)
+                dma("xe" + nm, "Y", hbm(lambda lo=lo, hi=hi: T.xe[:, lo:hi]), sb("x2", lo, hi), 4 * (hi - lo))
+        if t == 0:
+            cp("castl", sb("xw1", XO, own), sb("xh1", 0, H_))
+            cp("castr", sb("xw1", own + V_, XO + W_), sb("xh1", XO, W_))
+        m2, m4, c2, c4 = "m2t" + R, "m4t" + R, "m2c" + R, "m4c" + R
+        for h in (0, 1):
+            lo, hi = 1024 * h, 1024 * h + 1024
+            nm = "%d%d" % (t, h)
+            tt("m2" + nm, sb(m2, H_ + lo, H_ + hi), ind(sb(xw, XO, own + hi), col("ua1", h)), xh(lo, hi), A.max)
+            dma("m2c" + nm, "Y", sb(c2, lo, hi), sb(m2, H_ + lo, H_ + hi), 1024 * wide[m2])
+        for h in (0, 1):
+            lo, hi = 1024 * h, 1024 * h + 1024
+            nm = "%d%d" % (t, h)
+            tt("m4" + nm, sb(m4, H_ + lo, H_ + hi), ind(sb(m2, 0, H_ + hi), col("ua2", h)), sb(c2, lo, hi), A.max)
+            k4 = dma("m4c" + nm, "Y", sb(c4, lo, hi), sb(m4, H_ + lo, H_ + hi), 1024 * wide[m2])
+            tt("m8" + nm, sb("mm", lo, hi), ind(sb(m4, 0, H_ + hi), col("ua4", h)), sb(c4, lo, hi), A.max)
+            j1 = job(2)
+            how = OPTS["eng"].get("rn" + nm, "V")
+            if how != "P":
+                tt("dn" + nm, sb("dn", lo, hi), ind(win, lk(un, "r", h)), xh(lo, hi), A.subtract)
+            if how == "P":
+                cp("dn" + nm, sb("dn", lo, hi), ind(win, lk(un, "r", h)))
+                mm("ad" + nm, [[(ps(j1, q, q + 512), In, xh(lo + q, lo + q + 512)), (ps(j1, q, q + 512), I_, sb("dn", lo + q, lo + q + 512))]
+                               for q in (0, 512)], [k4])
+                act("rn" + nm, ps(j1, 0, 1024), ps(j1, 0, 1024), F.Abs)
+                act("exp" + nm, ps(j1, 0, 1024), ps(j1, 0, 1024), F.Exp, scale=-1.0)
+            elif how == "V":
+                ts("rn" + nm, sb("rn", lo, hi), sb("dn", lo, hi), 0.0, None, A.max)
+                mm("ad" + nm, [[(ps(j1, q, q + 512), l, sb(n, lo + q, lo + q + 512)) for (l, n) in ((In, "dn"), (I2, "rn"))]
+                               for q in (0, 512)], [k4])
+                act("exp" + nm, ps(j1, 0, 1024), ps(j1, 0, 1024), F.Exp, scale=-1.0)
+            else:
+                act("rn" + nm, sb("rn", lo, hi), sb("dn", lo, hi), F.Abs)
+                act("exp" + nm, ps(j1, 0, 1024), sb("rn", lo, hi), F.Exp, scale=-1.0, after=[k4])
+            tt("y" + nm, sb("yy", lo, hi), ps(j1, 0, 1024), sb("mm", lo, hi), A.mult)
+            out = hbm(lambda lo=lo, hi=hi: T.ye[:, lo:hi])
+            if t == 0:
+                ydone.append(dma("ye" + nm, "Y", out, sb("yy", lo, hi), 4096))
+            else:
+                dma("ye" + nm, "G", out, sb("yy", lo, hi), 8192, [ydone[h]], accum=True)
+
+    return ops, bank, sent, Q
+
+
+def rank_program(g, core, T, topo):
+    rank = T.rank_of(core)
+    if rank is None:
+        return
+    both = OPTS.get("both", False)
+    ops, bank, sent, Q = plan(g, core, T, topo, both or rank == len(T.cores) - 1, both or rank == 0)
+    names = [op["name"] for op in plan(g, core, T, topo, True, True)[0]]
+    order = issue_order(ops, names, OPTS["order"]) if OPTS["order"] else schedule(ops, MODEL, OPTS)[0]
+    DEBUG[rank] = (ops, order, None)
+    bk, extra = deal_banks(ops, order)
+    bank.update(bk)
+    DEBUG[rank] = (ops, order, extra)
+    place = {k: i for i, k in enumerate(order)}
+    count = {}
+    token = {}
+    clock = {}
+    known = {e: {} for e in Q}
+    for k in order:
+        op = ops[k]
+        e = op["eng"]
+        if e is None:
+            token[k] = op["sem"]
+            clock[k] = dict([op["sem"]])
+            continue
+        kn = known[e]
+        need = sorted([p for p in set(op["pre"] + extra.get(k, [])) if p in token], key=lambda p: -place[p])
+        for p in need:
+            s, v = token[p]
+            if kn.get(s, 0) < v and not (e == "P" and s == "cP"):
+                Q[e].wait_ge(T.sem[s], v)
+                for s2, v2 in clock[p].items():
+                    kn[s2] = max(kn.get(s2, 0), v2)
+        ins = op["emit"]()
+        if op["sem"]:
+            ins[0].then_inc(T.sem[op["sem"][0]], 16)
+            token[k] = op["sem"]
+        elif op["ninc"]:
+            s = "c" + e
+            for i in ins:
+                i.then_inc(T.sem[s], 1)
+            count[s] = count.get(s, 0) + op["ninc"]
+            token[k] = (s, count[s])
+        if k in token:
+            clock[k] = dict(kn)
+            clock[k][token[k][0]] = max(token[k][1], kn.get(token[k][0], 0))
+    total = dict(count)
+    total["sent"] = sent[0]
+    for k in order:
+        if ops[k]["sem"]:
+            total[ops[k]["sem"][0]] = ops[k]["sem"][1]
+    waited = {}
+    for e in Q:
+        for s, v in known[e].items():
+            waited[s] = max(waited.get(s, 0), v)
+    for s, v in total.items():
+        if waited.get(s, 0) < v:
+            g.wait_ge(T.sem[s], v)

@@ -2,214 +2,161 @@ from concourse.bass import DstId, RemoteDMATransfer
 from concourse.mybir import AluOpType as A, ActivationFunctionType as F
 
 V_, H_, W_ = 2048, 384, 2816
+PAD = 16
 XO = V_ + H_
+XW = PAD
+XA = XW + W_ + PAD
 OFF = 1408
-BLK = {("r", 0): 0, ("r", 1): 1, ("l", 0): 2, ("l", 1): 3}
+BLK = {("r", 0): 0, ("r", 1): 64, ("l", 0): 128, ("l", 1): 192}
+TA = XO + 128
+TB = TA + XO
 
 
 def scratch():
     s = {"ps": ("psum", [128, 4096], "float32")}
 
-    def add(names, shape, dt):
-        for n in names.split():
-            s[n] = ("sbuf", [128] + shape, dt)
-    add("xw0", [XO + W_], "bfloat16"); add("xh0 m2c0 m4c0", [V_], "bfloat16"); add("m2t0 m4t0", [XO], "bfloat16")
-    add("es0 et0", [H_], "bfloat16")
-    add("xw1", [XO + W_], "float32"); add("xh1", [W_], "float16"); add("es1 et1", [H_], "float16")
-    add("m2c1 m4c1 yy x2", [V_], "float32"); add("m2t1 m4t1", [XO], "float32"); add("a2t", [XO], "bfloat16")
-    add("dc de rc re nr xc xg sa pr nl ob oe o4 mm dn rn xs", [V_], "float16")
-    add("tb", [W_], "float32"); add("a1t", [XO], "bfloat16")
-    add("fold", [256], "float16"); add("fm", [512], "float16"); add("cw", [8, 128], "float16")
-    add("a1h", [128], "bfloat16"); add("a1l", [128], "float16")
-    add("li", [4, 64], "int32"); add("st0 st1 st2", [4, 64], "float16"); add("ul0 ul1 ul2 uc", [4, 64], "uint16")
-    add("thr", [4, 64], "bfloat16"); add("dl tt", [4, 64], "float32"); add("dec", [4, 64], "float16")
-    add("w1", [128], "bfloat16"); add("jk", [128], "float16"); add("jf", [128], "float32")
-    add("vq a1w a2w w2 w3 w4", [128], "float16"); add("vq2 vi w5 w6 w7", [128], "float32")
-    add("ua1 ua2 ua4 uix", [128], "uint16")
-    add("sb0 gb0", [16], "float16"); add("sr0 sr1 gl0 gl1", [24], "float16"); add("sl0 sl1 gr0 gr1", [32], "float16")
-    add("dd dm", [256], "int32"); add("jj ja jb", [256], "float16"); add("jn j2 jm s1 s3", [128], "float16")
-    add("zc z0 z8 zf", [144], "float16"); add("cv", [16, 136], "float16")
-    add("pi", [4], "int32"); add("pm c15", [4], "float32"); add("rr oh no", [16], "float32")
+    def add(names, n, dt):
+        for name in names.split():
+            s[name] = ("sbuf", [128, n], dt)
+    add("xw0", XA + XO, "bfloat16"); add("xh0 m2c0 m4c0 pr pl", V_, "bfloat16"); add("m2t0 m4t0 a2t", XO, "bfloat16")
+    add("es0 et0", H_, "bfloat16"); add("es1 et1 glo", H_, "float32")
+    add("xw1", XA + XO, "float32"); add("m2c1 m4c1 yy0 yy1", V_, "float32"); add("m2t1 m4t1", XO, "float32")
+    add("xh1 er ar el al ob oe o4 xs mm0 mm1 dn0 dn1 rn", V_, "float16")
+    add("tb", TB + V_ + 512, "float32")
+    add("li", 256, "int32"); add("st0 st1 st2 msk", 256, "float16"); add("ul0 ul1 ul2 uc0 uc1", 256, "uint16")
+    add("tt", 256, "float32"); add("xt0 xt1", 352, "float32"); add("xa0 xa1", 256, "float32")
+    add("gl0 gl1 gr1", 32, "float32"); add("gr0", 64, "float32"); add("ge", 2, "float16")
+    add("w1 nh", 128, "bfloat16"); add("vq a1w a2w a4w w3 w4 one", 128, "float16"); add("vi v2 w5 w6 w7 jf", 128, "float32")
+    add("ua10 ua20 ua40 ua11 ua21 ua41 uix", 128, "uint16")
+    add("sb0 gb0 kb", 16, "float16")
+    add("dd dm", 256, "int32"); add("jj ja jb je jo", 256, "float16"); add("jn j2 jm jk s1 s3 s15", 128, "float16")
+    add("zc z0 z8 zf", 144, "float16")
+    add("pi", 4, "int32"); add("pm", 8, "float32"); add("rr oh no", 16, "float32")
     return s
 
 
 SCRATCH = scratch()
-NDMA = 40
+NDMA = 90
 SEMAPHORES = ["cV", "cS", "cP", "cG", "sent"] + ["d%d" % k for k in range(NDMA)] + \
     ["x0l", "x0r", "b0", "r0", "l0", "x1l", "x1r", "r1", "l1"]
 
-MODEL = dict(cyc=0.83e-3 * 1.25, gat=1.56, fix=0.06, pe=0.42e-3 * 1.25, hop=0.1, dma=2.0, dmab=0.22e-3, iss=0.06,
-             giss=1.0, riss=0.8, rlat=2.2, remb=1.6e-3, gfix=0.17, exp1=1.3)
-DIGITS = "0123456789abcdefghijklmnopqrstuvwxyz"
-ENG = "moder00:S model00:V model10:V moder10:S rel00:S rcl10:S rn00:P rn01:P rn10:S rn11:V tb00a:V tb01a:V tb01b:V back01:V end00:V a200:V c200:V c201:V cast0:G cast1:G cast3:G castl:V dn00:V tb10b:V back10:V c211:V a410:V"
-ORDER = "000f0e010302040d110m0n0h0p0i0g060k0l0q0s120t0j0o0y090a15190x1b13051d1g1c1e0z0v0u10141h1i1a0w0r1l071f080b1n0c1x1m1k1o1z1j2b332g1y1p21202223242d2c252e2p262q2h2728292s322f343g3h352i1s373i2a2j382r362t392u2v1t2k1q3a2l1r3b2w2m2x3c2n3d3j3p2y3e2z3q3x2o303t313f3v3y3z3u3w3k164041424d434e3m3l44454f474g484h464j4b494i4k4l4n6b176r184c4a4m4v3n3o3r4o6d4w4x3s4p4z504q4s516c1v6f4y1u53545b4r52555j6e5c1w6g4t566i5d5k5e6x4u575f585g595h6j5a5l5o5i5t6o6p5m5w5u6k5p5n5q5x5v5y5z5r656z666l6y6h6s61676t726u626q6369706a646v6068715s7k7p7m767l7a8b77787n7o7b6m7q797c8g7y7r7d7z8d808c8e8h7e7f827g8f8i837h8j7i7s7j81848k8p85868q7t8l8m8n878897898t958u7u8o8r8v8w7v7w938s9196bk9892948a8x8y9l8z90a0999m7x9xbl9n9o9aa19b9p9c9d9r9f9g9s9j9v9t9e9q9h9k9w9ub7a2b5bc9i9ya79za8a9aa7574b8b66nbh73a3a4a5abajakala6bdasb9acadaebibmaramafanagaoahapaibjaqbn6wbobpbabbbebfatauavaxayawazb0b1b2b3bgb4"
-ENG = "moder00:S model00:V model10:V moder10:S rel00:S rcl10:S rn00:P rn01:P rn10:S rn11:V tgl0:V tb00f:V back00:V a100a:V a100b:V a101f:V a101b:V a200:V c200:V cast0:G cast1:G cast2:G cast3:V tgl1:V tb11a:V a110a:V a111f:V a111b:V c210:V"
-ORDER = "0e0f01030a0002040c110g0d0h120i1d0m0k160n0j091h0l1c1j060807131l1k0y0q19140p0r0v0x0o1e0s0t171i0u1f1o1a1p1g050b1q0w1s3a1b100z183b2j1m1n1v1x2526273c292y3f3d3e3g1w2k2a282b1r3h2c2o2d2l2m2e2x212z2p3i302f2n1t1u1z2g2h31321y203o333p342q3j2r3k2s352i3l3m2t472u36482v3q154b3738413s42494c45393u433r3t3v463x3n3y444a4r4d4e4f4g4h774s3w3z4t4j4k404u4l4i2w4v4x4w4m4p4y4q4n4o4z5051535b58555954525c565f5g5d5j7d5a6t5e5k5h576r5m5l5n5r5s5i5z5o5u5t605v5p5w5q23226u5x74246s6162645y696v636c656d6a6b7e7578666e76676f6h6i6l6j6y6m796n7f6o7a686g7b6q6k6p80817m7n85827o7q7p867g7h837r8r848e7s877t8w887i7u8i8t8f7v897w8g7x8s8u8h8j7y958x8v8k968a8l8y8b7z8z6w6z8m70908c8n8o8p99919h928d93c8719a9i979b9c989n9l9j9d9o9r9p9e9m9k949s8q9q9t9ua79fa89galao6xc09v9wa99xaaab9y9zada0aebtafaca1a2aga3a5ahc1aja4a6amaibvakapanarav7k7lbu7jbw72asatauawbxaxaqazb0b7ayb8c5b1b2b3bfb9bgbab4bbb573bybcb6bdc2c9bzbebhc6c7c3c4cabicb7cccbjbkbpbqblbrbmbsbnbocd"
-OPTS = dict(eps=0.12, eng=dict(x.split(":") for x in ENG.split()), off={}, order=ORDER,
-            groups=[[[("r", 1)], [("r", 0)], [("l", 0)], [("l", 1)]]] * 2,
-            cut=[[(0, 384), (1664, 2048), (384, 1024), (1024, 1664)], [(0, 768), (768, 1536), (1536, 2048)]])
+MODEL = dict(cyc=0.83e-3 * 1.15, gat=1.56, fix=0.06, pe=0.42e-3 * 1.15, hop=0.1, dma=1.7, dmab=0.22e-3, iss=0.06,
+             giss=1.0, riss=0.8, rlat=2.0, remb=1.2e-3, gfix=0.17, exp1=1.3)
+ST = ('b110:V cast00:V d200:V d201:V newl00:V newl01:V newl10:V newl11:V newr10:V newr11:V rn00:S rn01:V rn11:V xcl01:S xcl11:S',
+'a201 a211 a400 a401 back01 cl01 cl10 cl11 dn00 dn11 end00 end10 exp01 m200 m201 m211 m400 m411 nrl01 nrl11 nrr10 prl00 prl01 prl11 sal01 sal11 xa401 xcl00 xel10 xer00 xer11 xs01 xs10 xs11 y11',
+'xer01 xer00a xcl01 xel01 xel00 sal01 nrl00 back00 back01 end00 end01 a201 a400 xa400 xs00 xa401 xs01 rn00 xer11 xer10 xel10 xel11 nrr11 xcl11 nrr10a exp00 nrr10b sal11 nrl10 dn10 exp01 back10 rn10 back11 end10 end11 a210 a211 a410 a411 exp10 xa410 exp11 xs10a xa411 xs10b xs11',
+'xer00b xcr01 xcr00 prr01 nrr01 prr00 nrr00 xcl00 prl00 prl01 nrl01 dn00 m200 m201 a200 m400 a401 dn01 cl00 cl01 m401 xcr11 xcr10 prr11 prr10 rn01 xcl10 prl10 m800 prl11a prl11b nrl11 dn11 y00 m210 m211 m801 rn11 m410 m411 y01 m810 m811 y10 y11 cl10 cl11', 0.2)
+ENG = dict(x.split(":") for x in ST[0].split())
+SPLIT = set(ST[1].split())
+ORDER = {"S": ST[2].split(), "V": ST[3].split()}
+SHIFT = dict(sx1r=20, sx1l=20, ld_rt=9, ld_lf=9, st0=9, Xsb0=9, sb0=9, sb0_2=9)
+OPTS = dict(big=50.0, soon=ST[4], lead={"su": 3, "di": 2})
+ORDERS = {}
 DEBUG = {}
 
 
-def cost(op, m):
-    k, n = op["c"]
+def cost(eng, c, m):
+    k, n = c
     if k == "g":
         return m["fix"] + n * m["gat"] * m["cyc"], 0.0
     if k == "e":
         return m["fix"] + max(n, 64) * m["cyc"], 0.0
+    if k == "x":
+        return m["fix"] + m["exp1"], 0.0
     if k == "pe":
         return n * m["pe"] + 0.05, 0.0
     if k == "gp":
         return m["gfix"] + 2 * n * m["cyc"], 0.0
     if k == "dma":
-        return (m["giss"] if op["eng"] == "G" else m["iss"]), m["dma"] + n * m["dmab"]
+        return (m["giss"] if eng == "G" else m["iss"]), m["dma"] + n * m["dmab"]
     if k == "rem":
         return m["riss"], 0.0
     return 0.0, m["rlat"] + n * m["remb"]
 
 
-def deal_banks(ops, order):
-    jobs = {}
-    for k in order:
-        if ops[k]["job"]:
-            jobs.setdefault(ops[k]["job"][0], []).append(k)
-    holder = [None] * 8
-    since = [-1] * 8
-    bank = {}
-    extra = {}
-    for pos, k in enumerate(order):
-        jb = ops[k]["job"]
-        if not jb:
-            continue
-        j, size = jb
-        if j not in bank:
-            best = None
-            for b in range(0, 8, size):
-                if size == 2:
-                    if since[b] is None or since[b + 1] is None:
-                        continue
-                    key = max(since[b], since[b + 1])
-                else:
-                    if since[b] is None:
-                        continue
-                    key = since[b] - (1000 if since[b ^ 1] is None else 0)
-                if best is None or key < best[0]:
-                    best = (key, b)
-            if best is None:
-                raise ValueError("no PSUM bank left")
-            b = best[1]
-            bank[j] = b
-            extra[k] = [p for i in range(size) if holder[b + i] is not None for p in jobs[holder[b + i]]]
-            for i in range(size):
-                holder[b + i] = j
-                since[b + i] = None
-        if k == jobs[j][-1]:
-            for i in range(size):
-                since[bank[j] + i] = pos
-    return bank, extra
-
-
-def issue_order(ops, names, code):
-    where = {op["name"]: k for k, op in enumerate(ops)}
-    order = []
-    placed = set()
-
-    def put(k):
-        for p in ops[k]["pre"]:
-            if p not in placed:
-                put(p)
-        placed.add(k)
-        order.append(k)
-    for i in range(0, len(code), 2):
-        k = where.get(names[DIGITS.index(code[i]) * len(DIGITS) + DIGITS.index(code[i + 1])])
-        if k is not None and k not in placed:
-            put(k)
-    for k in range(len(ops)):
-        if k not in placed:
-            put(k)
-    return order
-
-
-def schedule(ops, m, opts):
+def schedule(ops, m):
     n = len(ops)
-    succ = [[] for _ in range(n)]
-    for k, op in enumerate(ops):
-        for p in op["pre"]:
-            succ[p].append(k)
-    cs = [cost(op, m) for op in ops]
-    prio = [0.0] * n
-    for k in range(n - 1, -1, -1):
-        prio[k] = cs[k][0] + cs[k][1] + m["hop"] + max([prio[s] for s in succ[k]] + [0.0])
-    for k in range(n):
-        prio[k] += opts["off"].get(ops[k]["name"], 0.0)
-    jobs = {}
-    for k, op in enumerate(ops):
-        if op["job"]:
-            jobs.setdefault(op["job"][0], []).append(k)
-    left = {j: len(v) for j, v in jobs.items()}
-    holder = [None] * 8
-    bank = {}
-    fin = [None] * n
-    start = [None] * n
-    free = {}
+    if "cs" not in ops[0]:
+        cs = [[cost(e, c, m) for (e, c, _f) in op["alt"]] for op in ops]
+        path = [0.0] * n
+        for k in range(n - 1, -1, -1):
+            path[k] = sum(cs[k][0]) + m["hop"] + max([path[s] for s in ops[k]["suc"]] + [0.0])
+        jobs = {}
+        for k, op in enumerate(ops):
+            if op["job"]:
+                jobs.setdefault(op["job"][0], []).append(k)
+        ops[0]["cs"] = (cs, path, jobs, {op["name"]: k for k, op in enumerate(ops)})
+    cs, path, jobs, where = ops[0]["cs"]
     wait = [len(op["pre"]) for op in ops]
-    ready = [k for k in range(n) if wait[k] == 0]
-    order = []
-    extra = [[] for _ in range(n)]
+    on, nxt = {}, {}
+    for e, names in ORDER.items():
+        ks = [where[y] for x in names for y in (x, x + "a", x + "b") if y in where]
+        on.update({k: e for k in ks})
+        for i in range(1, len(ks)):
+            nxt.setdefault(ks[i - 1], []).append(ks[i])
+            wait[ks[i]] += 1
+            job = ops[ks[i]]["job"]
+            first = jobs[job[0]][0] if job else None
+            if job and ops[first]["eng"] == "P" and ks[i] == jobs[job[0]][[ops[x]["eng"] == "P" for x in jobs[job[0]]].index(False)]:
+                a = ks[max(0, i - OPTS["lead"].get(ops[first]["name"][:2], 1))]
+                nxt.setdefault(a, []).append(first)
+                wait[first] += 1
+    prio = [p + SHIFT.get(op["name"], 0.0) - (OPTS["big"] if k in on else 0.0) for k, (p, op) in enumerate(zip(path, ops))]
+    left = {j: len(v) for j, v in jobs.items()}
+    holder, freed = [None] * 8, [0.0] * 8
+    bank, extra, free, order = {}, {}, dict.fromkeys(["V", "S", "P", "G", "Y", None], 0.0), []
+    can = [[(a, e) for a, (e, _c, _f) in enumerate(op["alt"]) if on.get(k, e) == e] for k, op in enumerate(ops)]
+    jobof, soon = [op["job"] for op in ops], OPTS["soon"]
+    rdy, beg, fin, use = [0.0] * n, [0.0] * n, [0.0] * n, [0] * n
+    ready = [k for k in range(n) if not wait[k]]
 
-    def banks_for(size):
-        best = None
-        for b in range(0, 8, size):
-            hs = [holder[b + i] for i in range(size)]
-            if any(h is not None and left[h] > 0 for h in hs):
-                continue
-            t = max([fin[k] for h in hs if h is not None for k in jobs[h]] + [0.0])
-            o = holder[b ^ 1]
-            key = (t, b) if size == 2 else (t + (0.0 if (o is not None and left[o] > 0) or b >= 6 else 1.0), -b)
-            if best is None or key < best[0]:
-                best = (key, b, t)
-        return best
+    def banks(size):
+        fits = [b for b in range(0, 8, size) if all(h is None or not left[h] for h in holder[b:b + size])]
+        lone = lambda b: size == 1 and (holder[b ^ 1] is None or not left[holder[b ^ 1]])
+        return min(fits, key=lambda b: (lone(b), max(freed[b:b + size]), -b)) if fits else None
     while ready:
+        spare = {}
         cand = []
         for k in ready:
-            op = ops[k]
-            t = max([fin[p] + m["hop"] for p in op["pre"]] + [free.get(op["eng"], 0.0)])
-            b = None
-            if op["job"] and op["job"][0] not in bank:
-                b = banks_for(op["job"][1])
+            t, job = rdy[k], jobof[k]
+            if job and job[0] not in bank:
+                if job[1] not in spare:
+                    spare[job[1]] = banks(job[1])
+                b = spare[job[1]]
                 if b is None:
                     continue
-                t = max(t, b[2] + m["hop"])
-            cand.append((t, k, b))
+                t = max(t, max(freed[b:b + job[1]]) + m["hop"])
+            for a, e in can[k]:
+                cand.append((t if t > free[e] else free[e], -prio[k], a, k, e))
         if not cand:
-            raise ValueError("no PSUM bank left")
-        t0, k0, _b = min(cand, key=lambda c: (c[0], -prio[c[1]]))
-        e = ops[k0]["eng"]
-        t, k, b = max([c for c in cand if ops[c[1]]["eng"] == e and c[0] <= t0 + opts["eps"]], key=lambda c: prio[c[1]])
-        op = ops[k]
-        if b is not None:
-            j, size = op["job"]
-            for i in range(size):
-                h = holder[b[1] + i]
-                if h is not None:
-                    extra[k] += jobs[h]
-                holder[b[1] + i] = j
-            bank[j] = b[1]
-        if op["job"]:
-            left[op["job"][0]] -= 1
-        start[k] = t
-        if op["eng"]:
-            free[op["eng"]] = t + cs[k][0]
-        fin[k] = t + cs[k][0] + cs[k][1]
+            return None
+        t0, _p, _a, _k, e = min(cand)
+        _p, t, use_k, k = min([(c[1], c[0], c[2], c[3]) for c in cand if c[4] == e and c[0] <= t0 + soon])
+        use[k], job = use_k, jobof[k]
+        beg[k], fin[k] = t, t + sum(cs[k][use_k])
+        if e:
+            free[e] = t + cs[k][use_k][0]
+        if job:
+            j, size = job
+            if j not in bank:
+                b = bank[j] = spare[size]
+                extra[k] = [p for h in holder[b:b + size] if h is not None for p in jobs[h]]
+                holder[b:b + size] = [j] * size
+            left[j] -= 1
+            for b in range(bank[j], bank[j] + size):
+                freed[b] = max(freed[b], fin[k])
         order.append(k)
         ready.remove(k)
-        for s in succ[k]:
+        for s in ops[k]["suc"] + nxt.get(k, []):
             wait[s] -= 1
-            if wait[s] == 0:
+            rdy[s] = max(rdy[s], t)
+            if not wait[s]:
                 ready.append(s)
-    if len(order) != n:
-        raise ValueError("calls left over")
-    return order, bank, extra, start, fin
+        for s in ops[k]["suc"]:
+            rdy[s] = max(rdy[s], fin[k] + m["hop"])
+    if len(order) < n:
+        return None
+    return max(fin), order, bank, extra, use, beg
 
 
 def plan(g, core, T, topo, turn_r, turn_l):
@@ -228,16 +175,12 @@ def plan(g, core, T, topo, turn_r, turn_l):
     wide = {n: (2 if s[2] in ("float16", "bfloat16", "uint16") else 4) for n, s in SCRATCH.items()}
 
     def sb(name, lo, hi, step=1):
-        return (lambda: T[name][:, lo:hi:step] if step > 1 else T[name][:, lo:hi], [(name, lo, hi)], None,
+        rng = [(name, lo, hi)] + ([("tb8", lo, hi)] if name == "tb" else [])
+        return (lambda: T[name][:, lo:hi:step] if step > 1 else T[name][:, lo:hi], rng, None,
                 (hi - lo + step - 1) // step, wide[name])
 
-    def b3(name, k0, k1, ks, c0, c1):
-        inner = SCRATCH[name][1][2]
-        ks_ = list(range(k0, k1, ks))
-        rng = [(name, k * inner + c0, k * inner + c1) for k in ks_] if ks > 1 else [(name, k0 * inner, k1 * inner)]
-        if len(ks_) == 1:
-            return (lambda: T[name][:, k0, c0:c1], [(name, k0 * inner + c0, k0 * inner + c1)], None, c1 - c0, wide[name])
-        return (lambda: T[name][:, k0:k1:ks, c0:c1], rng, None, len(ks_) * (c1 - c0), wide[name])
+    def row(name, p, lo, hi):
+        return (lambda: T[name][p:128:16, lo:hi], [(name + ("8" if p and name == "tb" else ""), lo, hi)], None, hi - lo, wide[name])
 
     def ps(job, lo, hi, step=1):
         return (lambda: T.ps[:, 512 * bank[job[0]] + lo:512 * bank[job[0]] + hi:step], [], job, (hi - lo + step - 1) // step, 4)
@@ -248,8 +191,10 @@ def plan(g, core, T, topo, turn_r, turn_l):
     def hbm(f):
         return (f, [], None, 0, 0)
 
-    def add(name, eng, c, outs, ins, emit, after=(), ninc=1, sem=None):
+    def add(name, eng, c, outs, ins, emit, after=(), ninc=1, sem=None, alt=None):
         k = len(ops)
+        if alt:
+            eng = "?%d" % k
         pre = set(after)
         job = None
         for lst, wr in ((ins, False), (outs, True)):
@@ -270,45 +215,62 @@ def plan(g, core, T, topo, turn_r, turn_l):
         seen[name] = seen.get(name, 0) + 1
         if seen[name] > 1:
             name = "%s_%d" % (name, seen[name])
-        ops.append(dict(name=name, eng=eng, c=c, pre=sorted(pre), job=job, emit=emit, ninc=ninc, sem=sem))
+        ops.append(dict(name=name, eng=eng, alt=alt or [(eng, c, emit)], pre=sorted(pre), suc=[], job=job, ninc=ninc, sem=sem))
+        for p in pre:
+            ops[p]["suc"].append(k)
         return k
+
+    def pick(name, choices):
+        DEBUG.setdefault("flex", {})[name] = choices
+        return ENG.get(name, choices[0])
+
+    def pieces(name, h):
+        DEBUG.setdefault("split", set()).add(name)
+        lo = 1024 * h
+        return [("a", lo, lo + 512), ("b", lo + 512, lo + 1024)] if name in SPLIT else [("", lo, lo + 1024)]
 
     def cyc(out, ins):
         return out[3] * (0.5 if all(o[4] == 2 for o in [out] + ins) else 1.0)
 
-    def ts(name, out, a, s1, s2, o0, o1=None, after=()):
-        ex = [s for s in (s1, s2) if isinstance(s, tuple)]
+    def ts_form(out, a, s1, s2, o0, o1):
         v = lambda s: s[0]() if isinstance(s, tuple) else s
         if o1 is None:
-            f = lambda: [g.vector.tensor_scalar(out[0](), a[0](), v(s1), None, o0)]
-        else:
-            f = lambda: [g.vector.tensor_scalar(out[0](), a[0](), v(s1), v(s2), o0, o1)]
-        return add(name, "V", ("e", cyc(out, [a])), [out], [a] + ex, f, after)
+            return ("V", ("e", cyc(out, [a])), lambda: [g.vector.tensor_scalar(out[0](), a[0](), v(s1), None, o0)])
+        return ("V", ("e", cyc(out, [a])), lambda: [g.vector.tensor_scalar(out[0](), a[0](), v(s1), v(s2), o0, o1)])
 
-    def tt(name, out, a, b, o, after=()):
+    def act_form(out, a, fn, bias=None, scale=None, c=None):
+        def f():
+            kw = {}
+            for key, s in (("bias", bias), ("scale", scale)):
+                if s is not None:
+                    kw[key] = s[0]() if isinstance(s, tuple) else s
+            return [g.scalar.activation(out[0](), a[0](), fn, **kw)]
+        return ("S", c or ("g" if a[4] == 0 else "e", out[3]), f)
+
+    def ts(name, out, a, s1, s2, o0, o1=None):
+        e, c, f = ts_form(out, a, s1, s2, o0, o1)
+        return add(name, e, c, [out], [a] + [s for s in (s1, s2) if isinstance(s, tuple)], f)
+
+    def tt(name, out, a, b, o):
         c = ("g", out[3]) if a[4] == 0 else ("e", out[3] * (1 if a[2] or b[2] else 2))
-        return add(name, "V", c, [out], [a, b], lambda: [g.vector.tensor_tensor(out[0](), a[0](), b[0](), o)], after)
+        return add(name, "V", c, [out], [a, b], lambda: [g.vector.tensor_tensor(out[0](), a[0](), b[0](), o)])
 
-    def act(name, out, a, fn, bias=None, scale=None, after=()):
-        kw = {}
-        if bias is not None:
-            kw["bias"] = bias
-        if scale is not None:
-            kw["scale"] = scale
-        c = ("g", out[3]) if a[4] == 0 else ("e", out[3])
-        return add(name, "S", c, [out], [a], lambda: [g.scalar.activation(out[0](), a[0](), fn, **kw)], after)
+    def act(name, out, a, fn, bias=None, scale=None, after=(), c=None):
+        e, c, f = act_form(out, a, fn, bias, scale, c)
+        return add(name, e, c, [out], [a] + [s for s in (bias, scale) if isinstance(s, tuple)], f, after)
 
-    def cp(name, out, a, after=(), default="S"):
-        e = OPTS["eng"].get(name, default)
-        DEBUG.setdefault("flex", {})[name] = {"S": ("g" if a[4] == 0 else "e", out[3]), "G": ("gp", out[3]),
-                                              "V": ("g", out[3]) if a[4] == 0 else ("e", cyc(out, [a]))}
-        if e == "S":
-            return act(name, out, a, F.Copy, after=after)
-        if e == "G":
-            return add(name, "G", ("gp", out[3]), [out], [a],
-                       lambda: [g.affine_select(out[0](), a[0](), [[0, out[3]]], A.is_ge, 0.0, 0, 0)], after)
-        c = ("g", out[3]) if a[4] == 0 else ("e", cyc(out, [a]))
-        return add(name, "V", c, [out], [a], lambda: [g.vector.tensor_copy(out[0](), a[0]())], after)
+    def cp(name, out, a, choices="SV"):
+        alt = {"S": act_form(out, a, F.Copy),
+               "V": ("V", ("g", out[3]) if a[4] == 0 else ("e", cyc(out, [a])), lambda: [g.vector.tensor_copy(out[0](), a[0]())]),
+               "G": ("G", ("gp", out[3]), lambda: [g.affine_select(out[0](), a[0](), [[0, out[3]]], A.is_ge, 0.0, 0, 0)])}
+        return add(name, None, None, [out], [a], None, alt=[alt[e] for e in choices])
+
+    def mul(name, out, a, s):
+        return add(name, None, None, [out], [a] + ([s] if isinstance(s, tuple) else []), None,
+                   alt=[act_form(out, a, F.Identity, scale=s), ts_form(out, a, s, None, A.mult, None)])
+
+    def flip(name, out, a):
+        return add(name, "V", ("e", out[3]), [out], [a], lambda: [g.vector.transpose(out[0](), a[0]())])
 
     def mm(name, groups, after=(), first=True, last=True):
         def f():
@@ -321,6 +283,9 @@ def plan(g, core, T, topo, turn_r, turn_l):
         n = sum(max(64, x[3]) * (4 if x[4] == 4 else 1) for gr in groups for (o, l, x) in gr)
         return add(name, "P", ("pe", n), [gr[0][0] for gr in groups], [y for gr in groups for (o, l, x) in gr for y in (l, x)],
                    f, after, ninc=len(groups))
+
+    def lin(jb, terms, lo, hi):
+        return [[(ps(jb, q - lo, min(q + 512, hi) - lo), l, sb(n, q, min(q + 512, hi))) for (l, n) in terms] for q in range(lo, hi, 512)]
 
     nd = [0]
 
@@ -336,30 +301,21 @@ def plan(g, core, T, topo, turn_r, turn_l):
     last_send = []
     sent = [0]
 
-    def send(name, parts):
-        es = [e for e in topo.engines(core, parts[0][0]) if all(e in topo.engines(core, p[0]) for p in parts)]
-        per = len(es) // len(parts)
-        masks = [sum(1 << e for e in es[i * per:(i + 1) * per]) for i in range(len(parts))]
+    def send(name, dst, src, land, sem):
+        es = topo.engines(core, dst)
 
         def f():
-            if len(parts) == 1:
-                dst, src, land, sem = parts[0]
-                rid, pid, _s = topo.addr(dst)
-                g.remote_dma(land[0](), src[0](), T.sem[sem], T.sem.sent, pid, rid, masks[0])
-            else:
-                g.remote_dma_fused([RemoteDMATransfer(dst_ids=[DstId(rid=topo.addr(p[0])[0], pnc=topo.addr(p[0])[1])],
-                                                      dma_engine_mask=masks[i], remote_sem=T.sem[p[3]], src=p[1][0](), dst=p[2][0]())
-                                    for i, p in enumerate(parts)], local_sem=T.sem.sent)
+            rid, pid, _s = topo.addr(dst)
+            g.remote_dma(land[0](), src[0](), T.sem[sem], T.sem.sent, pid, rid, topo.mask(core, dst))
             return []
-        k = add(name, "G", ("rem", 0), [], [p[1] for p in parts], f, last_send[-1:], ninc=0)
+        k = add(name, "G", ("rem", 0), [], [src], f, last_send[-1:], ninc=0)
         last_send.append(k)
-        sent[0] += per * len(parts)
-        for p in parts:
-            add("arr_" + p[3], None, ("arr", p[1][3] * p[1][4] * len(parts)), [p[2]], [], None, [k], sem=(p[3], per))
+        sent[0] += len(es)
+        add("arr_" + sem, None, ("arr", src[3] * src[4]), [land], [], None, [k], sem=(sem, len(es)))
 
     def io(name, out, pat, base, cm, flt):
         kw = {"allow_small_or_imprecise_dtypes": True} if flt else {}
-        return add(name, "G", ("gp", out[3]), [out], [], lambda: [g.iota(out[0](), pat, base, cm, **kw)])
+        return add(name, "G", ("gp", out[3]), [out], [], lambda: [g.iota(out[0](), pat, base, cm, **kw)], last_send[2:])
 
     jn_ = [0]
 
@@ -368,21 +324,22 @@ def plan(g, core, T, topo, turn_r, turn_l):
         return (jn_[0], size)
 
     x0 = T.x0
-    own = XO + H_
+    own = XW + H_
     src_r, src_l = sb("xw0", own + V_ - H_, own + V_), sb("xw0", own, own + H_)
-    if turn_r:
-        dma("Xld_a", "Y", (lambda: T.es0[16:128, :], [("es0", 0, H_)], None, 0, 2), hbm(lambda: x0[0:112, V_ - H_:V_]), 768)
-        dma("Xld_b", "S", (lambda: T.es0[0:16, :], [("es0b", 0, 1)], None, 0, 2), hbm(lambda: x0[112:128, V_ - H_:V_]), 768)
-        src_r = (lambda: T.es0[:, :], [("es0", 0, H_), ("es0b", 0, 1)], None, H_, 2)
     if turn_l:
         dma("Xld_c", "Y", (lambda: T.et0[0:112, :], [("et0", 0, H_)], None, 0, 2), hbm(lambda: x0[16:128, 0:H_]), 768)
         dma("Xld_d", "S", (lambda: T.et0[112:128, :], [("et0b", 0, 1)], None, 0, 2), hbm(lambda: x0[0:16, 0:H_]), 768)
         src_l = (lambda: T.et0[:, :], [("et0", 0, H_), ("et0b", 0, 1)], None, H_, 2)
-    dma("ld_r", "Y", sb("xw0", own + V_ - H_, own + V_), hbm(lambda: x0[:, V_ - H_:V_]), 768)
-    dma("ld_l", "S", sb("xw0", own, own + H_), hbm(lambda: x0[:, 0:H_]), 768)
-    send("sx0", [(right, src_r, sb("xw0", XO, XO + H_), "x0l"), (left, src_l, sb("xw0", own + V_, XO + W_), "x0r")])
-    dma("ld_rt", "Y", b3("li", 0, 2, 1, 0, 64), hbm(lambda: T.rt[:, :]), 512)
-    dma("ld_lf", "S", b3("li", 2, 4, 1, 0, 64), hbm(lambda: T.lf[:, :]), 512)
+    if turn_r:
+        dma("Xld_a", "Y", (lambda: T.es0[16:128, :], [("es0", 0, H_)], None, 0, 2), hbm(lambda: x0[0:112, V_ - H_:V_]), 768)
+        dma("Xld_b", "S", (lambda: T.es0[0:16, :], [("es0b", 0, 1)], None, 0, 2), hbm(lambda: x0[112:128, V_ - H_:V_]), 768)
+        src_r = (lambda: T.es0[:, :], [("es0", 0, H_), ("es0b", 0, 1)], None, H_, 2)
+    dma("ld_l", "Y", sb("xw0", own, own + H_), hbm(lambda: x0[:, 0:H_]), 768)
+    dma("ld_r", "S", sb("xw0", own + V_ - H_, own + V_), hbm(lambda: x0[:, V_ - H_:V_]), 768)
+    send("sx0l", left, src_l, sb("xw0", own + V_, XW + W_), "x0r")
+    send("sx0r", right, src_r, sb("xw0", XW, own), "x0l")
+    dma("ld_rt", "Y", sb("li", 0, 128), hbm(lambda: T.rt[:, :]), 512)
+    dma("ld_lf", "S", sb("li", 128, 256), hbm(lambda: T.lf[:, :]), 512)
     dma("ld_m", "Y", sb("xw0", own + H_, own + V_ - H_), hbm(lambda: x0[:, H_:V_ - H_]), 2560)
     dma("ld_h", "Y", sb("xh0", 0, V_), hbm(lambda: x0[:, :]), 4096)
 
@@ -391,327 +348,322 @@ def plan(g, core, T, topo, turn_r, turn_l):
     io("rr", sb("rr", 0, 16), [[1, 16]], 0, 0, True)
     io("vi", sb("vi", 0, 128), [[16, 128]], H_ - OFF, 0, True)
     ts("pi15", sb("pi", 1, 2), sb("pi", 0, 1), 15, None, A.bitwise_and)
-    cp("pm", sb("pm", 0, 1), sb("pi", 1, 2), default="V")
+    ts("pi16", sb("pi", 2, 3), sb("pi", 0, 1), 16, None, A.bitwise_and)
+    cp("pm", sb("pm", 0, 2), sb("pi", 1, 3), "V")
     pm = sb("pm", 0, 1)
+    ts("odd", sb("pm", 2, 3), sb("pm", 1, 2), 0.0, None, A.not_equal)
+    ts("even", sb("pm", 3, 4), sb("pm", 1, 2), 0.0, None, A.is_equal)
+    ts("c15", sb("pm", 4, 5), pm, -1.0, 15.0, A.mult, A.add)
     ts("oh", sb("oh", 0, 16), sb("rr", 0, 16), pm, None, A.is_equal)
     ts("no", sb("no", 0, 16), sb("rr", 0, 16), pm, None, A.not_equal)
-    ts("c15", sb("c15", 0, 1), pm, -1.0, 15.0, A.mult, A.add)
     ts("dm", sb("dm", 0, 256), sb("dd", 0, 256), 127, None, A.bitwise_and)
     ts("jj", sb("jj", 0, 256), sb("dm", 0, 256), 0.0, None, A.is_equal)
-    for n, c, w in (("jn", -1.0, 128), ("j2", 2.0, 128), ("jm", -2.0, 128), ("ja", 1.125, 256), ("jb", -0.125, 256)):
-        ts(n, sb(n, 0, w), sb("jj", 0, w), c, None, A.mult)
-    if OPTS.get("off_b"):
-        ts("jk", sb("jk", 0, 128), sb("jj", 0, 128), 4096.0, None, A.mult)
-    if OPTS.get("off_c"):
-        ts("jf", sb("jf", 0, 128), sb("jj", 0, 128), 0.5, None, A.mult)
-    ts("zc", sb("zc", 0, 144), sb("dd", 0, 144), sb("c15", 0, 1), None, A.is_equal)
+    wj = 256 if turn_r or turn_l else 128
+    for n, c, w in (("jn", -1.0, 128), ("j2", 2.0, 128), ("jm", -2.0, 128), ("jf", 1.0, 128), ("jk", 4096.0, 128),
+                    ("je", sb("pm", 3, 4), 256), ("jo", sb("pm", 2, 3), 256), ("ja", 1.125, wj), ("jb", -0.125, wj)):
+        mul(n, sb(n, 0, w), sb("jj", 0, w), c)
+    ts("s1", sb("s1", 0, 128), sb("dd", 0, 128), 1.0, sb("no", 15, 16), A.is_equal, A.mult)
+    ts("s15", sb("s15", 0, 128), sb("dd", 0, 128), -15.0, sb("oh", 15, 16), A.is_equal, A.mult)
+    ts("zc", sb("zc", 0, 144), sb("dd", 0, 144), sb("pm", 4, 5), None, A.is_equal)
     ts("z0", sb("z0", 0, 144), sb("dd", 0, 144), 15.0, sb("oh", 0, 1), A.is_equal, A.mult)
     ts("z8", sb("z8", 0, 144), sb("dd", 0, 144), 7.0, sb("oh", 8, 9), A.is_equal, A.mult)
-    tt("zf", sb("zf", 0, 144), sb("z0", 0, 144), sb("z8", 0, 144), A.add)
-    ts("s1", sb("s1", 0, 128), sb("dd", 0, 128), 1.0, sb("no", 15, 16), A.is_equal, A.mult)
+    tt("zf", sb("zf", 0, 144), sb("z8", 0, 144), sb("z0", 0, 144), A.subtract)
     ts("s3", sb("s3", 0, 128), sb("dd", 0, 128), -1.0, sb("no", 0, 1), A.is_equal, A.mult)
     ts("vq", sb("vq", 0, 128), sb("vi", 0, 128), pm, None, A.add)
-    ts("vq2", sb("vq2", 0, 128), sb("vi", 0, 128), pm, float(XO), A.add, A.add)
-    cva = b3("cv", 0, 16, 1, 0, 136)
-    add("cv0", "V", ("e", 1088), [cva], [], lambda: [g.vector.memset(T.cv[:], 0.0)])
-    ts("one", sb("a1w", 0, 128), sb("vi", 0, 128), 0.0, 1.0, A.mult, A.add)
-    add("cv1", "G", ("gp", 128), [cva], [sb("a1w", 0, 128)],
-        lambda: [g.affine_select(T.cv[:, :, 8:136:16], T.a1w[:, 0:128], [[-1, 16], [-16, 8]], A.is_equal, 0.0, 0, 1)])
-    cwa = b3("cw", 0, 8, 1, 0, 128)
-    add("cw0", "V", ("e", 512), [cwa], [], lambda: [g.vector.memset(T.cw[:], 0.0)])
-    add("cw1", "G", ("gp", 128), [cwa], [sb("a1w", 0, 128)],
-        lambda: [g.affine_select(T.cw[:, :, 0:128:8], T.a1w[:, 0:128], [[-1, 8], [-8, 16]], A.is_equal, 0.0, 0, 1)])
-    ts("low", sb("c15", 1, 2), pm, 8.0, None, A.is_lt)
-    ts("high", sb("c15", 2, 3), pm, 8.0, None, A.is_ge)
-    for i, (step, m_) in enumerate(((0.0, 1), (8.0, 1), (-8.0, 2), (0.0, 2))):
-        ts("fm", sb("fm", 128 * i, 128 * i + 128), sb("dd", 0, 128), step, sb("c15", m_, m_ + 1), A.is_equal, A.mult)
-    I_, In, I2, Im = sb("jj", 0, 128), sb("jn", 0, 128), sb("j2", 0, 128), sb("jm", 0, 128)
-    SA = lambda i: b3("cv", i, i + 1, 1, 8, 136)
-    SB = lambda i: b3("cv", i, i + 1, 1, 0, 128)
-    ts("ghi", sb("a1h", 0, 24), sb("vi", 0, 24), float(-H_), None, A.add)
-    ts("glo", sb("a1l", 0, 24), sb("vi", 0, 24), 0.0, pm, A.mult, A.add)
-    jg = job(1)
-    mm("ghp", [[(ps(jg, i, H_, 16), SA(i), sb("a1h", 0, 24)), (ps(jg, i, H_, 16), SB(i), sb("a1l", 0, 24))] for i in range(16)])
-    act("a1g", sb("a1t", 0, H_), ps(jg, 0, H_), F.Copy)
-    act("a2g", sb("a2t", 0, H_), ps(jg, 0, H_), F.Copy)
-    early = [k for k, op in enumerate(ops) if op["eng"] == "V"]
+    ts("v2", sb("v2", 0, 128), sb("vi", 0, 128), pm, float(4096 + XW - XA), A.add, A.add)
+    act("kb", sb("kb", 0, 16), sb("rr", 0, 16), F.Identity, bias=float(V_), scale=0.0)
+    act("one", sb("one", 0, 64), sb("vi", 0, 64), F.Identity, bias=1.0, scale=0.0)
+    for i, (n, c) in enumerate((("xw0", XW + W_), ("xw0", 0), ("xw1", XW + W_), ("xw1", 0))):
+        act("pad", sb(n, c, c + PAD), sb("rr", 0, 16), F.Exp, bias=4.0, scale=0.0, c=("x", 0) if i == 0 else None)
+    I_, In, I2, Im, Ik = (sb(n, 0, 128) for n in ("jj", "jn", "j2", "jm", "jk"))
     Z = lambda n, i: sb(n, 15 - i, 143 - i)
     RS, LS = 112, 16
 
     def ext(z, out, src, lo, more=()):
         return [(out, Z(z, i), sb(src, lo + i, lo + 1024, 16)) for i in range(16)] + list(more)
 
+    def spread(jb, c0, terms, n, turn=0, bias=None):
+        gs = []
+        for b in range(n // 32):
+            for gp in (0, 1):
+                o = ps(jb, c0 + 32 * b + 16 * gp, c0 + 32 * b + 16 * gp + 16)
+                gr = [(o, bias, sb("kb", 0, 16))] if bias else []
+                for cb in (0, 1):
+                    c = (-16 * (cb - gp + turn)) % 128
+                    sel = sb("jo" if (gp + turn) % 2 else "je", c, c + 128)
+                    gr += [(o, sel, sb(name, lo + 2 * b + cb, lo + n, n // 16)) for (name, lo) in terms]
+                gs.append(gr)
+        return gs
+
     def lk(name, side, h, c0=0, c1=64):
         b = BLK[(side, h)]
-        return b3(name, b, b + 1, 1, c0, c1)
+        return sb(name, b + c0, b + c1)
 
-    def tile_out(name, out, parts, turn, col, bias):
-        if turn:
-            j = job(1)
-            c = 0
-            gs = []
-            for p in parts:
-                gs.append([(ps(j, c, c + p[3]), sb("jj", col, col + 128), p)])
-                c += p[3]
-            mm("X" + name, gs)
-        c = 0
-        for p in parts:
-            act(name, sb(out, c, c + p[3]), ps(j, c, c + p[3]) if turn else p, F.Identity, bias=bias)
-            c += p[3]
+    def offs(name, side, lo, hi):
+        return sb(name, BLK[(side, 0)] + lo // 16, BLK[(side, 0)] + hi // 16)
 
-    allb = lambda n: b3(n, 0, 4, 1, 0, 64)
-    ts("st0", allb("st0"), allb("li"), float(-OFF), None, A.add)
-    cp("ul0", allb("ul0"), allb("li"), default="V")
-    tile_out("sb0", "sb0", [lk("st0", "l", 1, 56, 64), lk("st0", "r", 1, 56, 64)], turn_r, RS, float(-V_))
-    send("sb0", [(right, sb("sb0", 0, 16), sb("gb0", 0, 16), "b0")])
+    BIAS = {"r": -H_, "l": PAD}
+    ts("st0", sb("st0", 0, 256), sb("li", 0, 256), float(-OFF), None, A.add)
+    ts("ul0r", sb("ul0", 0, 128), sb("li", 0, 128), float(BIAS["r"]), None, A.add)
+    ts("ul0l", sb("ul0", 128, 256), sb("li", 128, 256), float(BIAS["l"]), None, A.add)
+    parts = [lk("st0", "l", 1, 56, 64), lk("st0", "r", 1, 56, 64)]
+    if turn_r:
+        j = job(1)
+        mm("Xsb0", [[(ps(j, 8 * i, 8 * i + 8), sb("jj", RS, RS + 128), p)] for i, p in enumerate(parts)])
+        act("sb0", sb("sb0", 0, 16), ps(j, 0, 16), F.Identity, bias=float(-V_))
+    else:
+        for i, p in enumerate(parts):
+            act("sb0", sb("sb0", 8 * i, 8 * i + 8), p, F.Identity, bias=float(-V_))
+    send("sb0s", right, sb("sb0", 0, 16), sb("gb0", 0, 16), "b0")
+    end_tb = SCRATCH["tb"][1][1]
+    for c in range(H_, end_tb, V_):
+        w = min(V_, end_tb - c)
+        dma("fill", "G", sb("tb", c, c + w), hbm(lambda w=w: x0[:, 0:w]), 4 * w, last_send[-1:])
+    io("ghi", sb("tb", 0, H_), [[-16, 24], [0, 16]], OFF, 0, True)
+    io("glo", sb("glo", 0, H_), [[0, 24], [1, 16]], 0, 0, True)
+    dma("glo", "Y", row("tb", 8, 0, H_), row("glo", 8, 0, H_), 1500)
+    cp("a2g", sb("a2t", 0, H_), sb("tb", 0, H_), "G")
 
-    ydone = []
+    ydone = {}
     for t in range(2):
         d = 1 if t == 0 else -1
         R = "%d" % t
-        xw, so, sn, uo, un = "xw" + R, "st" + R, "st%d" % (t + 1), "ul" + R, "ul%d" % (t + 1)
-        xh = (lambda lo, hi: sb("xh0", lo, hi)) if t == 0 else (lambda lo, hi: sb("xh1", H_ + lo, H_ + hi))
-        win = sb(xw, XO, XO + W_)
-        j = job(1)
+        xw, xh, so, sn, uo, un, uc, xt = "xw" + R, "xh" + R, "st" + R, "st%d" % (t + 1), "ul" + R, "ul%d" % (t + 1), "uc" + R, "xt" + R
+        win = lambda side, hi: sb(xw, own, XA) if side == "r" else sb(xw, 0, own + hi)
+        Id = I_ if d == 1 else In
 
-        def shift(out, side, h):
-            o = lambda a, b: ps(j, out + a, out + b)
+        def shift(j, c, side, h):
+            o = lambda a, b: ps(j, c + a, c + b)
             if d == 1:
                 edge = lk(so, side, 0, 63, 64) if h == 1 else sb("gb0", 15 if side == "r" else 7, 16 if side == "r" else 8)
-                return [(o(0, 64), sb("s1", 0, 128), lk(so, side, h)), (o(1, 64), SA(15), lk(so, side, h, 0, 63)),
-                        (o(0, 1), SA(15), edge)]
-            edge = lk(so, side, 1, 0, 1) if h == 0 else sb("gr0", 24 if side == "r" else 0, 25 if side == "r" else 1)
+                return [(o(0, 64), sb("s1", 0, 128), lk(so, side, h)), (o(1, 64), sb("s15", 0, 128), lk(so, side, h, 0, 63)),
+                        (o(0, 1), sb("s15", 0, 128), edge)]
+            edge = lk(so, side, 1, 0, 1) if h == 0 else sb("ge", 1 if side == "r" else 0, 2 if side == "r" else 1)
             return [(o(0, 64), sb("s3", 0, 128), lk(so, side, h)), (o(0, 63), Z("z0", 15), lk(so, side, h, 1, 64)),
                     (o(63, 64), Z("z0", 15), edge)]
-        parts = [[("r", 1), ("l", 1)], [("r", 0), ("l", 0)]] if t == 0 else [[("r", 0), ("r", 1), ("l", 0), ("l", 1)]]
-        for pi_, part in enumerate(parts):
-            if pi_ > 0:
-                j = job(1)
-            gs = []
-            for (side, h) in part:
-                b = BLK[(side, h)]
-                gs.append(shift(64 * b, side, h))
-                gs.append(shift(256 + 64 * b, side, h) + [(ps(j, 256 + 64 * b, 320 + 64 * b), In, lk(so, side, h))])
-            mm("shift" + R, gs)
-            runs = [(s_, BLK[(s_, h)], 1) for (s_, h) in part] if t == 0 else [("r", 0, 2), ("l", 2, 2)]
-            for (side, b, w) in runs:
-                p = ps(j, 64 * b, 64 * (b + w))
-                if side == "r":
-                    ts("uc" + R, b3("uc", b, b + w, 1, 0, 64), p, float(OFF + d), float(W_ - 1), A.add, A.min)
-                else:
-                    ts("uc" + R, b3("uc", b, b + w, 1, 0, 64), p, float(OFF + d), 0.0, A.add, A.max)
-            for (side, b, w) in runs:
-                p = ps(j, 64 * b, 64 * (b + w))
-                if side == "r":
-                    act("thr" + R, b3("thr", b, b + w, 1, 0, 64), p, F.Relu, bias=-100.0 * (W_ - 1 - OFF + 0.5 - d), scale=100.0)
-                else:
-                    act("thr" + R, b3("thr", b, b + w, 1, 0, 64), p, F.Relu, bias=100.0 * (-OFF - 0.5 - d), scale=-100.0)
-                if t == 0:
-                    act("dl" + R, b3("dl", b, b + 1, 1, 0, 64), ps(j, 256 + 64 * b, 320 + 64 * b), F.Identity, bias=float(d))
-            if t == 1:
-                act("dl" + R, allb("dl"), ps(j, 256, 512), F.Identity, bias=float(d))
-        for n in (xw, "m2t" + R, "m4t" + R):
-            dma("gh_" + n, "Y", sb(n, 0, H_), sb(xw, XO, XO + H_), H_ * wide[n])
+        for part in ([[("r", 1)], [("r", 0)], [("l", 0), ("l", 1)]] if t == 0 else [[("r", 0), ("r", 1)], [("l", 0), ("l", 1)]]):
+            j = job(1)
+            side, b, w = part[0][0], BLK[part[0]], 64 * len(part)
+            nm = "%s%d%d" % (side, t, part[0][1])
+            mm("shift" + nm, [shift(j, 64 * i, s_, h) for i, (s_, h) in enumerate(part)])
+            if side == "r":
+                ts("uc" + nm, sb(uc, b, b + w), ps(j, 0, w), float(OFF + d + BIAS[side]), float(W_ + BIAS[side]), A.add, A.min)
+            else:
+                ts("uc" + nm, sb(uc, b, b + w), ps(j, 0, w), float(OFF + d + BIAS[side]), float(PAD - 1), A.add, A.max)
+        for n, c in ((xw, XA), ("m2t" + R, 0), ("m4t" + R, 0)):
+            dma("gh_" + n, "Y", sb(n, c, c + H_), sb(xw, XW, own), H_ * wide[n])
 
-        def judge(side, h, jc, c):
-            lo, hi = 1024 * h, 1024 * h + 1024
+        for (side, h) in (("r", 1), ("r", 0), ("l", 0), ("l", 1)):
             nm = "%s%d%d" % (side, t, h)
-            b0, b1, b2, b3_, near = ("de", "dc", "re", "rc", "nr") if side == "r" else ("xg", "xc", "sa", "pr", "nl")
-            part = lambda j1, l, n: [[(ps(j1, q, q + 512), l, sb(n, lo + q, lo + q + 512))] for q in (0, 512)]
-            mode = OPTS["eng"].get("mode" + nm, "V" if side == "r" else "S")
-            if mode != "S":
-                tt("de" + nm, sb(b0, lo, hi), ind(win, lk(uo, side, h)), xh(lo, hi), A.subtract, early)
-                tt("dc" + nm, sb(b1, lo, hi), ind(win, lk("uc", side, h)), xh(lo, hi), A.subtract, early)
-                terms = []
-                for (n, a, b, lv, ls) in (("re", b0, b2, [(I_, b0), (Im, b2)], [(In, b2)]), ("rc", b1, b3_, [(In, b1), (I2, b3_)], [(I_, b3_)])):
-                    if OPTS["eng"].get(n + nm, "V") == "V":
-                        ts(n + nm, sb(b, lo, hi), sb(a, lo, hi), 0.0, None, A.max)
-                        terms += lv
-                    else:
-                        act(n + nm, sb(b, lo, hi), sb(a, lo, hi), F.Abs)
-                        terms += ls
-                j1 = job(2)
-                for i, (l, n) in enumerate(terms):
-                    mm("dif%d" % i + nm, part(j1, l, n), first=i == 0, last=i == len(terms) - 1)
-                if OPTS["eng"].get("nr" + nm, "S") == "S":
-                    act("nr" + nm, sb(near, lo, hi), ps(j1, 0, 1024), F.Sign, bias=-2.0 ** -11, scale=-1.0)
+            e_, a_, p_ = "e" + side, "a" + side, "p" + side
+            for (s, lo, hi) in pieces("xe" + nm, h):
+                cp("xe" + nm + s, sb(e_, lo, hi), ind(win(side, hi), offs(uo, side, lo, hi)))
+            plain = pick("xc" + nm, "VS") == "S"
+            for (s, lo, hi) in pieces("xc" + nm, h):
+                a = ind(win(side, hi), offs(uc, side, lo, hi))
+                if plain:
+                    cp("xc" + nm + s, sb(a_, lo, hi), a)
                 else:
-                    ts("nr" + nm, sb(near, lo, hi), ps(j1, 0, 1024), 0.0, -0.5, A.is_lt, A.add)
-            else:
-                cp("xg" + nm, sb(b0, lo, hi), ind(win, lk(uo, side, h)))
-                cp("xc" + nm, sb(b1, lo, hi), ind(win, lk("uc", side, h)))
-                j1, j2 = job(2), job(2)
-                mm("Ag" + nm, part(j1, In, b0), last=False)
-                mm("Ac" + nm, part(j1, I_, b1), first=False)
-                act("sa" + nm, sb(b2, lo, hi), ps(j1, 0, 1024), F.Sign)
-                mm("Bg" + nm, [[(ps(j2, q, q + 512), Im, xh(lo + q, lo + q + 512)),
-                                (ps(j2, q, q + 512), I_, sb(b0, lo + q, lo + q + 512))] for q in (0, 512)], last=False)
-                mm("Bc" + nm, part(j2, I_, b1), first=False)
-                tt("pr" + nm, sb(b3_, lo, hi), ps(j2, 0, 1024), sb(b2, lo, hi), A.mult)
-                ts("nl" + nm, sb(near, lo, hi), sb(b3_, lo, hi), 0.0, -0.5, A.is_lt, A.add)
-            less = [(ps(jc, c, c + 64), In, lk("thr", side, h))] if OPTS.get("off_c") else []
-            mm("cnt" + nm, [ext("zc", ps(jc, c, c + 64), near, lo, less)])
-
-        for grp in OPTS["groups"][t]:
+                    tt("xc" + nm + s, sb(a_, lo, hi), a, sb(e_, lo, hi), A.subtract)
+            for (s, lo, hi) in pieces("sa" + nm, h) if plain else []:
+                j1 = job((hi - lo) // 512)
+                mm("dif" + nm + s, lin(j1, [(In, e_), (I_, a_)], lo, hi))
+                act("sa" + nm + s, sb(p_, lo, hi), ps(j1, 0, hi - lo), F.Sign)
+            for (s, lo, hi) in pieces("pr" + nm, h):
+                j1 = job((hi - lo) // 512)
+                mm("sue" + nm + s, lin(j1, [(Im, xh), (I_ if plain else I2, e_)], lo, hi), last=False)
+                mm("sum" + nm + s, lin(j1, [(I_, a_)], lo, hi), first=False)
+                tt("pr" + nm + s, sb(p_, lo, hi), ps(j1, 0, hi - lo), sb(p_ if plain else a_, lo, hi), A.mult)
+            for (s, lo, hi) in pieces("nr" + nm, h):
+                p = sb(p_, lo, hi)
+                add("nr" + nm + s, None, None, [p], [p], None,
+                    alt=[ts_form(p, p, 0.0, -0.5, A.is_lt, A.add), act_form(p, p, F.Sign, -2.0 ** -20, -1.0)])
+            lo = 1024 * h
             jc = job(1)
-            b = min(BLK[x] for x in grp)
-            for x in grp:
-                judge(x[0], x[1], jc, 64 * (BLK[x] - b))
-            pr_ = lambda n: b3(n, b, b + len(grp), 1, 0, 64)
-            w = 64 * len(grp)
-            if OPTS.get("off_c"):
-                act("dec" + R, ps(jc, 0, w), ps(jc, 0, w), F.Sign, bias=-0.5)
-                tt("tt" + R, pr_("tt"), ps(jc, 0, w), pr_("dl"), A.mult)
-                mm("newp" + R, [[(ps(jc, 256, 256 + w), I_, pr_(so)), (ps(jc, 256, 256 + w), sb("jf", 0, 128), pr_("dl")),
-                                 (ps(jc, 256, 256 + w), sb("jf", 0, 128), pr_("tt"))]])
-                act("new" + R, pr_(sn), ps(jc, 256, 256 + w), F.Copy)
+            how = pick("new" + nm, "PV")
+            step = [(ps(jc, 64, 128), In, lk(so, side, h))] + ([(ps(jc, 64, 128), Id, sb("one", 0, 64))] if how == "V" else [])
+            mm("cnt" + nm, [shift(jc, 64, side, h) + step, ext("zc", ps(jc, 0, 64), p_, lo)])
+            ts("dec" + nm, lk("msk", side, h), ps(jc, 0, 64), 0.0, None, A.is_gt)
+            tt("tt" + nm, lk("tt", side, h), ps(jc, 64, 128), lk("msk", side, h), A.mult)
+            if how == "P":
+                p = ps(jc, 128, 192)
+                mm("new" + nm, [[(p, I_, lk(so, side, h)), (p, Id, lk("msk", side, h)), (p, sb("jf", 0, 128), lk("tt", side, h))]])
+                cp("sn" + nm, lk(sn, side, h), p)
             else:
-                tt("dec" + R, pr_("dec"), ps(jc, 0, w), pr_("thr"), A.is_gt)
-                tt("tt" + R, pr_("tt"), pr_("dec"), pr_("dl"), A.mult)
-                tt("new" + R, pr_(sn), pr_("tt"), pr_(so), A.add)
-            ts("unew" + R, pr_(un), pr_(sn), float(OFF), None, A.add)
-        tile_out("sr" + R, "sr" + R, [lk(sn, "r", 1, 40, 64)], turn_r, RS, float(-V_))
-        send("sr" + R, [(right, sb("sr" + R, 0, 24), sb("gl" + R, 0, 24), "r" + R)])
-        tile_out("sl" + R, "sl" + R, [lk(sn, "l", 0, 0, 24), lk(sn, "r", 0, 0, 8)][:2 - t], turn_l, LS, float(V_))
-        wl = 32 - 8 * t
-        send("sl" + R, [(left, sb("sl" + R, 0, wl), sb("gr" + R, 0, wl), "l" + R)])
+                p = lk(sn, side, h)
+                tt("sn" + nm, p, lk("tt", side, h), lk(so, side, h), A.add)
+            ts("un" + nm, lk(un, side, h), p, float(OFF + BIAS[side]), None, A.add)
+            b = BLK[(side, h)]
+            c = {("r", 1): 0, ("r", 0): 96, ("l", 0): 160, ("l", 1): 288}[(side, h)]
+            j2 = job(1)
+            gs = spread(j2, 0, [(sn, b)], 64)
+            w = 64
+            if (side, h) == ("r", 1):
+                gs = spread(j2, 64, [(sn, b + 32)], 32, 1 if turn_r else 0, In) + gs
+                w = 96
+            if (side, h) == ("l", 0):
+                for s_ in "lr"[:2 - t]:
+                    gs += spread(j2, w, [(sn, BLK[(s_, 0)])], 32, -1 if turn_l else 0, I_)
+                    w += 32
+            mm("tbp" + nm, gs)
+            flip("tbt" + nm, sb(xt, c, c + w), ps(j2, 0, w))
+            if (side, h) == ("r", 1):
+                send("sr" + R, right, sb(xt, c + 64, c + w), sb("gl" + R, 0, 32), "r" + R)
+                dma("tgl" + R, "Y", row("tb", 0, TA - 128, TA + H_), sb("gl" + R, 0, 32), 1000)
+            if (side, h) == ("l", 0):
+                send("sl" + R, left, sb(xt, c + 64, c + w), sb("gr" + R, 0, w - 64), "l" + R)
+                dma("tgr" + R, "Y", row("tb", 0, TB + V_, TB + V_ + 512), sb("gr" + R, 0, 32), 1000)
+                if t == 0:
+                    cp("ge", sb("ge", 0, 2), sb("gr0", 0, 64, 32))
+            c0 = (TA + H_ if side == "r" else TB) + lo
+            dma("tbd" + nm, "Y", row("tb", 0, c0, c0 + 1024), sb(xt, c, c + 64), 1500)
 
-        def spread(name, tab, k0, srcs):
-            j0 = job(1)
-            w = sb("fold", 128 * (k0 // 64), 128 * (k0 // 64) + 128)
-            mm(name + "q", [[(ps(j0, s, 128, 2), sb("fm", 256 * s + 128 * i, 256 * s + 128 * i + 128), srcs[i]) for i in (0, 1)]
-                            for s in (0, 1)])
-            cp(name + "f", w, ps(j0, 0, 128))
-            for b in (0, 1):
-                j1 = job(1)
-                c = w[1][0][1] + 64 * b
-                mm(name + "p", [[(ps(j1, i, 512, 8), b3("cw", i, i + 1, 1, 0, 128), sb("fold", c, c + 64))] for i in range(8)])
-                cp(name + "ab"[b], sb(tab, 16 * k0 + 512 * b, 16 * k0 + 512 * b + 512), ps(j1, 0, 512))
-
-        def table(tab, k1):
-            return sb(tab, 0, 16 * k1)
-        for (nm, s, src, k0) in (("tgl", SA, "gl", 0), ("tgr", SB, "gr", 152)):
-            j1 = job(1)
-            mm(nm + R + "p", [[(ps(j1, i, H_, 16), s(i), sb(src + R, 0, 24))] for i in range(16)])
-            cp(nm + R, sb("tb", 16 * k0, 16 * k0 + H_), ps(j1, 0, H_))
-        for h in (0, 1):
-            spread("tb%d%d" % (t, h), "tb", 24 + 64 * h, [lk(sn, "r", h), lk(sn, "l", h)])
         col = lambda n, h: sb(n, 64 * h, 64 * h + 64)
+        lst = lambda n, lo, hi: sb(n, lo // 16, hi // 16)
+        ua1, ua2, ua4, xa = "ua1" + R, "ua2" + R, "ua4" + R, "xa" + R
         for h in (0, 1):
-            lo, hi = 1024 * h, 1024 * h + 1024
             nm = "%d%d" % (t, h)
-            cp("back" + nm, sb("ob", lo, hi), ind(table("tb", 88 + 64 * h), lk(un, "l", h)))
+            for (s, lo, hi) in pieces("back" + nm, h):
+                cp("back" + nm + s, sb("ob", lo, hi), ind(sb("tb", TA - PAD, TA + H_ + hi), offs(un, "l", lo, hi)))
+            lo, hi = 1024 * h, 1024 * h + 1024
             j1 = job(1)
-            mm("backx" + nm, [ext("z0", ps(j1, 0, 64), "ob", lo, [(ps(j1, 0, 64), In, col("vq", h))])])
-            if OPTS.get("off_b"):
-                act("b1" + nm, col("w1", h), ps(j1, 0, 64), F.Abs)
-                mm("b2" + nm, [[(ps(j1, 64, 128), I_, lk(sn, "l", h)), (ps(j1, 64, 128), sb("jk", 0, 128), col("w1", h))]])
-                tt("b3" + nm, col("a1w", h), ps(j1, 64, 128), col("vq", h), A.min)
+            how = pick("b1" + nm, "SVW")
+            more = [[(ps(j1, 64, 128), I_, lk(sn, "l", h)), (ps(j1, 64, 128), In, col("vq", h))]] if how == "W" else []
+            mm("backx" + nm, more + [ext("z0", ps(j1, 0, 64), "ob", lo, [(ps(j1, 0, 64), In, col("vq", h))])])
+            if how == "W":
+                ts("b1" + nm, col("w1", h), ps(j1, 0, 64), 0.0, None, A.is_equal)
+                tt("b2" + nm, col("w5", h), ps(j1, 64, 128), col("w1", h), A.mult)
+                tt("b3" + nm, col("a1w", h), col("w5", h), col("vq", h), A.add)
             else:
-                ts("b1" + nm, col("w1", h), ps(j1, 0, 64), 0.0, -4096.0, A.is_equal, A.mult)
-                tt("b2" + nm, col("w2", h), col("w1", h), col("vq", h), A.add)
-                tt("b3" + nm, col("a1w", h), col("w2", h), lk(sn, "l", h), A.max)
-            ts("b4" + nm, col("ua1", h), col("a1w", h), float(OFF), None, A.add)
-            cp("b5" + nm, col("a1h", h), col("a1w", h), default="V")
-            tt("b6" + nm, col("a1l", h), col("a1w", h), col("a1h", h), A.subtract)
-            spread("a1" + nm, "a1t", 24 + 64 * h, [col("a1h", h), col("a1l", h)])
+                if how == "S":
+                    act("b1" + nm, col("w1", h), ps(j1, 0, 64), F.Abs)
+                else:
+                    ts("b1" + nm, col("w1", h), ps(j1, 0, 64), 0.0, None, A.not_equal)
+                mm("b2" + nm, [[(ps(j1, 64, 128), I_, lk(sn, "l", h)), (ps(j1, 64, 128), Ik, col("w1", h))]])
+                tt("b3" + nm, col("a1w", h), ps(j1, 64, 128), col("vq", h), A.min)
+            mul("b5" + nm, col("nh", h), col("a1w", h), -1.0)
+            ts("b4" + nm, col(ua1, h), col("a1w", h), float(OFF), None, A.add)
+            j2 = job(1)
+            mm("a1p" + nm, spread(j2, 0, [("nh", 64 * h)], 64) + spread(j2, 64, [("a1w", 64 * h), ("nh", 64 * h)], 64))
+            flip("a1t" + nm, sb(xa, 128 * h, 128 * h + 128), ps(j2, 0, 128))
+            for i in (0, 1):
+                dma("a1d" + nm, "Y", row("tb", 8 * i, H_ + lo, H_ + hi), sb(xa, 128 * h + 64 * i, 128 * h + 64 * i + 64), 1500)
         for h in (0, 1):
-            lo, hi = 1024 * h, 1024 * h + 1024
             nm = "%d%d" % (t, h)
-            cp("end" + nm, sb("oe", lo, hi), ind(table("tb", 176), lk(un, "r", h)))
+            for (s, lo, hi) in pieces("end" + nm, h):
+                cp("end" + nm + s, sb("oe", lo, hi), ind(sb("tb", TB, TB + XO), offs(un, "r", lo, hi)))
             j1 = job(1)
-            mm("endx" + nm, [ext("z8", ps(j1, 0, 64), "oe", lo, [(ps(j1, 0, 64), In, col("vq", h))])])
-            ts("g1" + nm, col("w3", h), ps(j1, 0, 64), 0.0, 8192.0, A.not_equal, A.mult)
+            mm("endx" + nm, [ext("z0", ps(j1, 0, 64), "oe", 1024 * h, [(ps(j1, 0, 64), In, col("vq", h))])])
+            ts("g1" + nm, col("w3", h), ps(j1, 0, 64), 0.0, None, A.is_equal if pick("d2" + nm, "PV") == "P" else A.not_equal)
         for h in (0, 1):
-            lo, hi = 1024 * h, 1024 * h + 1024
             nm = "%d%d" % (t, h)
-            cp("a2" + nm, sb("a2t", H_ + lo, H_ + hi), ind(table("a1t", 88 + 64 * h), col("ua1", h)))
+            for (s, lo, hi) in pieces("a2" + nm, h):
+                cp("a2" + nm + s, sb("a2t", H_ + lo, H_ + hi), ind(sb("tb", 0, H_ + hi), lst(ua1, lo, hi)))
             j1 = job(1)
-            mm("a2x" + nm, [ext("zf", ps(j1, 0, 64), "a2t", H_ + lo)])
-            ts("c1" + nm, col("ua2", h), ps(j1, 0, 64), float(OFF), None, A.add)
+            mm("a2x" + nm, [ext("zf", ps(j1, 0, 64), "a2t", H_ + 1024 * h)])
+            ts("c1" + nm, col(ua2, h), ps(j1, 0, 64), float(OFF), None, A.add)
             cp("c2" + nm, col("a2w", h), ps(j1, 0, 64))
         for h in (0, 1):
-            lo, hi = 1024 * h, 1024 * h + 1024
             nm = "%d%d" % (t, h)
-            cp("a4" + nm, sb("o4", lo, hi), ind(sb("a2t", 0, H_ + hi), col("ua2", h)))
+            for (s, lo, hi) in pieces("a4" + nm, h):
+                cp("a4" + nm + s, sb("o4", lo, hi), ind(sb("a2t", 0, H_ + hi), lst(ua2, lo, hi)))
             j1 = job(1)
             p = ps(j1, 0, 64)
-            mm("a4x" + nm, [ext("zf", p, "o4", lo)])
-            ts("d1" + nm, col("ua4", h), p, float(OFF), None, A.add)
-            tt("d2" + nm, col("w4", h), p, col("a2w", h), A.subtract)
-            tt("d3" + nm, col("w5", h), col("w4", h), col("w3", h), A.mult)
-            tt("d4" + nm, col("w6", h), col("w5", h), col("vq2", h), A.add)
-            tt("d5" + nm, col("w7", h), p, col("w6", h), A.max)
-            ts("d6" + nm, col("uix", h), col("w7", h), float(OFF), None, A.add)
-        for h in (0, 1):
-            lo, hi = 1024 * h, 1024 * h + 1024
-            cp("xa4%d%d" % (t, h), sb(xw, H_ + lo, H_ + hi), ind(sb(xw, XO, own + hi), col("ua4", h)))
-        for h, (lo, hi) in enumerate(OPTS["cut"][t]):
-            nm = "%d%d" % (t, h)
-            cp("xs" + nm, sb("xs", lo, hi), ind(sb(xw, 0, own + hi), sb("uix", lo // 16, hi // 16)))
-            mv = lambda jj, c, a, b, c0: [(ps(jj, c, c + b - a), sb("ja", c0, c0 + 128), xh(a, b)),
-                                          (ps(jj, c, c + b - a), sb("jb", c0, c0 + 128), sb("xs", a, b))]
-            turn = t == 0 and ((turn_r and hi == V_) or (turn_l and lo == 0))
-            ea, eb = (V_ - H_, V_) if hi == V_ else (0, H_)
-            if turn:
-                j2 = job(1)
-                mm("Xmve" + nm, [mv(j2, 0, ea, eb, RS if hi == V_ else LS)])
-                ts("Xcle" + nm, sb("es1" if hi == V_ else "et1", 0, H_), ps(j2, 0, H_), 0.0, 4.0, A.max, A.min)
-            j1 = job(2 if hi - lo > 512 else 1)
-            mm("mv" + nm, [mv(j1, q, lo + q, min(hi, lo + q + 512), 0) for q in range(0, hi - lo, 512)])
-            if t == 0:
-                ts("cl" + nm, sb("xh1", H_ + lo, H_ + hi), ps(j1, 0, hi - lo), 0.0, 4.0, A.max, A.min)
-                src = sb("xh1", H_ + ea, H_ + eb)
-                if turn:
-                    e1 = sb("es1" if hi == V_ else "et1", 0, H_)
-                    src = (e1[0], e1[1] + src[1]) + e1[2:]
-                if hi == V_:
-                    send("sx1r", [(right, src, sb("xh1", 0, H_), "x1l")])
-                if lo == 0:
-                    send("sx1l", [(left, src, sb("xh1", XO, W_), "x1r")])
-                cp("cast%d" % h, sb("xw1", own + lo, own + hi), sb("xh1", H_ + lo, H_ + hi))
-            else:
-                ts("cl" + nm, sb("x2", lo, hi), ps(j1, 0, hi - lo), 0.0, 4.0, A.max, A.min)
-                dma("xe" + nm, "Y", hbm(lambda lo=lo, hi=hi: T.xe[:, lo:hi]), sb("x2", lo, hi), 4 * (hi - lo))
-        if t == 0:
-            cp("castl", sb("xw1", XO, own), sb("xh1", 0, H_))
-            cp("castr", sb("xw1", own + V_, XO + W_), sb("xh1", XO, W_))
-        m2, m4, c2, c4 = "m2t" + R, "m4t" + R, "m2c" + R, "m4c" + R
-        for h in (0, 1):
-            lo, hi = 1024 * h, 1024 * h + 1024
-            nm = "%d%d" % (t, h)
-            tt("m2" + nm, sb(m2, H_ + lo, H_ + hi), ind(sb(xw, XO, own + hi), col("ua1", h)), xh(lo, hi), A.max)
-            dma("m2c" + nm, "Y", sb(c2, lo, hi), sb(m2, H_ + lo, H_ + hi), 1024 * wide[m2])
-        for h in (0, 1):
-            lo, hi = 1024 * h, 1024 * h + 1024
-            nm = "%d%d" % (t, h)
-            tt("m4" + nm, sb(m4, H_ + lo, H_ + hi), ind(sb(m2, 0, H_ + hi), col("ua2", h)), sb(c2, lo, hi), A.max)
-            k4 = dma("m4c" + nm, "Y", sb(c4, lo, hi), sb(m4, H_ + lo, H_ + hi), 1024 * wide[m2])
-            tt("m8" + nm, sb("mm", lo, hi), ind(sb(m4, 0, H_ + hi), col("ua4", h)), sb(c4, lo, hi), A.max)
-            j1 = job(2)
-            how = OPTS["eng"].get("rn" + nm, "V")
-            if how != "P":
-                tt("dn" + nm, sb("dn", lo, hi), ind(win, lk(un, "r", h)), xh(lo, hi), A.subtract)
+            how = pick("d2" + nm, "PV")
+            mm("a4x" + nm, [ext("zf", p, "o4", 1024 * h, [(p, Ik, sb("one", 0, 64))] if how == "V" else [])])
+            ts("d1" + nm, col(ua4, h), p, float(OFF - (4096 if how == "V" else 0)), None, A.add)
             if how == "P":
-                cp("dn" + nm, sb("dn", lo, hi), ind(win, lk(un, "r", h)))
-                mm("ad" + nm, [[(ps(j1, q, q + 512), In, xh(lo + q, lo + q + 512)), (ps(j1, q, q + 512), I_, sb("dn", lo + q, lo + q + 512))]
-                               for q in (0, 512)], [k4])
-                act("rn" + nm, ps(j1, 0, 1024), ps(j1, 0, 1024), F.Abs)
-                act("exp" + nm, ps(j1, 0, 1024), ps(j1, 0, 1024), F.Exp, scale=-1.0)
-            elif how == "V":
-                ts("rn" + nm, sb("rn", lo, hi), sb("dn", lo, hi), 0.0, None, A.max)
-                mm("ad" + nm, [[(ps(j1, q, q + 512), l, sb(n, lo + q, lo + q + 512)) for (l, n) in ((In, "dn"), (I2, "rn"))]
-                               for q in (0, 512)], [k4])
-                act("exp" + nm, ps(j1, 0, 1024), ps(j1, 0, 1024), F.Exp, scale=-1.0)
+                cp("d2" + nm, col("a4w", h), p)
+                p = ps(j1, 64, 128)
+                mm("d3" + nm, [[(p, I_, col("a4w", h)), (p, In, col("a2w", h)), (p, Ik, col("w3", h))]])
+                act("d4" + nm, col("w4", h), p, F.Sign, bias=-0.5, scale=-1.0)
+                p = ps(j1, 128, 192)
+                mm("d5" + nm, [[(p, I_, col("a4w", h)), (p, Ik, col("w4", h))]])
+                tt("d6" + nm, col("w7", h), p, col("v2", h), A.max)
             else:
-                act("rn" + nm, sb("rn", lo, hi), sb("dn", lo, hi), F.Abs)
-                act("exp" + nm, ps(j1, 0, 1024), sb("rn", lo, hi), F.Exp, scale=-1.0, after=[k4])
-            tt("y" + nm, sb("yy", lo, hi), ps(j1, 0, 1024), sb("mm", lo, hi), A.mult)
-            out = hbm(lambda lo=lo, hi=hi: T.ye[:, lo:hi])
-            if t == 0:
-                ydone.append(dma("ye" + nm, "Y", out, sb("yy", lo, hi), 4096))
-            else:
-                dma("ye" + nm, "G", out, sb("yy", lo, hi), 8192, [ydone[h]], accum=True)
+                j2 = job(1)
+                q = ps(j2, 0, 64)
+                mm("d3" + nm, [[(q, I_, col("a2w", h)), (q, Ik, col("w3", h))]])
+                cp("d2" + nm, col("w6", h), q)
+                tt("d4" + nm, col("w4", h), p, col("w6", h), A.is_lt)
+                tt("d5" + nm, col("w5", h), p, col("w4", h), A.mult)
+                tt("d6" + nm, col("w7", h), col("w5", h), col("v2", h), A.max)
+            ts("d7" + nm, col("uix", h), col("w7", h), float(XA - own + OFF - 4096), None, A.add)
+        for h in (0, 1):
+            nm = "%d%d" % (t, h)
+            for (s, lo, hi) in pieces("xa4" + nm, h):
+                cp("xa4" + nm + s, sb(xw, XA + H_ + lo, XA + H_ + hi), ind(sb(xw, XW, own + hi), lst(ua4, lo, hi)))
+        for h in (0, 1):
+            nm = "%d%d" % (t, h)
+            for (s, lo, hi) in pieces("xs" + nm, h):
+                cp("xs" + nm + s, sb("xs", lo, hi), ind(sb(xw, own, XA + H_ + hi), lst("uix", lo, hi)))
+            for (s, lo, hi) in pieces("cl" + nm, h):
+                turn = t == 0 and ((turn_r and hi == V_) or (turn_l and lo == 0))
+                ea, eb = (V_ - H_, V_) if hi == V_ else (0, H_)
+                if turn:
+                    j2 = job(1)
+                    c0 = RS if hi == V_ else LS
+                    mm("Xmve" + nm, lin(j2, [(sb("ja", c0, c0 + 128), xh), (sb("jb", c0, c0 + 128), "xs")], ea, eb))
+                    ts("Xcle" + nm, sb("es1" if hi == V_ else "et1", 0, H_), ps(j2, 0, H_), 0.0, 4.0, A.max, A.min)
+                j1 = job((hi - lo) // 512)
+                mm("mv" + nm + s, lin(j1, [(sb("ja", 0, 128), xh), (sb("jb", 0, 128), "xs")], lo, hi))
+                if t == 0:
+                    ts("cl" + nm + s, sb("xw1", own + lo, own + hi), ps(j1, 0, hi - lo), 0.0, 4.0, A.max, A.min)
+                    src = sb("es1" if hi == V_ else "et1", 0, H_) if turn else sb("xw1", own + ea, own + eb)
+                    if lo == 0:
+                        send("sx1l", left, src, sb("xw1", own + V_, XW + W_), "x1r")
+                    if hi == V_:
+                        send("sx1r", right, src, sb("xw1", XW, own), "x1l")
+                    cp("cast" + nm + s, sb("xh1", lo, hi), sb("xw1", own + lo, own + hi), pick("cast" + nm, "GSV"))
+                else:
+                    ts("cl" + nm + s, sb("yy0", lo, hi), ps(j1, 0, hi - lo), 0.0, 4.0, A.max, A.min)
+                    dma("xe" + nm + s, "Y", hbm(lambda lo=lo, hi=hi: T.xe[:, lo:hi]), sb("yy0", lo, hi), 4 * (hi - lo))
+        m2, m4, c2, c4, mx, dn, yy = "m2t" + R, "m4t" + R, "m2c" + R, "m4c" + R, "mm" + R, "dn" + R, "yy" + R
+        for h in (0, 1):
+            nm = "%d%d" % (t, h)
+            for (s, lo, hi) in pieces("m2" + nm, h):
+                tt("m2" + nm + s, sb(m2, H_ + lo, H_ + hi), ind(sb(xw, XW, own + hi), lst(ua1, lo, hi)), sb(xh, lo, hi), A.max)
+                dma("m2c" + nm + s, "Y", sb(c2, lo, hi), sb(m2, H_ + lo, H_ + hi), (hi - lo) * wide[m2])
+        for h in (0, 1):
+            nm = "%d%d" % (t, h)
+            for (s, lo, hi) in pieces("m4" + nm, h):
+                tt("m4" + nm + s, sb(m4, H_ + lo, H_ + hi), ind(sb(m2, 0, H_ + hi), lst(ua2, lo, hi)), sb(c2, lo, hi), A.max)
+                dma("m4c" + nm + s, "Y", sb(c4, lo, hi), sb(m4, H_ + lo, H_ + hi), (hi - lo) * wide[m2])
+        for h in (0, 1):
+            nm = "%d%d" % (t, h)
+            for (s, lo, hi) in pieces("m8" + nm, h):
+                tt("m8" + nm + s, sb(mx, lo, hi), ind(sb(m4, 0, H_ + hi), lst(ua4, lo, hi)), sb(c4, lo, hi), A.max)
+            how = pick("rn" + nm, "PVS")
+            for (s, lo, hi) in pieces("dn" + nm, h):
+                a = ind(win("r", hi), offs(un, "r", lo, hi))
+                if how == "P":
+                    act("dn" + nm + s, sb(dn, lo, hi), a, F.Copy)
+                else:
+                    tt("dn" + nm + s, sb(dn, lo, hi), a, sb(xh, lo, hi), A.subtract)
+            lo, hi = 1024 * h, 1024 * h + 1024
+            if how == "V":
+                ts("rn" + nm, sb("rn", lo, hi), sb(dn, lo, hi), 0.0, None, A.max)
+            if how == "S":
+                act("rn" + nm, sb(dn, lo, hi), sb(dn, lo, hi), F.Abs)
+            for (s, lo, hi) in pieces("exp" + nm, h):
+                if how == "S":
+                    p = sb(dn, lo, hi)
+                else:
+                    j1 = job((hi - lo) // 512)
+                    p = ps(j1, 0, hi - lo)
+                    mm("ad" + nm + s, lin(j1, [(In, xh), (I_, dn)] if how == "P" else [(In, dn), (I2, "rn")], lo, hi))
+                    if how == "P":
+                        act("rn" + nm + s, p, p, F.Abs)
+                act("exp" + nm + s, sb(yy, lo, hi), p, F.Exp, scale=-1.0)
+            for (s, lo, hi) in pieces("y" + nm, h):
+                j1 = job((hi - lo) // 512)
+                mm("mc" + nm + s, lin(j1, [(I_, mx)], lo, hi))
+                tt("y" + nm + s, sb(yy, lo, hi), ps(j1, 0, hi - lo), sb(yy, lo, hi), A.mult)
+                out = hbm(lambda lo=lo, hi=hi: T.ye[:, lo:hi])
+                if t == 0:
+                    ydone.setdefault(h, []).append(dma("ye" + nm + s, "Y", out, sb(yy, lo, hi), 4 * (hi - lo)))
+                else:
+                    dma("ye" + nm + s, "G", out, sb(yy, lo, hi), 8 * (hi - lo), ydone[h], accum=True)
 
     return ops, bank, sent, Q
 
@@ -720,35 +672,33 @@ def rank_program(g, core, T, topo):
     rank = T.rank_of(core)
     if rank is None:
         return
-    both = OPTS.get("both", False)
-    ops, bank, sent, Q = plan(g, core, T, topo, both or rank == len(T.cores) - 1, both or rank == 0)
-    names = [op["name"] for op in plan(g, core, T, topo, True, True)[0]]
-    order = issue_order(ops, names, OPTS["order"]) if OPTS["order"] else schedule(ops, MODEL, OPTS)[0]
-    DEBUG[rank] = (ops, order, None)
-    bk, extra = deal_banks(ops, order)
+    kind = (rank == len(T.cores) - 1, rank == 0)
+    ops, bank, sent, Q = plan(g, core, T, topo, kind[0], kind[1])
+    if kind not in ORDERS:
+        ORDERS[kind] = schedule(ops, MODEL)
+    _time, order, bk, extra, use, _beg = ORDERS[kind]
     bank.update(bk)
-    DEBUG[rank] = (ops, order, extra)
-    place = {k: i for i, k in enumerate(order)}
+    where = {k: i for i, k in enumerate(order)}
     count = {}
     token = {}
     clock = {}
     known = {e: {} for e in Q}
     for k in order:
         op = ops[k]
-        e = op["eng"]
+        e, _c, emit = op["alt"][use[k]]
         if e is None:
             token[k] = op["sem"]
             clock[k] = dict([op["sem"]])
             continue
         kn = known[e]
-        need = sorted([p for p in set(op["pre"] + extra.get(k, [])) if p in token], key=lambda p: -place[p])
+        need = sorted([p for p in set(op["pre"] + extra.get(k, [])) if p in token], key=lambda p: -where[p])
         for p in need:
             s, v = token[p]
             if kn.get(s, 0) < v and not (e == "P" and s == "cP"):
                 Q[e].wait_ge(T.sem[s], v)
                 for s2, v2 in clock[p].items():
                     kn[s2] = max(kn.get(s2, 0), v2)
-        ins = op["emit"]()
+        ins = emit()
         if op["sem"]:
             ins[0].then_inc(T.sem[op["sem"][0]], 16)
             token[k] = op["sem"]

@@ -18,10 +18,10 @@ def scratch():
     def add(names, n, dt):
         for name in names.split():
             s[name] = ("sbuf", [128, n], dt)
-    add("xw0", XA + XO, "bfloat16"); add("xh0 m2c0 m4c0 pr pl", V_, "bfloat16"); add("m2t0 m4t0 a2t", XO, "bfloat16")
+    add("xw0", XA + XO, "bfloat16"); add("xh0 m2c0 m4c0 mm0 pr pl", V_, "bfloat16"); add("m2t0 m4t0 a2t", XO, "bfloat16")
     add("es0 et0", H_, "bfloat16"); add("es1 et1 glo", H_, "float32")
     add("xw1", XA + XO, "float32"); add("m2c1 m4c1 yy0 yy1", V_, "float32"); add("m2t1 m4t1", XO, "float32")
-    add("xh1 er ar el al ob oe o4 xs mm0 mm1 dn0 dn1 rn", V_, "float16")
+    add("xh1 er ar el al ob oe o4 xs mm1 dn0 dn1 rn", V_, "float16")
     add("tb", TB + V_ + 512, "float32")
     add("li", 256, "int32"); add("st0 st1 st2 msk", 256, "float16"); add("ul0 ul1 ul2 uc0 uc1", 256, "uint16")
     add("tt", 256, "float32"); add("xt0 xt1", 352, "float32"); add("xa0 xa1", 256, "float32")
@@ -30,7 +30,7 @@ def scratch():
     add("ua10 ua20 ua40 ua11 ua21 ua41 uix", 128, "uint16")
     add("sb0 gb0 kb", 16, "float16")
     add("dd dm", 256, "int32"); add("jj ja jb je jo", 256, "float16"); add("jn j2 jm jk s1 s3 s15", 128, "float16")
-    add("zc z0 z8 zf", 144, "float16")
+    add("zc z0 z8 zf", 144, "float16"); add("fm", 512, "float16"); add("fold", 256, "float16"); add("cw", 1024, "float16")
     add("pi", 4, "int32"); add("pm", 8, "float32"); add("rr oh no", 16, "float32")
     return s
 
@@ -38,19 +38,24 @@ def scratch():
 SCRATCH = scratch()
 NDMA = 90
 SEMAPHORES = ["cV", "cS", "cP", "cG", "sent"] + ["d%d" % k for k in range(NDMA)] + \
-    ["x0l", "x0r", "b0", "r0", "l0", "x1l", "x1r", "r1", "l1"]
+    ["x0l", "x0r", "b0", "r0", "l0", "x1l", "x1r", "r1", "l1"] + [a + b + c for a in "fh" for b in "248" for c in ("00", "01")]
 
-MODEL = dict(cyc=0.83e-3 * 1.15, gat=1.56, fix=0.06, pe=0.42e-3 * 1.15, hop=0.1, dma=1.7, dmab=0.22e-3, iss=0.06,
+MODEL = dict(cyc=0.83e-3 * 1.12, gat=1.56, fix=0.055, efix=0.025, pe=0.42e-3 * 1.12, hop=0.12, dma=1.8, dmab=0.22e-3, iss=0.06,
              giss=1.0, riss=0.8, rlat=2.0, remb=1.2e-3, gfix=0.17, exp1=1.3)
 ST = ('b110:V cast00:V d200:V d201:V newl00:V newl01:V newl10:V newl11:V newr10:V newr11:V rn00:S rn01:V rn11:V xcl01:S xcl11:S',
 'a201 a211 a400 a401 back01 cl01 cl10 cl11 dn00 dn11 end00 end10 exp01 m200 m201 m211 m400 m411 nrl01 nrl11 nrr10 prl00 prl01 prl11 sal01 sal11 xa401 xcl00 xel10 xer00 xer11 xs01 xs10 xs11 y11',
 'xer01 xer00a xcl01 xel01 xel00 sal01 nrl00 back00 back01 end00 end01 a201 a400 xa400 xs00 xa401 xs01 rn00 xer11 xer10 xel10 xel11 nrr11 xcl11 nrr10a exp00 nrr10b sal11 nrl10 dn10 exp01 back10 rn10 back11 end10 end11 a210 a211 a410 a411 exp10 xa410 exp11 xs10a xa411 xs10b xs11',
 'xer00b xcr01 xcr00 prr01 nrr01 prr00 nrr00 xcl00 prl00 prl01 nrl01 dn00 m200 m201 a200 m400 a401 dn01 cl00 cl01 m401 xcr11 xcr10 prr11 prr10 rn01 xcl10 prl10 m800 prl11a prl11b nrl11 dn11 y00 m210 m211 m801 rn11 m410 m411 y01 m810 m811 y10 y11 cl10 cl11', 0.2)
+ST = ('a100:E a101:E b100:W b101:V b110:V b111:V cast00:S d200:V d210:V m400:F m401:F newl01:V newl11:V newr00:V newr01:V newr10:V newr11:V rn10:S xcl01:S xcl11:S',
+'a200 a400 back11 cl00 cl01 cl11 dn01 end01 end10 exp00 exp10 m211 m401 m410 m411 m800 m810 m811 nrl01 nrl10 nrl11 nrr10 prl01 prl10 prl11 prr10 sal01 sal11 xa400 xa401 xa411 xcr00 xcr01 xcr10 xcr11 xel01 xer01 xer10 xer11 xs00 xs01 xs11 y00',
+'xer01a xer00 xcl01 xel01 xel00 sal01b sal01a dn01b dn01a nrl00 dn00 snl00 back00 rn01 b500 rn00 a1e00b a200b end00 a201 a400b d200 end01a a401 xs00 xa401 m401 exp00a m400 xer11b xer10 exp00b xel10 nrr10a nrr10b xcl11 xel11 nrl10 sal11 dn11 snl10 exp01 back10 rn10 back11 exp10 end10 end11 rn11 a211 a410 c210 a411 d210 xa410 exp11 d411 xa411a xs10 xs11a xa411b xs11b',
+'xer01b xcr01 xcr00 prr01 nrr01 prr00 decr01 ttr01 snr01 xcl00 nrr00 prl00 prl01a prl01b nrl01b nrl01a decl01 back01 tbtl01 m200 a1e00a a200a a1e01 m201 a400a end01b xa400a g101 d700 xa400b cl00a cl00b d701 xs01a xs01b cl01 xer11a xcr11 xcr10 prr11 prr10 nrr11 xcl10 prl10 dn10 m800 prl11 nrl11a nrl11b m801 decl11 b410 m210 y00b m211 a210 y01 y00a m410 c211 m411 m810a d211 d710 m810b m811 y10 y11 cl10 cl11a cl11b', 0.1)
 ENG = dict(x.split(":") for x in ST[0].split())
 SPLIT = set(ST[1].split())
 ORDER = {"S": ST[2].split(), "V": ST[3].split()}
 SHIFT = dict(sx1r=20, sx1l=20, ld_rt=9, ld_lf=9, st0=9, Xsb0=9, sb0=9, sb0_2=9)
-OPTS = dict(big=50.0, soon=ST[4], lead={"su": 3, "di": 2})
+OPTS = dict(big=50.0, soon=ST[4], lead={"su": 3, "di": 2}, fold=[])
+LEAD = {}
 ORDERS = {}
 DEBUG = {}
 
@@ -60,7 +65,7 @@ def cost(eng, c, m):
     if k == "g":
         return m["fix"] + n * m["gat"] * m["cyc"], 0.0
     if k == "e":
-        return m["fix"] + max(n, 64) * m["cyc"], 0.0
+        return m["efix"] + max(n, 64) * m["cyc"], 0.0
     if k == "x":
         return m["fix"] + m["exp1"], 0.0
     if k == "pe":
@@ -71,6 +76,8 @@ def cost(eng, c, m):
         return (m["giss"] if eng == "G" else m["iss"]), m["dma"] + n * m["dmab"]
     if k == "rem":
         return m["riss"], 0.0
+    if k == "two":
+        return 0.0, 2 * m["rlat"] + m["riss"] + 4 * n * m["dmab"] + 2.0
     return 0.0, m["rlat"] + n * m["remb"]
 
 
@@ -98,9 +105,10 @@ def schedule(ops, m):
             job = ops[ks[i]]["job"]
             first = jobs[job[0]][0] if job else None
             if job and ops[first]["eng"] == "P" and ks[i] == jobs[job[0]][[ops[x]["eng"] == "P" for x in jobs[job[0]]].index(False)]:
-                a = ks[max(0, i - OPTS["lead"].get(ops[first]["name"][:2], 1))]
-                nxt.setdefault(a, []).append(first)
-                wait[first] += 1
+                lead = LEAD.get(ops[first]["name"][:6], OPTS["lead"].get(ops[first]["name"][:2], 1))
+                if lead <= i:
+                    nxt.setdefault(ks[i - lead], []).append(first)
+                    wait[first] += 1
     prio = [p + SHIFT.get(op["name"], 0.0) - (OPTS["big"] if k in on else 0.0) for k, (p, op) in enumerate(zip(path, ops))]
     left = {j: len(v) for j, v in jobs.items()}
     holder, freed = [None] * 8, [0.0] * 8
@@ -111,11 +119,13 @@ def schedule(ops, m):
     ready = [k for k in range(n) if not wait[k]]
 
     def banks(size):
-        fits = [b for b in range(0, 8, size) if all(h is None or not left[h] for h in holder[b:b + size])]
-        lone = lambda b: size == 1 and (holder[b ^ 1] is None or not left[holder[b ^ 1]])
-        return min(fits, key=lambda b: (lone(b), max(freed[b:b + size]), -b)) if fits else None
+        if size == 1:
+            fits = [(not held[b ^ 1], freed[b], -b) for b in range(8) if not held[b]]
+        else:
+            fits = [(False, max(freed[b], freed[b + 1]), -b) for b in (0, 2, 4, 6) if not held[b] and not held[b + 1]]
+        return min(fits)[1:] if fits else None
+    spare, held = {}, [False] * 8
     while ready:
-        spare = {}
         cand = []
         for k in ready:
             t, job = rdy[k], jobof[k]
@@ -125,7 +135,7 @@ def schedule(ops, m):
                 b = spare[job[1]]
                 if b is None:
                     continue
-                t = max(t, max(freed[b:b + job[1]]) + m["hop"])
+                t = max(t, b[0] + m["hop"])
             for a, e in can[k]:
                 cand.append((t if t > free[e] else free[e], -prio[k], a, k, e))
         if not cand:
@@ -139,12 +149,15 @@ def schedule(ops, m):
         if job:
             j, size = job
             if j not in bank:
-                b = bank[j] = spare[size]
+                b = bank[j] = -spare[size][1]
                 extra[k] = [p for h in holder[b:b + size] if h is not None for p in jobs[h]]
                 holder[b:b + size] = [j] * size
             left[j] -= 1
             for b in range(bank[j], bank[j] + size):
                 freed[b] = max(freed[b], fin[k])
+                if held[b] != (left[j] > 0):
+                    held[b] = left[j] > 0
+                    spare = {}
         order.append(k)
         ready.remove(k)
         for s in ops[k]["suc"] + nxt.get(k, []):
@@ -187,6 +200,9 @@ def plan(g, core, T, topo, turn_r, turn_l):
 
     def ind(win, off):
         return (lambda: win[0]().indirect(off[0]()), win[1] + off[1], None, 16 * off[3], 0)
+
+    def both(a, b):
+        return (a[0], a[1] + b[1]) + a[2:]
 
     def hbm(f):
         return (f, [], None, 0, 0)
@@ -300,6 +316,7 @@ def plan(g, core, T, topo, turn_r, turn_l):
 
     last_send = []
     sent = [0]
+    back = []
 
     def send(name, dst, src, land, sem):
         es = topo.engines(core, dst)
@@ -312,6 +329,20 @@ def plan(g, core, T, topo, turn_r, turn_l):
         last_send.append(k)
         sent[0] += len(es)
         add("arr_" + sem, None, ("arr", src[3] * src[4]), [land], [], None, [k], sem=(sem, len(es)))
+
+    def fold(nm, srcs, there, land):
+        aid = helper(core, T, topo)
+        es = topo.engines(core, aid)
+
+        def f():
+            rid, pid, _s = topo.addr(aid)
+            g.remote_dma_fused([RemoteDMATransfer(dst_ids=[DstId(rid=rid, pnc=pid)], dma_engine_mask=topo.mask(core, aid), remote_sem=T.sem["f" + nm],
+                                                  srcs=[s[0]() for s in srcs], dsts=[there[0]()], alu_op=2)], local_sem=T.sem.sent)
+            return []
+        k = add("fold" + nm, "G", ("rem", 0), [], srcs, f, ninc=0)
+        sent[0] += len(es)
+        add("arr_f" + nm, None, ("two", there[3] * there[4]), land, srcs, None, [k], sem=("h" + nm, len(es)))
+        back.append(("fold" + nm, "f" + nm, there, land, "h" + nm))
 
     def io(name, out, pat, base, cm, flt):
         kw = {"allow_small_or_imprecise_dtypes": True} if flt else {}
@@ -329,11 +360,11 @@ def plan(g, core, T, topo, turn_r, turn_l):
     if turn_l:
         dma("Xld_c", "Y", (lambda: T.et0[0:112, :], [("et0", 0, H_)], None, 0, 2), hbm(lambda: x0[16:128, 0:H_]), 768)
         dma("Xld_d", "S", (lambda: T.et0[112:128, :], [("et0b", 0, 1)], None, 0, 2), hbm(lambda: x0[0:16, 0:H_]), 768)
-        src_l = (lambda: T.et0[:, :], [("et0", 0, H_), ("et0b", 0, 1)], None, H_, 2)
+        src_l = both((lambda: T.et0[:, :], [("et0", 0, H_), ("et0b", 0, 1)], None, H_, 2), src_l)
     if turn_r:
         dma("Xld_a", "Y", (lambda: T.es0[16:128, :], [("es0", 0, H_)], None, 0, 2), hbm(lambda: x0[0:112, V_ - H_:V_]), 768)
         dma("Xld_b", "S", (lambda: T.es0[0:16, :], [("es0b", 0, 1)], None, 0, 2), hbm(lambda: x0[112:128, V_ - H_:V_]), 768)
-        src_r = (lambda: T.es0[:, :], [("es0", 0, H_), ("es0b", 0, 1)], None, H_, 2)
+        src_r = both((lambda: T.es0[:, :], [("es0", 0, H_), ("es0b", 0, 1)], None, H_, 2), src_r)
     dma("ld_l", "Y", sb("xw0", own, own + H_), hbm(lambda: x0[:, 0:H_]), 768)
     dma("ld_r", "S", sb("xw0", own + V_ - H_, own + V_), hbm(lambda: x0[:, V_ - H_:V_]), 768)
     send("sx0l", left, src_l, sb("xw0", own + V_, XW + W_), "x0r")
@@ -372,7 +403,15 @@ def plan(g, core, T, topo, turn_r, turn_l):
     ts("vq", sb("vq", 0, 128), sb("vi", 0, 128), pm, None, A.add)
     ts("v2", sb("v2", 0, 128), sb("vi", 0, 128), pm, float(4096 + XW - XA), A.add, A.add)
     act("kb", sb("kb", 0, 16), sb("rr", 0, 16), F.Identity, bias=float(V_), scale=0.0)
-    act("one", sb("one", 0, 64), sb("vi", 0, 64), F.Identity, bias=1.0, scale=0.0)
+    act("one", sb("one", 0, 128), sb("vi", 0, 128), F.Identity, bias=1.0, scale=0.0)
+    if any(pick("a1%d%d" % (t, h), "DE") == "E" for t in (0, 1) for h in (0, 1)):
+        ts("low", sb("pm", 5, 6), pm, 8.0, None, A.is_lt)
+        ts("high", sb("pm", 6, 7), pm, 8.0, None, A.is_ge)
+        for i, (step, m_) in enumerate(((0.0, 5), (8.0, 5), (-8.0, 6), (0.0, 6))):
+            ts("fm", sb("fm", 128 * i, 128 * i + 128), sb("dd", 0, 128), step, sb("pm", m_, m_ + 1), A.is_equal, A.mult)
+        add("cw0", "V", ("e", 512), [sb("cw", 0, 1024)], [], lambda: [g.vector.memset(T.cw[:, :], 0.0)])
+        add("cw1", "G", ("gp", 128), [sb("cw", 0, 1024)], [sb("one", 0, 128)],
+            lambda: [g.affine_select(T.cw[:, 0:1024:8], T.one[:, 0:128], [[-1, 8], [-8, 16]], A.is_equal, 0.0, 0, 1)])
     for i, (n, c) in enumerate((("xw0", XW + W_), ("xw0", 0), ("xw1", XW + W_), ("xw1", 0))):
         act("pad", sb(n, c, c + PAD), sb("rr", 0, 16), F.Exp, bias=4.0, scale=0.0, c=("x", 0) if i == 0 else None)
     I_, In, I2, Im, Ik = (sb(n, 0, 128) for n in ("jj", "jn", "j2", "jm", "jk"))
@@ -410,10 +449,8 @@ def plan(g, core, T, topo, turn_r, turn_l):
     if turn_r:
         j = job(1)
         mm("Xsb0", [[(ps(j, 8 * i, 8 * i + 8), sb("jj", RS, RS + 128), p)] for i, p in enumerate(parts)])
-        act("sb0", sb("sb0", 0, 16), ps(j, 0, 16), F.Identity, bias=float(-V_))
-    else:
-        for i, p in enumerate(parts):
-            act("sb0", sb("sb0", 8 * i, 8 * i + 8), p, F.Identity, bias=float(-V_))
+    for i, p in enumerate(parts):
+        act("sb0", sb("sb0", 8 * i, 8 * i + 8), ps(j, 8 * i, 8 * i + 8) if turn_r else p, F.Identity, bias=float(-V_))
     send("sb0s", right, sb("sb0", 0, 16), sb("gb0", 0, 16), "b0")
     end_tb = SCRATCH["tb"][1][1]
     for c in range(H_, end_tb, V_):
@@ -471,7 +508,8 @@ def plan(g, core, T, topo, turn_r, turn_l):
                 act("sa" + nm + s, sb(p_, lo, hi), ps(j1, 0, hi - lo), F.Sign)
             for (s, lo, hi) in pieces("pr" + nm, h):
                 j1 = job((hi - lo) // 512)
-                mm("sue" + nm + s, lin(j1, [(Im, xh), (I_ if plain else I2, e_)], lo, hi), last=False)
+                mm("sux" + nm + s, lin(j1, [(Im, xh)], lo, hi), last=False)
+                mm("sue" + nm + s, lin(j1, [(I_ if plain else I2, e_)], lo, hi), first=False, last=False)
                 mm("sum" + nm + s, lin(j1, [(I_, a_)], lo, hi), first=False)
                 tt("pr" + nm + s, sb(p_, lo, hi), ps(j1, 0, hi - lo), sb(p_ if plain else a_, lo, hi), A.mult)
             for (s, lo, hi) in pieces("nr" + nm, h):
@@ -544,6 +582,17 @@ def plan(g, core, T, topo, turn_r, turn_l):
             mul("b5" + nm, col("nh", h), col("a1w", h), -1.0)
             ts("b4" + nm, col(ua1, h), col("a1w", h), float(OFF), None, A.add)
             j2 = job(1)
+            if pick("a1" + nm, "DE") == "E":
+                fm = lambda i: sb("fm", 128 * i, 128 * i + 128)
+                mm("a1q" + nm, [[(ps(j2, s, 128, 2), fm(2 * s), col("nh", h)), (ps(j2, s, 128, 2), fm(2 * s + 1), col("nh", h)),
+                                 (ps(j2, s, 128, 2), fm(2 * s + 1), col("a1w", h))] for s in (0, 1)])
+                cp("a1f" + nm, sb("fold", 128 * h, 128 * h + 128), ps(j2, 0, 128))
+                for b in (0, 1):
+                    j3 = job(1)
+                    c = 128 * h + 64 * b
+                    mm("a1r" + nm, [[(ps(j3, i, 512, 8), sb("cw", 128 * i, 128 * i + 128), sb("fold", c, c + 64))] for i in range(8)])
+                    cp("a1e" + nm + "ab"[b], sb("tb", H_ + lo + 512 * b, H_ + lo + 512 * b + 512), ps(j3, 0, 512))
+                continue
             mm("a1p" + nm, spread(j2, 0, [("nh", 64 * h)], 64) + spread(j2, 64, [("a1w", 64 * h), ("nh", 64 * h)], 64))
             flip("a1t" + nm, sb(xa, 128 * h, 128 * h + 128), ps(j2, 0, 128))
             for i in (0, 1):
@@ -609,7 +658,9 @@ def plan(g, core, T, topo, turn_r, turn_l):
                 mm("mv" + nm + s, lin(j1, [(sb("ja", 0, 128), xh), (sb("jb", 0, 128), "xs")], lo, hi))
                 if t == 0:
                     ts("cl" + nm + s, sb("xw1", own + lo, own + hi), ps(j1, 0, hi - lo), 0.0, 4.0, A.max, A.min)
-                    src = sb("es1" if hi == V_ else "et1", 0, H_) if turn else sb("xw1", own + ea, own + eb)
+                    src = sb("xw1", own + ea, own + eb)
+                    if turn:
+                        src = both(sb("es1" if hi == V_ else "et1", 0, H_), src)
                     if lo == 0:
                         send("sx1l", left, src, sb("xw1", own + V_, XW + W_), "x1r")
                     if hi == V_:
@@ -621,18 +672,43 @@ def plan(g, core, T, topo, turn_r, turn_l):
         m2, m4, c2, c4, mx, dn, yy = "m2t" + R, "m4t" + R, "m2c" + R, "m4c" + R, "mm" + R, "dn" + R, "yy" + R
         for h in (0, 1):
             nm = "%d%d" % (t, h)
+            if t in OPTS["fold"]:
+                lo, hi = 1024 * h, 1024 * h + 1024
+                fold("2" + nm, [sb(xw, XA + H_ + lo, XA + H_ + hi), sb(xw, own + lo, own + hi)], sb(c2, lo, hi),
+                     [sb(m2, H_ + lo, H_ + hi), sb(c2, lo, hi)])
+                continue
             for (s, lo, hi) in pieces("m2" + nm, h):
                 tt("m2" + nm + s, sb(m2, H_ + lo, H_ + hi), ind(sb(xw, XW, own + hi), lst(ua1, lo, hi)), sb(xh, lo, hi), A.max)
                 dma("m2c" + nm + s, "Y", sb(c2, lo, hi), sb(m2, H_ + lo, H_ + hi), (hi - lo) * wide[m2])
+        if t in OPTS["fold"]:
+            ua4 = ua1
         for h in (0, 1):
             nm = "%d%d" % (t, h)
+            plain = t == 0 and pick("m4" + nm, "VF") == "F"
             for (s, lo, hi) in pieces("m4" + nm, h):
-                tt("m4" + nm + s, sb(m4, H_ + lo, H_ + hi), ind(sb(m2, 0, H_ + hi), lst(ua2, lo, hi)), sb(c2, lo, hi), A.max)
-                dma("m4c" + nm + s, "Y", sb(c4, lo, hi), sb(m4, H_ + lo, H_ + hi), (hi - lo) * wide[m2])
+                a = ind(sb(m2, 0, H_ + hi), lst(ua2, lo, hi))
+                if plain:
+                    cp("m4" + nm + s, sb(mx, lo, hi), a)
+                else:
+                    tt("m4" + nm + s, sb(m4, H_ + lo, H_ + hi), a, sb(c2, lo, hi), A.max)
+                    dma("m4c" + nm + s, "Y", sb(c4, lo, hi), sb(m4, H_ + lo, H_ + hi), (hi - lo) * wide[m2])
+            if plain:
+                lo, hi = 1024 * h, 1024 * h + 1024
+                fold("4" + nm, [sb(mx, lo, hi), sb(c2, lo, hi)], sb(c4, lo, hi), [sb(m4, H_ + lo, H_ + hi), sb(c4, lo, hi)])
         for h in (0, 1):
             nm = "%d%d" % (t, h)
+            plain = t == 0 and pick("m8" + nm, "VF") == "F"
+            mx = "mm" + R
             for (s, lo, hi) in pieces("m8" + nm, h):
-                tt("m8" + nm + s, sb(mx, lo, hi), ind(sb(m4, 0, H_ + hi), lst(ua4, lo, hi)), sb(c4, lo, hi), A.max)
+                a = ind(sb(m4, 0, H_ + hi), lst(ua4, lo, hi))
+                if plain:
+                    cp("m8" + nm + s, sb(mx, lo, hi), a)
+                else:
+                    tt("m8" + nm + s, sb(mx, lo, hi), a, sb(c4, lo, hi), A.max)
+            if plain:
+                lo, hi = 1024 * h, 1024 * h + 1024
+                fold("8" + nm, [sb(mx, lo, hi), sb(c4, lo, hi)], sb(mx, lo, hi), [sb(c2, lo, hi)])
+                mx = c2
             how = pick("rn" + nm, "PVS")
             for (s, lo, hi) in pieces("dn" + nm, h):
                 a = ind(win("r", hi), offs(un, "r", lo, hi))
@@ -665,19 +741,64 @@ def plan(g, core, T, topo, turn_r, turn_l):
                 else:
                     dma("ye" + nm + s, "G", out, sb(yy, lo, hi), 8 * (hi - lo), ydone[h], accum=True)
 
-    return ops, bank, sent, Q
+    return ops, bank, sent, Q, back
+
+
+def timetable(g, core, T, topo):
+    if not ORDERS:
+        ops = plan(g, core, T, topo, True, True)[0]
+        _time, order, bank, _extra, use, _beg = schedule(ops, MODEL)
+        ORDERS.update({ops[k]["name"]: (use[k], bank[ops[k]["job"][0]] if ops[k]["job"] else None) for k in order})
+    return ORDERS
+
+
+def follow(ops, bank, table):
+    where = {op["name"]: k for k, op in enumerate(ops)}
+    order = [where[x] for x in table if x in where]
+    place = {k: i for i, k in enumerate(order)}
+    if len(order) < len(ops) or any(place[p] > place[k] for k in order for p in ops[k]["pre"]):
+        raise ValueError("the table doesn't fit this rank's calls")
+    jobs, holder, extra = {}, [[]] * 8, {}
+    for k in order:
+        if ops[k]["job"]:
+            jobs.setdefault(ops[k]["job"][0], []).append(k)
+    for k in order:
+        if ops[k]["job"] and ops[k]["job"][0] not in bank:
+            j, size = ops[k]["job"]
+            b = bank[j] = table[ops[k]["name"]][1]
+            extra[k] = [p for held in holder[b:b + size] for p in held]
+            holder[b:b + size] = [jobs[j]] * size
+    return order, [table[op["name"]][0] for op in ops], extra
+
+
+def helper(core, T, topo):
+    return [c for c in topo.cores_of(core) if T.rank_of(c) is None and topo.die(c) == topo.die(core)][0]
+
+
+def hand_back(g, core, boss, T, topo):
+    es = topo.engines(core, boss)
+    rid, pid, _s = topo.addr(boss)
+    back = plan(g, boss, T, topo, False, False)[4]
+    names = list(timetable(g, boss, T, topo))
+    for (_name, came, src, land, sem) in sorted(back, key=lambda b: names.index(b[0])):
+        g.wait_ge(T.sem[came], len(topo.engines(boss, core)))
+        per = len(es) // len(land)
+        g.remote_dma_fused([RemoteDMATransfer(dst_ids=[DstId(rid=rid, pnc=pid)], dma_engine_mask=sum(1 << e for e in es[i * per:(i + 1) * per]),
+                                              remote_sem=T.sem[sem], src=src[0](), dst=x[0]()) for i, x in enumerate(land)], local_sem=T.sem.sent)
+    if back:
+        g.wait_ge(T.sem.sent, len(es) * len(back))
 
 
 def rank_program(g, core, T, topo):
     rank = T.rank_of(core)
     if rank is None:
+        for boss in T.cores:
+            if helper(boss, T, topo) == core:
+                hand_back(g, core, boss, T, topo)
         return
     kind = (rank == len(T.cores) - 1, rank == 0)
-    ops, bank, sent, Q = plan(g, core, T, topo, kind[0], kind[1])
-    if kind not in ORDERS:
-        ORDERS[kind] = schedule(ops, MODEL)
-    _time, order, bk, extra, use, _beg = ORDERS[kind]
-    bank.update(bk)
+    ops, bank, sent, Q, _back = plan(g, core, T, topo, kind[0], kind[1])
+    order, use, extra = follow(ops, bank, timetable(g, core, T, topo))
     where = {k: i for i, k in enumerate(order)}
     count = {}
     token = {}

from concourse.bass import DstId, RemoteDMATransfer
from concourse.mybir import AluOpType as A, ActivationFunctionType as F

V_, H_, W_ = 2048, 384, 2816
PAD = 16
XO = V_ + H_
XW = PAD
XA = XW + W_ + PAD
OFF = 1408
BLK = {("r", 0): 0, ("r", 1): 64, ("l", 0): 128, ("l", 1): 192}
TA = XO + 128
TB = TA + XO


def scratch():
    s = {"ps": ("psum", [128, 4096], "float32")}

    def add(names, n, dt):
        for name in names.split():
            s[name] = ("sbuf", [128, n], dt)
    add("xw0", XA + XO, "bfloat16"); add("xh0 m2c0 m4c0 mm0 pr pl", V_, "bfloat16"); add("m2t0 m4t0 a2t", XO, "bfloat16")
    add("es0 et0", H_, "bfloat16"); add("es1 et1 glo", H_, "float32")
    add("xw1", XA + XO, "float32"); add("m2c1 m4c1 yy0 yy1", V_, "float32"); add("m2t1 m4t1", XO, "float32")
    add("xh1 er ar el al ob oe o4 xs mm1 dn0 dn1 rn", V_, "float16")
    add("tb", TB + V_ + 512, "float32")
    add("li", 256, "int32"); add("st0 st1 st2 msk", 256, "float16"); add("ul0 ul1 ul2 uc0 uc1", 256, "uint16")
    add("tt", 256, "float32"); add("xt0 xt1", 352, "float32"); add("xa0 xa1", 256, "float32")
    add("gl0 gl1 gr1", 32, "float32"); add("gr0", 64, "float32"); add("ge", 2, "float16")
    add("w1 nh", 128, "bfloat16"); add("vq a1w a2w a4w w3 w4 one", 128, "float16"); add("vi v2 w5 w6 w7 jf", 128, "float32")
    add("ua10 ua20 ua40 ua11 ua21 ua41 uix", 128, "uint16")
    add("sb0 gb0 kb", 16, "float16")
    add("dd dm", 256, "int32"); add("jj ja jb je jo", 256, "float16"); add("jn j2 jm jk s1 s3 s15", 128, "float16")
    add("zc z0 z8 zf", 144, "float16"); add("fm", 512, "float16"); add("fold", 256, "float16"); add("cw", 1024, "float16")
    add("pi", 4, "int32"); add("pm", 8, "float32"); add("rr oh no", 16, "float32")
    return s


SCRATCH = scratch()
NDMA = 90
SEMAPHORES = ["cV", "cS", "cP", "cG", "sent"] + ["d%d" % k for k in range(NDMA)] + \
    ["x0l", "x0r", "b0", "r0", "l0", "x1l", "x1r", "r1", "l1"] + [a + b + c for a in "fh" for b in "248" for c in ("00", "01")]

MODEL = dict(cyc=0.83e-3 * 1.12, gat=1.56, fix=0.055, efix=0.025, pe=0.42e-3 * 1.12, hop=0.12, dma=1.8, dmab=0.22e-3, iss=0.06,
             giss=1.0, riss=0.8, rlat=2.0, remb=1.2e-3, gfix=0.17, exp1=1.3)
ST = ('b110:V cast00:V d200:V d201:V newl00:V newl01:V newl10:V newl11:V newr10:V newr11:V rn00:S rn01:V rn11:V xcl01:S xcl11:S',
'a201 a211 a400 a401 back01 cl01 cl10 cl11 dn00 dn11 end00 end10 exp01 m200 m201 m211 m400 m411 nrl01 nrl11 nrr10 prl00 prl01 prl11 sal01 sal11 xa401 xcl00 xel10 xer00 xer11 xs01 xs10 xs11 y11',
'xer01 xer00a xcl01 xel01 xel00 sal01 nrl00 back00 back01 end00 end01 a201 a400 xa400 xs00 xa401 xs01 rn00 xer11 xer10 xel10 xel11 nrr11 xcl11 nrr10a exp00 nrr10b sal11 nrl10 dn10 exp01 back10 rn10 back11 end10 end11 a210 a211 a410 a411 exp10 xa410 exp11 xs10a xa411 xs10b xs11',
'xer00b xcr01 xcr00 prr01 nrr01 prr00 nrr00 xcl00 prl00 prl01 nrl01 dn00 m200 m201 a200 m400 a401 dn01 cl00 cl01 m401 xcr11 xcr10 prr11 prr10 rn01 xcl10 prl10 m800 prl11a prl11b nrl11 dn11 y00 m210 m211 m801 rn11 m410 m411 y01 m810 m811 y10 y11 cl10 cl11', 0.2)
ST = ('a100:E a101:E b100:W b101:V b110:V b111:V cast00:S d200:V d210:V m400:F m401:F newl01:V newl11:V newr00:V newr01:V newr10:V newr11:V rn10:S xcl01:S xcl11:S',
'a200 a400 back11 cl00 cl01 cl11 dn01 end01 end10 exp00 exp10 m211 m401 m410 m411 m800 m810 m811 nrl01 nrl10 nrl11 nrr10 prl01 prl10 prl11 prr10 sal01 sal11 xa400 xa401 xa411 xcr00 xcr01 xcr10 xcr11 xel01 xer01 xer10 xer11 xs00 xs01 xs11 y00',
'xer01a xer00 xcl01 xel01 xel00 sal01b sal01a dn01b dn01a nrl00 dn00 snl00 back00 rn01 b500 rn00 a1e00b a200b end00 a201 a400b d200 end01a a401 xs00 xa401 m401 exp00a m400 xer11b xer10 exp00b xel10 nrr10a nrr10b xcl11 xel11 nrl10 sal11 dn11 snl10 exp01 back10 rn10 back11 exp10 end10 end11 rn11 a211 a410 c210 a411 d210 xa410 exp11 d411 xa411a xs10 xs11a xa411b xs11b',
'xer01b xcr01 xcr00 prr01 nrr01 prr00 decr01 ttr01 snr01 xcl00 nrr00 prl00 prl01a prl01b nrl01b nrl01a decl01 back01 tbtl01 m200 a1e00a a200a a1e01 m201 a400a end01b xa400a g101 d700 xa400b cl00a cl00b d701 xs01a xs01b cl01 xer11a xcr11 xcr10 prr11 prr10 nrr11 xcl10 prl10 dn10 m800 prl11 nrl11a nrl11b m801 decl11 b410 m210 y00b m211 a210 y01 y00a m410 c211 m411 m810a d211 d710 m810b m811 y10 y11 cl10 cl11a cl11b', 0.1)
ENG = dict(x.split(":") for x in ST[0].split())
SPLIT = set(ST[1].split())
ORDER = {"S": ST[2].split(), "V": ST[3].split()}
SHIFT = dict(sx1r=20, sx1l=20, ld_rt=9, ld_lf=9, st0=9, Xsb0=9, sb0=9, sb0_2=9)
OPTS = dict(big=50.0, soon=ST[4], lead={"su": 3, "di": 2}, fold=[])
LEAD = {}
ORDERS = {}
DEBUG = {}


def cost(eng, c, m):
    k, n = c
    if k == "g":
        return m["fix"] + n * m["gat"] * m["cyc"], 0.0
    if k == "e":
        return m["efix"] + max(n, 64) * m["cyc"], 0.0
    if k == "x":
        return m["fix"] + m["exp1"], 0.0
    if k == "pe":
        return n * m["pe"] + 0.05, 0.0
    if k == "gp":
        return m["gfix"] + 2 * n * m["cyc"], 0.0
    if k == "dma":
        return (m["giss"] if eng == "G" else m["iss"]), m["dma"] + n * m["dmab"]
    if k == "rem":
        return m["riss"], 0.0
    if k == "two":
        return 0.0, 2 * m["rlat"] + m["riss"] + 4 * n * m["dmab"] + 2.0
    return 0.0, m["rlat"] + n * m["remb"]


def schedule(ops, m):
    n = len(ops)
    if "cs" not in ops[0]:
        cs = [[cost(e, c, m) for (e, c, _f) in op["alt"]] for op in ops]
        path = [0.0] * n
        for k in range(n - 1, -1, -1):
            path[k] = sum(cs[k][0]) + m["hop"] + max([path[s] for s in ops[k]["suc"]] + [0.0])
        jobs = {}
        for k, op in enumerate(ops):
            if op["job"]:
                jobs.setdefault(op["job"][0], []).append(k)
        ops[0]["cs"] = (cs, path, jobs, {op["name"]: k for k, op in enumerate(ops)})
    cs, path, jobs, where = ops[0]["cs"]
    wait = [len(op["pre"]) for op in ops]
    on, nxt = {}, {}
    for e, names in ORDER.items():
        ks = [where[y] for x in names for y in (x, x + "a", x + "b") if y in where]
        on.update({k: e for k in ks})
        for i in range(1, len(ks)):
            nxt.setdefault(ks[i - 1], []).append(ks[i])
            wait[ks[i]] += 1
            job = ops[ks[i]]["job"]
            first = jobs[job[0]][0] if job else None
            if job and ops[first]["eng"] == "P" and ks[i] == jobs[job[0]][[ops[x]["eng"] == "P" for x in jobs[job[0]]].index(False)]:
                lead = LEAD.get(ops[first]["name"][:6], OPTS["lead"].get(ops[first]["name"][:2], 1))
                if lead <= i:
                    nxt.setdefault(ks[i - lead], []).append(first)
                    wait[first] += 1
    prio = [p + SHIFT.get(op["name"], 0.0) - (OPTS["big"] if k in on else 0.0) for k, (p, op) in enumerate(zip(path, ops))]
    left = {j: len(v) for j, v in jobs.items()}
    holder, freed = [None] * 8, [0.0] * 8
    bank, extra, free, order = {}, {}, dict.fromkeys(["V", "S", "P", "G", "Y", None], 0.0), []
    can = [[(a, e) for a, (e, _c, _f) in enumerate(op["alt"]) if on.get(k, e) == e] for k, op in enumerate(ops)]
    jobof, soon = [op["job"] for op in ops], OPTS["soon"]
    rdy, beg, fin, use = [0.0] * n, [0.0] * n, [0.0] * n, [0] * n
    ready = [k for k in range(n) if not wait[k]]

    def banks(size):
        if size == 1:
            fits = [(not held[b ^ 1], freed[b], -b) for b in range(8) if not held[b]]
        else:
            fits = [(False, max(freed[b], freed[b + 1]), -b) for b in (0, 2, 4, 6) if not held[b] and not held[b + 1]]
        return min(fits)[1:] if fits else None
    spare, held = {}, [False] * 8
    while ready:
        cand = []
        for k in ready:
            t, job = rdy[k], jobof[k]
            if job and job[0] not in bank:
                if job[1] not in spare:
                    spare[job[1]] = banks(job[1])
                b = spare[job[1]]
                if b is None:
                    continue
                t = max(t, b[0] + m["hop"])
            for a, e in can[k]:
                cand.append((t if t > free[e] else free[e], -prio[k], a, k, e))
        if not cand:
            return None
        t0, _p, _a, _k, e = min(cand)
        _p, t, use_k, k = min([(c[1], c[0], c[2], c[3]) for c in cand if c[4] == e and c[0] <= t0 + soon])
        use[k], job = use_k, jobof[k]
        beg[k], fin[k] = t, t + sum(cs[k][use_k])
        if e:
            free[e] = t + cs[k][use_k][0]
        if job:
            j, size = job
            if j not in bank:
                b = bank[j] = -spare[size][1]
                extra[k] = [p for h in holder[b:b + size] if h is not None for p in jobs[h]]
                holder[b:b + size] = [j] * size
            left[j] -= 1
            for b in range(bank[j], bank[j] + size):
                freed[b] = max(freed[b], fin[k])
                if held[b] != (left[j] > 0):
                    held[b] = left[j] > 0
                    spare = {}
        order.append(k)
        ready.remove(k)
        for s in ops[k]["suc"] + nxt.get(k, []):
            wait[s] -= 1
            rdy[s] = max(rdy[s], t)
            if not wait[s]:
                ready.append(s)
        for s in ops[k]["suc"]:
            rdy[s] = max(rdy[s], fin[k] + m["hop"])
    if len(order) < n:
        return None
    return max(fin), order, bank, extra, use, beg


def plan(g, core, T, topo, turn_r, turn_l):
    rank = T.rank_of(core)
    N = len(T.cores)
    right, left = T.cores[(rank + 1) % N], T.cores[(rank - 1) % N]
    for dst in (right, left):
        if not topo.may_write(core, dst):
            raise ValueError("this core can't reach its neighbour")
    Q = {"V": g.vector, "S": g.scalar, "P": g.tensor, "G": g, "Y": g.sync}
    ops = []
    bank = {}
    acc = {}
    jacc = {}
    seen = {}
    wide = {n: (2 if s[2] in ("float16", "bfloat16", "uint16") else 4) for n, s in SCRATCH.items()}

    def sb(name, lo, hi, step=1):
        rng = [(name, lo, hi)] + ([("tb8", lo, hi)] if name == "tb" else [])
        return (lambda: T[name][:, lo:hi:step] if step > 1 else T[name][:, lo:hi], rng, None,
                (hi - lo + step - 1) // step, wide[name])

    def row(name, p, lo, hi):
        return (lambda: T[name][p:128:16, lo:hi], [(name + ("8" if p and name == "tb" else ""), lo, hi)], None, hi - lo, wide[name])

    def ps(job, lo, hi, step=1):
        return (lambda: T.ps[:, 512 * bank[job[0]] + lo:512 * bank[job[0]] + hi:step], [], job, (hi - lo + step - 1) // step, 4)

    def ind(win, off):
        return (lambda: win[0]().indirect(off[0]()), win[1] + off[1], None, 16 * off[3], 0)

    def both(a, b):
        return (a[0], a[1] + b[1]) + a[2:]

    def hbm(f):
        return (f, [], None, 0, 0)

    def add(name, eng, c, outs, ins, emit, after=(), ninc=1, sem=None, alt=None):
        k = len(ops)
        if alt:
            eng = "?%d" % k
        pre = set(after)
        job = None
        for lst, wr in ((ins, False), (outs, True)):
            for o in lst:
                if o[2]:
                    job = o[2]
                for (b, lo, hi) in o[1]:
                    for (l2, h2, p, w2) in acc.get(b, []):
                        if l2 < hi and lo < h2 and (wr or w2) and p != k:
                            pre.add(p)
                    acc.setdefault(b, []).append((lo, hi, k, wr))
        if job:
            wr = any(o[2] for o in outs)
            for (p, w2) in jacc.get(job[0], []):
                if ops[p]["eng"] != eng or wr or w2:
                    pre.add(p)
            jacc.setdefault(job[0], []).append((k, wr))
        seen[name] = seen.get(name, 0) + 1
        if seen[name] > 1:
            name = "%s_%d" % (name, seen[name])
        ops.append(dict(name=name, eng=eng, alt=alt or [(eng, c, emit)], pre=sorted(pre), suc=[], job=job, ninc=ninc, sem=sem))
        for p in pre:
            ops[p]["suc"].append(k)
        return k

    def pick(name, choices):
        DEBUG.setdefault("flex", {})[name] = choices
        return ENG.get(name, choices[0])

    def pieces(name, h):
        DEBUG.setdefault("split", set()).add(name)
        lo = 1024 * h
        return [("a", lo, lo + 512), ("b", lo + 512, lo + 1024)] if name in SPLIT else [("", lo, lo + 1024)]

    def cyc(out, ins):
        return out[3] * (0.5 if all(o[4] == 2 for o in [out] + ins) else 1.0)

    def ts_form(out, a, s1, s2, o0, o1):
        v = lambda s: s[0]() if isinstance(s, tuple) else s
        if o1 is None:
            return ("V", ("e", cyc(out, [a])), lambda: [g.vector.tensor_scalar(out[0](), a[0](), v(s1), None, o0)])
        return ("V", ("e", cyc(out, [a])), lambda: [g.vector.tensor_scalar(out[0](), a[0](), v(s1), v(s2), o0, o1)])

    def act_form(out, a, fn, bias=None, scale=None, c=None):
        def f():
            kw = {}
            for key, s in (("bias", bias), ("scale", scale)):
                if s is not None:
                    kw[key] = s[0]() if isinstance(s, tuple) else s
            return [g.scalar.activation(out[0](), a[0](), fn, **kw)]
        return ("S", c or ("g" if a[4] == 0 else "e", out[3]), f)

    def ts(name, out, a, s1, s2, o0, o1=None):
        e, c, f = ts_form(out, a, s1, s2, o0, o1)
        return add(name, e, c, [out], [a] + [s for s in (s1, s2) if isinstance(s, tuple)], f)

    def tt(name, out, a, b, o):
        c = ("g", out[3]) if a[4] == 0 else ("e", out[3] * (1 if a[2] or b[2] else 2))
        return add(name, "V", c, [out], [a, b], lambda: [g.vector.tensor_tensor(out[0](), a[0](), b[0](), o)])

    def act(name, out, a, fn, bias=None, scale=None, after=(), c=None):
        e, c, f = act_form(out, a, fn, bias, scale, c)
        return add(name, e, c, [out], [a] + [s for s in (bias, scale) if isinstance(s, tuple)], f, after)

    def cp(name, out, a, choices="SV"):
        alt = {"S": act_form(out, a, F.Copy),
               "V": ("V", ("g", out[3]) if a[4] == 0 else ("e", cyc(out, [a])), lambda: [g.vector.tensor_copy(out[0](), a[0]())]),
               "G": ("G", ("gp", out[3]), lambda: [g.affine_select(out[0](), a[0](), [[0, out[3]]], A.is_ge, 0.0, 0, 0)])}
        return add(name, None, None, [out], [a], None, alt=[alt[e] for e in choices])

    def mul(name, out, a, s):
        return add(name, None, None, [out], [a] + ([s] if isinstance(s, tuple) else []), None,
                   alt=[act_form(out, a, F.Identity, scale=s), ts_form(out, a, s, None, A.mult, None)])

    def flip(name, out, a):
        return add(name, "V", ("e", out[3]), [out], [a], lambda: [g.vector.transpose(out[0](), a[0]())])

    def mm(name, groups, after=(), first=True, last=True):
        def f():
            r = []
            for gr in groups:
                for i, (o, l, x) in enumerate(gr):
                    ins = g.tensor.matmul(o[0](), l[0](), x[0](), first and i == 0, last and i == len(gr) - 1)
                r.append(ins)
            return r
        n = sum(max(64, x[3]) * (4 if x[4] == 4 else 1) for gr in groups for (o, l, x) in gr)
        return add(name, "P", ("pe", n), [gr[0][0] for gr in groups], [y for gr in groups for (o, l, x) in gr for y in (l, x)],
                   f, after, ninc=len(groups))

    def lin(jb, terms, lo, hi):
        return [[(ps(jb, q - lo, min(q + 512, hi) - lo), l, sb(n, q, min(q + 512, hi))) for (l, n) in terms] for q in range(lo, hi, 512)]

    nd = [0]

    def dma(name, q, out, a, nbytes, after=(), accum=False):
        sem = "d%d" % nd[0]
        nd[0] += 1
        if accum:
            f = lambda: [g.dma_start(out[0](), a[0](), accum_op=A.add)]
        else:
            f = lambda: [Q[q].dma_start(out[0](), a[0]())]
        return add(name, q, ("dma", nbytes), [out], [a], f, after, sem=(sem, 16))

    last_send = []
    sent = [0]
    back = []

    def send(name, dst, src, land, sem):
        es = topo.engines(core, dst)

        def f():
            rid, pid, _s = topo.addr(dst)
            g.remote_dma(land[0](), src[0](), T.sem[sem], T.sem.sent, pid, rid, topo.mask(core, dst))
            return []
        k = add(name, "G", ("rem", 0), [], [src], f, last_send[-1:], ninc=0)
        last_send.append(k)
        sent[0] += len(es)
        add("arr_" + sem, None, ("arr", src[3] * src[4]), [land], [], None, [k], sem=(sem, len(es)))

    def fold(nm, srcs, there, land):
        aid = helper(core, T, topo)
        es = topo.engines(core, aid)

        def f():
            rid, pid, _s = topo.addr(aid)
            g.remote_dma_fused([RemoteDMATransfer(dst_ids=[DstId(rid=rid, pnc=pid)], dma_engine_mask=topo.mask(core, aid), remote_sem=T.sem["f" + nm],
                                                  srcs=[s[0]() for s in srcs], dsts=[there[0]()], alu_op=2)], local_sem=T.sem.sent)
            return []
        k = add("fold" + nm, "G", ("rem", 0), [], srcs, f, ninc=0)
        sent[0] += len(es)
        add("arr_f" + nm, None, ("two", there[3] * there[4]), land, srcs, None, [k], sem=("h" + nm, len(es)))
        back.append(("fold" + nm, "f" + nm, there, land, "h" + nm))

    def io(name, out, pat, base, cm, flt):
        kw = {"allow_small_or_imprecise_dtypes": True} if flt else {}
        return add(name, "G", ("gp", out[3]), [out], [], lambda: [g.iota(out[0](), pat, base, cm, **kw)], last_send[2:])

    jn_ = [0]

    def job(size):
        jn_[0] += 1
        return (jn_[0], size)

    x0 = T.x0
    own = XW + H_
    src_r, src_l = sb("xw0", own + V_ - H_, own + V_), sb("xw0", own, own + H_)
    if turn_l:
        dma("Xld_c", "Y", (lambda: T.et0[0:112, :], [("et0", 0, H_)], None, 0, 2), hbm(lambda: x0[16:128, 0:H_]), 768)
        dma("Xld_d", "S", (lambda: T.et0[112:128, :], [("et0b", 0, 1)], None, 0, 2), hbm(lambda: x0[0:16, 0:H_]), 768)
        src_l = both((lambda: T.et0[:, :], [("et0", 0, H_), ("et0b", 0, 1)], None, H_, 2), src_l)
    if turn_r:
        dma("Xld_a", "Y", (lambda: T.es0[16:128, :], [("es0", 0, H_)], None, 0, 2), hbm(lambda: x0[0:112, V_ - H_:V_]), 768)
        dma("Xld_b", "S", (lambda: T.es0[0:16, :], [("es0b", 0, 1)], None, 0, 2), hbm(lambda: x0[112:128, V_ - H_:V_]), 768)
        src_r = both((lambda: T.es0[:, :], [("es0", 0, H_), ("es0b", 0, 1)], None, H_, 2), src_r)
    dma("ld_l", "Y", sb("xw0", own, own + H_), hbm(lambda: x0[:, 0:H_]), 768)
    dma("ld_r", "S", sb("xw0", own + V_ - H_, own + V_), hbm(lambda: x0[:, V_ - H_:V_]), 768)
    send("sx0l", left, src_l, sb("xw0", own + V_, XW + W_), "x0r")
    send("sx0r", right, src_r, sb("xw0", XW, own), "x0l")
    dma("ld_rt", "Y", sb("li", 0, 128), hbm(lambda: T.rt[:, :]), 512)
    dma("ld_lf", "S", sb("li", 128, 256), hbm(lambda: T.lf[:, :]), 512)
    dma("ld_m", "Y", sb("xw0", own + H_, own + V_ - H_), hbm(lambda: x0[:, H_:V_ - H_]), 2560)
    dma("ld_h", "Y", sb("xh0", 0, V_), hbm(lambda: x0[:, :]), 4096)

    io("dd", sb("dd", 0, 256), [[1, 256]], 0, -1, False)
    io("pi", sb("pi", 0, 1), [[0, 1]], 0, 1, False)
    io("rr", sb("rr", 0, 16), [[1, 16]], 0, 0, True)
    io("vi", sb("vi", 0, 128), [[16, 128]], H_ - OFF, 0, True)
    ts("pi15", sb("pi", 1, 2), sb("pi", 0, 1), 15, None, A.bitwise_and)
    ts("pi16", sb("pi", 2, 3), sb("pi", 0, 1), 16, None, A.bitwise_and)
    cp("pm", sb("pm", 0, 2), sb("pi", 1, 3), "V")
    pm = sb("pm", 0, 1)
    ts("odd", sb("pm", 2, 3), sb("pm", 1, 2), 0.0, None, A.not_equal)
    ts("even", sb("pm", 3, 4), sb("pm", 1, 2), 0.0, None, A.is_equal)
    ts("c15", sb("pm", 4, 5), pm, -1.0, 15.0, A.mult, A.add)
    ts("oh", sb("oh", 0, 16), sb("rr", 0, 16), pm, None, A.is_equal)
    ts("no", sb("no", 0, 16), sb("rr", 0, 16), pm, None, A.not_equal)
    ts("dm", sb("dm", 0, 256), sb("dd", 0, 256), 127, None, A.bitwise_and)
    ts("jj", sb("jj", 0, 256), sb("dm", 0, 256), 0.0, None, A.is_equal)
    wj = 256 if turn_r or turn_l else 128
    for n, c, w in (("jn", -1.0, 128), ("j2", 2.0, 128), ("jm", -2.0, 128), ("jf", 1.0, 128), ("jk", 4096.0, 128),
                    ("je", sb("pm", 3, 4), 256), ("jo", sb("pm", 2, 3), 256), ("ja", 1.125, wj), ("jb", -0.125, wj)):
        mul(n, sb(n, 0, w), sb("jj", 0, w), c)
    ts("s1", sb("s1", 0, 128), sb("dd", 0, 128), 1.0, sb("no", 15, 16), A.is_equal, A.mult)
    ts("s15", sb("s15", 0, 128), sb("dd", 0, 128), -15.0, sb("oh", 15, 16), A.is_equal, A.mult)
    ts("zc", sb("zc", 0, 144), sb("dd", 0, 144), sb("pm", 4, 5), None, A.is_equal)
    ts("z0", sb("z0", 0, 144), sb("dd", 0, 144), 15.0, sb("oh", 0, 1), A.is_equal, A.mult)
    ts("z8", sb("z8", 0, 144), sb("dd", 0, 144), 7.0, sb("oh", 8, 9), A.is_equal, A.mult)
    tt("zf", sb("zf", 0, 144), sb("z8", 0, 144), sb("z0", 0, 144), A.subtract)
    ts("s3", sb("s3", 0, 128), sb("dd", 0, 128), -1.0, sb("no", 0, 1), A.is_equal, A.mult)
    ts("vq", sb("vq", 0, 128), sb("vi", 0, 128), pm, None, A.add)
    ts("v2", sb("v2", 0, 128), sb("vi", 0, 128), pm, float(4096 + XW - XA), A.add, A.add)
    act("kb", sb("kb", 0, 16), sb("rr", 0, 16), F.Identity, bias=float(V_), scale=0.0)
    act("one", sb("one", 0, 128), sb("vi", 0, 128), F.Identity, bias=1.0, scale=0.0)
    if any(pick("a1%d%d" % (t, h), "DE") == "E" for t in (0, 1) for h in (0, 1)):
        ts("low", sb("pm", 5, 6), pm, 8.0, None, A.is_lt)
        ts("high", sb("pm", 6, 7), pm, 8.0, None, A.is_ge)
        for i, (step, m_) in enumerate(((0.0, 5), (8.0, 5), (-8.0, 6), (0.0, 6))):
            ts("fm", sb("fm", 128 * i, 128 * i + 128), sb("dd", 0, 128), step, sb("pm", m_, m_ + 1), A.is_equal, A.mult)
        add("cw0", "V", ("e", 512), [sb("cw", 0, 1024)], [], lambda: [g.vector.memset(T.cw[:, :], 0.0)])
        add("cw1", "G", ("gp", 128), [sb("cw", 0, 1024)], [sb("one", 0, 128)],
            lambda: [g.affine_select(T.cw[:, 0:1024:8], T.one[:, 0:128], [[-1, 8], [-8, 16]], A.is_equal, 0.0, 0, 1)])
    for i, (n, c) in enumerate((("xw0", XW + W_), ("xw0", 0), ("xw1", XW + W_), ("xw1", 0))):
        act("pad", sb(n, c, c + PAD), sb("rr", 0, 16), F.Exp, bias=4.0, scale=0.0, c=("x", 0) if i == 0 else None)
    I_, In, I2, Im, Ik = (sb(n, 0, 128) for n in ("jj", "jn", "j2", "jm", "jk"))
    Z = lambda n, i: sb(n, 15 - i, 143 - i)
    RS, LS = 112, 16

    def ext(z, out, src, lo, more=()):
        return [(out, Z(z, i), sb(src, lo + i, lo + 1024, 16)) for i in range(16)] + list(more)

    def spread(jb, c0, terms, n, turn=0, bias=None):
        gs = []
        for b in range(n // 32):
            for gp in (0, 1):
                o = ps(jb, c0 + 32 * b + 16 * gp, c0 + 32 * b + 16 * gp + 16)
                gr = [(o, bias, sb("kb", 0, 16))] if bias else []
                for cb in (0, 1):
                    c = (-16 * (cb - gp + turn)) % 128
                    sel = sb("jo" if (gp + turn) % 2 else "je", c, c + 128)
                    gr += [(o, sel, sb(name, lo + 2 * b + cb, lo + n, n // 16)) for (name, lo) in terms]
                gs.append(gr)
        return gs

    def lk(name, side, h, c0=0, c1=64):
        b = BLK[(side, h)]
        return sb(name, b + c0, b + c1)

    def offs(name, side, lo, hi):
        return sb(name, BLK[(side, 0)] + lo // 16, BLK[(side, 0)] + hi // 16)

    BIAS = {"r": -H_, "l": PAD}
    ts("st0", sb("st0", 0, 256), sb("li", 0, 256), float(-OFF), None, A.add)
    ts("ul0r", sb("ul0", 0, 128), sb("li", 0, 128), float(BIAS["r"]), None, A.add)
    ts("ul0l", sb("ul0", 128, 256), sb("li", 128, 256), float(BIAS["l"]), None, A.add)
    parts = [lk("st0", "l", 1, 56, 64), lk("st0", "r", 1, 56, 64)]
    if turn_r:
        j = job(1)
        mm("Xsb0", [[(ps(j, 8 * i, 8 * i + 8), sb("jj", RS, RS + 128), p)] for i, p in enumerate(parts)])
    for i, p in enumerate(parts):
        act("sb0", sb("sb0", 8 * i, 8 * i + 8), ps(j, 8 * i, 8 * i + 8) if turn_r else p, F.Identity, bias=float(-V_))
    send("sb0s", right, sb("sb0", 0, 16), sb("gb0", 0, 16), "b0")
    end_tb = SCRATCH["tb"][1][1]
    for c in range(H_, end_tb, V_):
        w = min(V_, end_tb - c)
        dma("fill", "G", sb("tb", c, c + w), hbm(lambda w=w: x0[:, 0:w]), 4 * w, last_send[-1:])
    io("ghi", sb("tb", 0, H_), [[-16, 24], [0, 16]], OFF, 0, True)
    io("glo", sb("glo", 0, H_), [[0, 24], [1, 16]], 0, 0, True)
    dma("glo", "Y", row("tb", 8, 0, H_), row("glo", 8, 0, H_), 1500)
    cp("a2g", sb("a2t", 0, H_), sb("tb", 0, H_), "G")

    ydone = {}
    for t in range(2):
        d = 1 if t == 0 else -1
        R = "%d" % t
        xw, xh, so, sn, uo, un, uc, xt = "xw" + R, "xh" + R, "st" + R, "st%d" % (t + 1), "ul" + R, "ul%d" % (t + 1), "uc" + R, "xt" + R
        win = lambda side, hi: sb(xw, own, XA) if side == "r" else sb(xw, 0, own + hi)
        Id = I_ if d == 1 else In

        def shift(j, c, side, h):
            o = lambda a, b: ps(j, c + a, c + b)
            if d == 1:
                edge = lk(so, side, 0, 63, 64) if h == 1 else sb("gb0", 15 if side == "r" else 7, 16 if side == "r" else 8)
                return [(o(0, 64), sb("s1", 0, 128), lk(so, side, h)), (o(1, 64), sb("s15", 0, 128), lk(so, side, h, 0, 63)),
                        (o(0, 1), sb("s15", 0, 128), edge)]
            edge = lk(so, side, 1, 0, 1) if h == 0 else sb("ge", 1 if side == "r" else 0, 2 if side == "r" else 1)
            return [(o(0, 64), sb("s3", 0, 128), lk(so, side, h)), (o(0, 63), Z("z0", 15), lk(so, side, h, 1, 64)),
                    (o(63, 64), Z("z0", 15), edge)]
        for part in ([[("r", 1)], [("r", 0)], [("l", 0), ("l", 1)]] if t == 0 else [[("r", 0), ("r", 1)], [("l", 0), ("l", 1)]]):
            j = job(1)
            side, b, w = part[0][0], BLK[part[0]], 64 * len(part)
            nm = "%s%d%d" % (side, t, part[0][1])
            mm("shift" + nm, [shift(j, 64 * i, s_, h) for i, (s_, h) in enumerate(part)])
            if side == "r":
                ts("uc" + nm, sb(uc, b, b + w), ps(j, 0, w), float(OFF + d + BIAS[side]), float(W_ + BIAS[side]), A.add, A.min)
            else:
                ts("uc" + nm, sb(uc, b, b + w), ps(j, 0, w), float(OFF + d + BIAS[side]), float(PAD - 1), A.add, A.max)
        for n, c in ((xw, XA), ("m2t" + R, 0), ("m4t" + R, 0)):
            dma("gh_" + n, "Y", sb(n, c, c + H_), sb(xw, XW, own), H_ * wide[n])

        for (side, h) in (("r", 1), ("r", 0), ("l", 0), ("l", 1)):
            nm = "%s%d%d" % (side, t, h)
            e_, a_, p_ = "e" + side, "a" + side, "p" + side
            for (s, lo, hi) in pieces("xe" + nm, h):
                cp("xe" + nm + s, sb(e_, lo, hi), ind(win(side, hi), offs(uo, side, lo, hi)))
            plain = pick("xc" + nm, "VS") == "S"
            for (s, lo, hi) in pieces("xc" + nm, h):
                a = ind(win(side, hi), offs(uc, side, lo, hi))
                if plain:
                    cp("xc" + nm + s, sb(a_, lo, hi), a)
                else:
                    tt("xc" + nm + s, sb(a_, lo, hi), a, sb(e_, lo, hi), A.subtract)
            for (s, lo, hi) in pieces("sa" + nm, h) if plain else []:
                j1 = job((hi - lo) // 512)
                mm("dif" + nm + s, lin(j1, [(In, e_), (I_, a_)], lo, hi))
                act("sa" + nm + s, sb(p_, lo, hi), ps(j1, 0, hi - lo), F.Sign)
            for (s, lo, hi) in pieces("pr" + nm, h):
                j1 = job((hi - lo) // 512)
                mm("sux" + nm + s, lin(j1, [(Im, xh)], lo, hi), last=False)
                mm("sue" + nm + s, lin(j1, [(I_ if plain else I2, e_)], lo, hi), first=False, last=False)
                mm("sum" + nm + s, lin(j1, [(I_, a_)], lo, hi), first=False)
                tt("pr" + nm + s, sb(p_, lo, hi), ps(j1, 0, hi - lo), sb(p_ if plain else a_, lo, hi), A.mult)
            for (s, lo, hi) in pieces("nr" + nm, h):
                p = sb(p_, lo, hi)
                add("nr" + nm + s, None, None, [p], [p], None,
                    alt=[ts_form(p, p, 0.0, -0.5, A.is_lt, A.add), act_form(p, p, F.Sign, -2.0 ** -20, -1.0)])
            lo = 1024 * h
            jc = job(1)
            how = pick("new" + nm, "PV")
            step = [(ps(jc, 64, 128), In, lk(so, side, h))] + ([(ps(jc, 64, 128), Id, sb("one", 0, 64))] if how == "V" else [])
            mm("cnt" + nm, [shift(jc, 64, side, h) + step, ext("zc", ps(jc, 0, 64), p_, lo)])
            ts("dec" + nm, lk("msk", side, h), ps(jc, 0, 64), 0.0, None, A.is_gt)
            tt("tt" + nm, lk("tt", side, h), ps(jc, 64, 128), lk("msk", side, h), A.mult)
            if how == "P":
                p = ps(jc, 128, 192)
                mm("new" + nm, [[(p, I_, lk(so, side, h)), (p, Id, lk("msk", side, h)), (p, sb("jf", 0, 128), lk("tt", side, h))]])
                cp("sn" + nm, lk(sn, side, h), p)
            else:
                p = lk(sn, side, h)
                tt("sn" + nm, p, lk("tt", side, h), lk(so, side, h), A.add)
            ts("un" + nm, lk(un, side, h), p, float(OFF + BIAS[side]), None, A.add)
            b = BLK[(side, h)]
            c = {("r", 1): 0, ("r", 0): 96, ("l", 0): 160, ("l", 1): 288}[(side, h)]
            j2 = job(1)
            gs = spread(j2, 0, [(sn, b)], 64)
            w = 64
            if (side, h) == ("r", 1):
                gs = spread(j2, 64, [(sn, b + 32)], 32, 1 if turn_r else 0, In) + gs
                w = 96
            if (side, h) == ("l", 0):
                for s_ in "lr"[:2 - t]:
                    gs += spread(j2, w, [(sn, BLK[(s_, 0)])], 32, -1 if turn_l else 0, I_)
                    w += 32
            mm("tbp" + nm, gs)
            flip("tbt" + nm, sb(xt, c, c + w), ps(j2, 0, w))
            if (side, h) == ("r", 1):
                send("sr" + R, right, sb(xt, c + 64, c + w), sb("gl" + R, 0, 32), "r" + R)
                dma("tgl" + R, "Y", row("tb", 0, TA - 128, TA + H_), sb("gl" + R, 0, 32), 1000)
            if (side, h) == ("l", 0):
                send("sl" + R, left, sb(xt, c + 64, c + w), sb("gr" + R, 0, w - 64), "l" + R)
                dma("tgr" + R, "Y", row("tb", 0, TB + V_, TB + V_ + 512), sb("gr" + R, 0, 32), 1000)
                if t == 0:
                    cp("ge", sb("ge", 0, 2), sb("gr0", 0, 64, 32))
            c0 = (TA + H_ if side == "r" else TB) + lo
            dma("tbd" + nm, "Y", row("tb", 0, c0, c0 + 1024), sb(xt, c, c + 64), 1500)

        col = lambda n, h: sb(n, 64 * h, 64 * h + 64)
        lst = lambda n, lo, hi: sb(n, lo // 16, hi // 16)
        ua1, ua2, ua4, xa = "ua1" + R, "ua2" + R, "ua4" + R, "xa" + R
        for h in (0, 1):
            nm = "%d%d" % (t, h)
            for (s, lo, hi) in pieces("back" + nm, h):
                cp("back" + nm + s, sb("ob", lo, hi), ind(sb("tb", TA - PAD, TA + H_ + hi), offs(un, "l", lo, hi)))
            lo, hi = 1024 * h, 1024 * h + 1024
            j1 = job(1)
            how = pick("b1" + nm, "SVW")
            more = [[(ps(j1, 64, 128), I_, lk(sn, "l", h)), (ps(j1, 64, 128), In, col("vq", h))]] if how == "W" else []
            mm("backx" + nm, more + [ext("z0", ps(j1, 0, 64), "ob", lo, [(ps(j1, 0, 64), In, col("vq", h))])])
            if how == "W":
                ts("b1" + nm, col("w1", h), ps(j1, 0, 64), 0.0, None, A.is_equal)
                tt("b2" + nm, col("w5", h), ps(j1, 64, 128), col("w1", h), A.mult)
                tt("b3" + nm, col("a1w", h), col("w5", h), col("vq", h), A.add)
            else:
                if how == "S":
                    act("b1" + nm, col("w1", h), ps(j1, 0, 64), F.Abs)
                else:
                    ts("b1" + nm, col("w1", h), ps(j1, 0, 64), 0.0, None, A.not_equal)
                mm("b2" + nm, [[(ps(j1, 64, 128), I_, lk(sn, "l", h)), (ps(j1, 64, 128), Ik, col("w1", h))]])
                tt("b3" + nm, col("a1w", h), ps(j1, 64, 128), col("vq", h), A.min)
            mul("b5" + nm, col("nh", h), col("a1w", h), -1.0)
            ts("b4" + nm, col(ua1, h), col("a1w", h), float(OFF), None, A.add)
            j2 = job(1)
            if pick("a1" + nm, "DE") == "E":
                fm = lambda i: sb("fm", 128 * i, 128 * i + 128)
                mm("a1q" + nm, [[(ps(j2, s, 128, 2), fm(2 * s), col("nh", h)), (ps(j2, s, 128, 2), fm(2 * s + 1), col("nh", h)),
                                 (ps(j2, s, 128, 2), fm(2 * s + 1), col("a1w", h))] for s in (0, 1)])
                cp("a1f" + nm, sb("fold", 128 * h, 128 * h + 128), ps(j2, 0, 128))
                for b in (0, 1):
                    j3 = job(1)
                    c = 128 * h + 64 * b
                    mm("a1r" + nm, [[(ps(j3, i, 512, 8), sb("cw", 128 * i, 128 * i + 128), sb("fold", c, c + 64))] for i in range(8)])
                    cp("a1e" + nm + "ab"[b], sb("tb", H_ + lo + 512 * b, H_ + lo + 512 * b + 512), ps(j3, 0, 512))
                continue
            mm("a1p" + nm, spread(j2, 0, [("nh", 64 * h)], 64) + spread(j2, 64, [("a1w", 64 * h), ("nh", 64 * h)], 64))
            flip("a1t" + nm, sb(xa, 128 * h, 128 * h + 128), ps(j2, 0, 128))
            for i in (0, 1):
                dma("a1d" + nm, "Y", row("tb", 8 * i, H_ + lo, H_ + hi), sb(xa, 128 * h + 64 * i, 128 * h + 64 * i + 64), 1500)
        for h in (0, 1):
            nm = "%d%d" % (t, h)
            for (s, lo, hi) in pieces("end" + nm, h):
                cp("end" + nm + s, sb("oe", lo, hi), ind(sb("tb", TB, TB + XO), offs(un, "r", lo, hi)))
            j1 = job(1)
            mm("endx" + nm, [ext("z0", ps(j1, 0, 64), "oe", 1024 * h, [(ps(j1, 0, 64), In, col("vq", h))])])
            ts("g1" + nm, col("w3", h), ps(j1, 0, 64), 0.0, None, A.is_equal if pick("d2" + nm, "PV") == "P" else A.not_equal)
        for h in (0, 1):
            nm = "%d%d" % (t, h)
            for (s, lo, hi) in pieces("a2" + nm, h):
                cp("a2" + nm + s, sb("a2t", H_ + lo, H_ + hi), ind(sb("tb", 0, H_ + hi), lst(ua1, lo, hi)))
            j1 = job(1)
            mm("a2x" + nm, [ext("zf", ps(j1, 0, 64), "a2t", H_ + 1024 * h)])
            ts("c1" + nm, col(ua2, h), ps(j1, 0, 64), float(OFF), None, A.add)
            cp("c2" + nm, col("a2w", h), ps(j1, 0, 64))
        for h in (0, 1):
            nm = "%d%d" % (t, h)
            for (s, lo, hi) in pieces("a4" + nm, h):
                cp("a4" + nm + s, sb("o4", lo, hi), ind(sb("a2t", 0, H_ + hi), lst(ua2, lo, hi)))
            j1 = job(1)
            p = ps(j1, 0, 64)
            how = pick("d2" + nm, "PV")
            mm("a4x" + nm, [ext("zf", p, "o4", 1024 * h, [(p, Ik, sb("one", 0, 64))] if how == "V" else [])])
            ts("d1" + nm, col(ua4, h), p, float(OFF - (4096 if how == "V" else 0)), None, A.add)
            if how == "P":
                cp("d2" + nm, col("a4w", h), p)
                p = ps(j1, 64, 128)
                mm("d3" + nm, [[(p, I_, col("a4w", h)), (p, In, col("a2w", h)), (p, Ik, col("w3", h))]])
                act("d4" + nm, col("w4", h), p, F.Sign, bias=-0.5, scale=-1.0)
                p = ps(j1, 128, 192)
                mm("d5" + nm, [[(p, I_, col("a4w", h)), (p, Ik, col("w4", h))]])
                tt("d6" + nm, col("w7", h), p, col("v2", h), A.max)
            else:
                j2 = job(1)
                q = ps(j2, 0, 64)
                mm("d3" + nm, [[(q, I_, col("a2w", h)), (q, Ik, col("w3", h))]])
                cp("d2" + nm, col("w6", h), q)
                tt("d4" + nm, col("w4", h), p, col("w6", h), A.is_lt)
                tt("d5" + nm, col("w5", h), p, col("w4", h), A.mult)
                tt("d6" + nm, col("w7", h), col("w5", h), col("v2", h), A.max)
            ts("d7" + nm, col("uix", h), col("w7", h), float(XA - own + OFF - 4096), None, A.add)
        for h in (0, 1):
            nm = "%d%d" % (t, h)
            for (s, lo, hi) in pieces("xa4" + nm, h):
                cp("xa4" + nm + s, sb(xw, XA + H_ + lo, XA + H_ + hi), ind(sb(xw, XW, own + hi), lst(ua4, lo, hi)))
        for h in (0, 1):
            nm = "%d%d" % (t, h)
            for (s, lo, hi) in pieces("xs" + nm, h):
                cp("xs" + nm + s, sb("xs", lo, hi), ind(sb(xw, own, XA + H_ + hi), lst("uix", lo, hi)))
            for (s, lo, hi) in pieces("cl" + nm, h):
                turn = t == 0 and ((turn_r and hi == V_) or (turn_l and lo == 0))
                ea, eb = (V_ - H_, V_) if hi == V_ else (0, H_)
                if turn:
                    j2 = job(1)
                    c0 = RS if hi == V_ else LS
                    mm("Xmve" + nm, lin(j2, [(sb("ja", c0, c0 + 128), xh), (sb("jb", c0, c0 + 128), "xs")], ea, eb))
                    ts("Xcle" + nm, sb("es1" if hi == V_ else "et1", 0, H_), ps(j2, 0, H_), 0.0, 4.0, A.max, A.min)
                j1 = job((hi - lo) // 512)
                mm("mv" + nm + s, lin(j1, [(sb("ja", 0, 128), xh), (sb("jb", 0, 128), "xs")], lo, hi))
                if t == 0:
                    ts("cl" + nm + s, sb("xw1", own + lo, own + hi), ps(j1, 0, hi - lo), 0.0, 4.0, A.max, A.min)
                    src = sb("xw1", own + ea, own + eb)
                    if turn:
                        src = both(sb("es1" if hi == V_ else "et1", 0, H_), src)
                    if lo == 0:
                        send("sx1l", left, src, sb("xw1", own + V_, XW + W_), "x1r")
                    if hi == V_:
                        send("sx1r", right, src, sb("xw1", XW, own), "x1l")
                    cp("cast" + nm + s, sb("xh1", lo, hi), sb("xw1", own + lo, own + hi), pick("cast" + nm, "GSV"))
                else:
                    ts("cl" + nm + s, sb("yy0", lo, hi), ps(j1, 0, hi - lo), 0.0, 4.0, A.max, A.min)
                    dma("xe" + nm + s, "Y", hbm(lambda lo=lo, hi=hi: T.xe[:, lo:hi]), sb("yy0", lo, hi), 4 * (hi - lo))
        m2, m4, c2, c4, mx, dn, yy = "m2t" + R, "m4t" + R, "m2c" + R, "m4c" + R, "mm" + R, "dn" + R, "yy" + R
        for h in (0, 1):
            nm = "%d%d" % (t, h)
            if t in OPTS["fold"]:
                lo, hi = 1024 * h, 1024 * h + 1024
                fold("2" + nm, [sb(xw, XA + H_ + lo, XA + H_ + hi), sb(xw, own + lo, own + hi)], sb(c2, lo, hi),
                     [sb(m2, H_ + lo, H_ + hi), sb(c2, lo, hi)])
                continue
            for (s, lo, hi) in pieces("m2" + nm, h):
                tt("m2" + nm + s, sb(m2, H_ + lo, H_ + hi), ind(sb(xw, XW, own + hi), lst(ua1, lo, hi)), sb(xh, lo, hi), A.max)
                dma("m2c" + nm + s, "Y", sb(c2, lo, hi), sb(m2, H_ + lo, H_ + hi), (hi - lo) * wide[m2])
        if t in OPTS["fold"]:
            ua4 = ua1
        for h in (0, 1):
            nm = "%d%d" % (t, h)
            plain = t == 0 and pick("m4" + nm, "VF") == "F"
            for (s, lo, hi) in pieces("m4" + nm, h):
                a = ind(sb(m2, 0, H_ + hi), lst(ua2, lo, hi))
                if plain:
                    cp("m4" + nm + s, sb(mx, lo, hi), a)
                else:
                    tt("m4" + nm + s, sb(m4, H_ + lo, H_ + hi), a, sb(c2, lo, hi), A.max)
                    dma("m4c" + nm + s, "Y", sb(c4, lo, hi), sb(m4, H_ + lo, H_ + hi), (hi - lo) * wide[m2])
            if plain:
                lo, hi = 1024 * h, 1024 * h + 1024
                fold("4" + nm, [sb(mx, lo, hi), sb(c2, lo, hi)], sb(c4, lo, hi), [sb(m4, H_ + lo, H_ + hi), sb(c4, lo, hi)])
        for h in (0, 1):
            nm = "%d%d" % (t, h)
            plain = t == 0 and pick("m8" + nm, "VF") == "F"
            mx = "mm" + R
            for (s, lo, hi) in pieces("m8" + nm, h):
                a = ind(sb(m4, 0, H_ + hi), lst(ua4, lo, hi))
                if plain:
                    cp("m8" + nm + s, sb(mx, lo, hi), a)
                else:
                    tt("m8" + nm + s, sb(mx, lo, hi), a, sb(c4, lo, hi), A.max)
            if plain:
                lo, hi = 1024 * h, 1024 * h + 1024
                fold("8" + nm, [sb(mx, lo, hi), sb(c4, lo, hi)], sb(mx, lo, hi), [sb(c2, lo, hi)])
                mx = c2
            how = pick("rn" + nm, "PVS")
            for (s, lo, hi) in pieces("dn" + nm, h):
                a = ind(win("r", hi), offs(un, "r", lo, hi))
                if how == "P":
                    act("dn" + nm + s, sb(dn, lo, hi), a, F.Copy)
                else:
                    tt("dn" + nm + s, sb(dn, lo, hi), a, sb(xh, lo, hi), A.subtract)
            lo, hi = 1024 * h, 1024 * h + 1024
            if how == "V":
                ts("rn" + nm, sb("rn", lo, hi), sb(dn, lo, hi), 0.0, None, A.max)
            if how == "S":
                act("rn" + nm, sb(dn, lo, hi), sb(dn, lo, hi), F.Abs)
            for (s, lo, hi) in pieces("exp" + nm, h):
                if how == "S":
                    p = sb(dn, lo, hi)
                else:
                    j1 = job((hi - lo) // 512)
                    p = ps(j1, 0, hi - lo)
                    mm("ad" + nm + s, lin(j1, [(In, xh), (I_, dn)] if how == "P" else [(In, dn), (I2, "rn")], lo, hi))
                    if how == "P":
                        act("rn" + nm + s, p, p, F.Abs)
                act("exp" + nm + s, sb(yy, lo, hi), p, F.Exp, scale=-1.0)
            for (s, lo, hi) in pieces("y" + nm, h):
                j1 = job((hi - lo) // 512)
                mm("mc" + nm + s, lin(j1, [(I_, mx)], lo, hi))
                tt("y" + nm + s, sb(yy, lo, hi), ps(j1, 0, hi - lo), sb(yy, lo, hi), A.mult)
                out = hbm(lambda lo=lo, hi=hi: T.ye[:, lo:hi])
                if t == 0:
                    ydone.setdefault(h, []).append(dma("ye" + nm + s, "Y", out, sb(yy, lo, hi), 4 * (hi - lo)))
                else:
                    dma("ye" + nm + s, "G", out, sb(yy, lo, hi), 8 * (hi - lo), ydone[h], accum=True)

    return ops, bank, sent, Q, back


def timetable(g, core, T, topo):
    if not ORDERS:
        ops = plan(g, core, T, topo, True, True)[0]
        _time, order, bank, _extra, use, _beg = schedule(ops, MODEL)
        ORDERS.update({ops[k]["name"]: (use[k], bank[ops[k]["job"][0]] if ops[k]["job"] else None) for k in order})
    return ORDERS


def follow(ops, bank, table):
    where = {op["name"]: k for k, op in enumerate(ops)}
    order = [where[x] for x in table if x in where]
    place = {k: i for i, k in enumerate(order)}
    if len(order) < len(ops) or any(place[p] > place[k] for k in order for p in ops[k]["pre"]):
        raise ValueError("the table doesn't fit this rank's calls")
    jobs, holder, extra = {}, [[]] * 8, {}
    for k in order:
        if ops[k]["job"]:
            jobs.setdefault(ops[k]["job"][0], []).append(k)
    for k in order:
        if ops[k]["job"] and ops[k]["job"][0] not in bank:
            j, size = ops[k]["job"]
            b = bank[j] = table[ops[k]["name"]][1]
            extra[k] = [p for held in holder[b:b + size] for p in held]
            holder[b:b + size] = [jobs[j]] * size
    return order, [table[op["name"]][0] for op in ops], extra


def helper(core, T, topo):
    return [c for c in topo.cores_of(core) if T.rank_of(c) is None and topo.die(c) == topo.die(core)][0]


def hand_back(g, core, boss, T, topo):
    es = topo.engines(core, boss)
    rid, pid, _s = topo.addr(boss)
    back = plan(g, boss, T, topo, False, False)[4]
    names = list(timetable(g, boss, T, topo))
    for (_name, came, src, land, sem) in sorted(back, key=lambda b: names.index(b[0])):
        g.wait_ge(T.sem[came], len(topo.engines(boss, core)))
        per = len(es) // len(land)
        g.remote_dma_fused([RemoteDMATransfer(dst_ids=[DstId(rid=rid, pnc=pid)], dma_engine_mask=sum(1 << e for e in es[i * per:(i + 1) * per]),
                                              remote_sem=T.sem[sem], src=src[0](), dst=x[0]()) for i, x in enumerate(land)], local_sem=T.sem.sent)
    if back:
        g.wait_ge(T.sem.sent, len(es) * len(back))


def rank_program(g, core, T, topo):
    rank = T.rank_of(core)
    if rank is None:
        for boss in T.cores:
            if helper(boss, T, topo) == core:
                hand_back(g, core, boss, T, topo)
        return
    kind = (rank == len(T.cores) - 1, rank == 0)
    ops, bank, sent, Q, _back = plan(g, core, T, topo, kind[0], kind[1])
    order, use, extra = follow(ops, bank, timetable(g, core, T, topo))
    where = {k: i for i, k in enumerate(order)}
    count = {}
    token = {}
    clock = {}
    known = {e: {} for e in Q}
    for k in order:
        op = ops[k]
        e, _c, emit = op["alt"][use[k]]
        if e is None:
            token[k] = op["sem"]
            clock[k] = dict([op["sem"]])
            continue
        kn = known[e]
        need = sorted([p for p in set(op["pre"] + extra.get(k, [])) if p in token], key=lambda p: -where[p])
        for p in need:
            s, v = token[p]
            if kn.get(s, 0) < v and not (e == "P" and s == "cP"):
                Q[e].wait_ge(T.sem[s], v)
                for s2, v2 in clock[p].items():
                    kn[s2] = max(kn.get(s2, 0), v2)
        ins = emit()
        if op["sem"]:
            ins[0].then_inc(T.sem[op["sem"][0]], 16)
            token[k] = op["sem"]
        elif op["ninc"]:
            s = "c" + e
            for i in ins:
                i.then_inc(T.sem[s], 1)
            count[s] = count.get(s, 0) + op["ninc"]
            token[k] = (s, count[s])
        if k in token:
            clock[k] = dict(kn)
            clock[k][token[k][0]] = max(token[k][1], kn.get(token[k][0], 0))
    total = dict(count)
    total["sent"] = sent[0]
    for k in order:
        if ops[k]["sem"]:
            total[ops[k]["sem"][0]] = ops[k]["sem"][1]
    waited = {}
    for e in Q:
        for s, v in known[e].items():
            waited[s] = max(waited.get(s, 0), v)
    for s, v in total.items():
        if waited.get(s, 0) < v:
            g.wait_ge(T.sem[s], v)
